import numpy as np, ml_dtypes
CORES = [35,38,43,46]
N = 4
BF = ml_dtypes.bfloat16
def gentries(a):
    return np.ascontiguousarray(a.reshape(8, 16, -1).transpose(0, 2, 1)).reshape(8, -1)
def gtable(e):
    e = np.asarray(e); return np.ascontiguousarray(e.reshape(8, -1, 16).transpose(0, 2, 1)).reshape(128, -1).astype(np.int32)
M, D, B, RO, Q = 256, 2048, 512, 4, 6
NV = 16 * M
def parts(rng):
    v = rng.integers(0, 256, (N, 8, 16, NV)); a = rng.integers(0, NV, (N, 8, 16, D)); l = rng.integers(0, NV, (N, 8, 16, B))
    z = rng.integers(0, 256, (N, 8, 16, M)); c = rng.integers(0, B, (N, 8, M)); ka = rng.integers(0, 4096, (N, 8, 16))
    th = rng.integers(1150, 1450, (N, 8, 1)) + rng.integers(-150, 151, (N, 8, 16))
    return v, a, l, z, c, ka, th
def pack(v, a, l, z, c, ka, th):
    return {"vf": np.ascontiguousarray(v.reshape(N, 128, NV)).astype(np.float32).astype(BF), "ad": np.ascontiguousarray(a.reshape(N, 128, D)).astype(np.int32),
            "le": np.ascontiguousarray(l.reshape(N, 128, B)).astype(np.int32), "z0": np.ascontiguousarray(z.reshape(N, 128, M)).astype(np.float32).astype(BF),
            "cb": np.stack([gtable(x) for x in c]), "ka": ka.reshape(N, 128, 1).astype(np.int32), "th": th.reshape(N, 128, 1).astype(np.int32)}
def setup_inputs(rng):
    return pack(*parts(rng))
def setup_inputs_spread(rng):
    def uneven(n, *shape):
        v = np.minimum((n * rng.random((N, 8) + shape) ** 3).astype(np.int64), n - 1)
        up = (np.arange(8) % 2 == 1).reshape((1, 8) + (1,) * len(shape))
        return np.where(up, n - 1 - v, v)
    def sizes(n):
        return np.minimum((np.exp2(8.5 * rng.random((N, 8, 1, n))) * rng.random((N, 8, 16, n))).astype(np.int64), 255)
    th = np.minimum((4081 * rng.random((N, 8, 16)) ** 2.5).astype(np.int64), 4080)
    return pack(sizes(NV), uneven(NV, 16, D), uneven(NV, 16, B), sizes(M), uneven(B, M), uneven(4096, 16), th)
def setup_inputs_ends(rng):
    def halves(n):
        e = rng.random((N, 8, 16, n)) < 0.5; a = rng.random((N, 8, 1, n)) < 0.5
        return np.where(rng.random((N, 8, 1, n)) < 0.5, a, e).astype(np.int64)
    def coin(*shape):
        return (rng.random((N, 8) + shape) < 0.5).astype(np.int64)
    v = 255 * halves(NV); v[:, 1::2, :, 0] = 0; v[:, 1::2, :, NV - 1] = 255; v[:, 0, :, 0] = 255; v[:, 0, :, NV - 1] = 0
    top = np.zeros(16, np.int64); top[np.array([0, 1, 2, 6, 9])] = 255
    z = np.where(rng.random((N, 8, 1, M)) < 0.15, top[:, None], 255 * halves(M)); z[..., M - 1] = top; z[..., M - 2] = 255; z[..., 0] = 0
    c = (B - 1) * coin(M); c[..., M - 1] = B - 1; c[..., 0] = 0
    l = (NV - 1) * coin(16, B); l[:, :, 15, B - 1] = NV - 1; l[:, :, 0, 0] = 0
    a = (NV - 1) * coin(16, D); a[:, 7, 15] = 0
    ka = 4095 * coin(16); ka[:, 0, 0] = 0; ka[:, 7, 15] = 4095
    th = 4080 * (rng.random((N, 8, 16)) < rng.choice(np.array([0.1, 0.3, 0.6]), (N, 8, 1))).astype(np.int64); th[:, 0, 0] = 0; th[:, 7, 15] = 4080
    return pack(v, a, l, z, c, ka, th)
def setup_inputs_corners(rng):
    v, a, l, z, c, ka, th = parts(rng); h = NV // 2; late = int(rng.integers(0, 7)); last = int(rng.integers(0, 8))
    for r in range(N):
        kinds = rng.permutation(np.array([1, 2, 3, 4, 5, 7])).tolist(); kinds.insert(late, 0); kinds.insert(last, 6)
        for g, kind in enumerate(kinds):
            if kind < 5:
                n = (0, int(rng.choice(np.array([1, 15]))), Q - 1, Q, 16)[kind]
                if kind == 0 or (kind + r) % 2 == 0:
                    d = rng.integers(129, 250, 16); odd = r & 1 if kind == 0 else 1 if kind == 4 else int(rng.integers(0, 2))
                    d[0] -= (int(np.add.reduce(d)) - odd) & 3
                else:
                    d = rng.integers(3, 120, 16)
                p = rng.integers(0, 256 - d); e = int(np.add.reduce(d))
                v[r, g, :, :h] = p[:, None]; v[r, g, :, h:] = (p + d)[:, None]
                l[r, g] = np.where(rng.random((16, B)) < 0.5, rng.integers(0, h, (16, B)), rng.choice(np.array([0, h - 1]), (16, B)))
                a[r, g] = np.where(rng.random((16, D)) < 0.5, rng.integers(h, NV, (16, D)), rng.choice(np.array([h, NV - 1]), (16, D)))
                t = rng.choice(np.array([e - 1, e - 32, e - 33]), 16); o = rng.permutation(16); t[o[:n]] = e
                if kind == 0:
                    t[o[Q - 1:]] = e - 32 * (RO - 1) - rng.integers(0, 2, 17 - Q); c[r, g] = int(rng.integers(0, B))
                th[r, g] = t
            elif kind == 5:
                o = rng.permutation(B)[:M]; c[r, g] = o
                l[r, g][:, o] = 16 * np.arange(M)[None, :] + np.arange(16)[:, None]
                a[r, g] = rng.choice(np.array([0, NV - 1]), (16, D))
            elif kind == 6:
                j = np.arange(NV) & 15; v[r, g] = np.where((j > 0) & (j < 8), 0, np.maximum(v[r, g], 1))
                l[r, g] = 16 * rng.integers(0, M, (16, B)) + rng.integers(1, 8, (16, B))
                a[r, g] = 16 * rng.integers(0, M, (16, D)) + rng.integers(1, 8, (16, D)); a[r, g, 15] = 16 * rng.integers(0, M, D) + rng.integers(8, 16, D)
                x = rng.integers(0, 255, (16, M)); y = (32 - np.add.reduce(x[2:] * (14 * np.arange(2, 16) + 1)[:, None], axis=0)) & 4095
                over = (y > 4080).astype(np.int64); x[2] += over; y = y - 29 * over
                x[1] = np.minimum(y // 15, 255); x[0] = y - 15 * x[1]; z[r, g] = x
                b = (1103 * 32 >> 4) & (B - 1); c[r, g] = b; th[r, g] = 0
                ka[r, g, 15] = ((D - 1 - 37 * 32 - 613 * b) & (D - 1)) + D * int(rng.integers(0, 4096 // D))
            else:
                th[r, g] = 4080 * (r & 1)
    return pack(v, a, l, z, c, ka, th)
def setup_inputs_crowd(rng):
    v, a, l, z, c, ka, th = parts(rng); o = rng.permutation(8).tolist(); q = np.arange(N)
    x = rng.choice(np.array([0, M // 2, M - 1]), N)
    c[:, o[0]] = rng.integers(0, B, (N, 1))
    c[:, o[1]] = rng.integers(0, B, (N, 1)); c[q, o[1], x] = (c[q, o[1], x] + 1) % B
    for g in (o[2], o[3], o[7]):
        z[:, g] = rng.integers(0, 256, (16, 1)); c[:, g] = int(rng.integers(0, B))
    z[q, o[3], :, x] = rng.integers(0, 256, (N, 16))
    two = rng.integers(0, 256, (2, 16)); z[:, o[4]] = two[rng.integers(0, 2, (N, M))].transpose(0, 2, 1); c[:, o[4]] = rng.choice(rng.integers(0, B, 2), (N, M))
    z[:, o[5]] = rng.integers(0, 256, (16, 1))
    z[:, o[6]] = 0; ka[:, o[6]] = 0
    n = int(rng.integers(0, NV)); l[:, o[7]] = n; a[:, o[7]] = (n + int(rng.integers(1, NV))) % NV
    return pack(v, a, l, z, c, ka, th)
def check_inputs(d):
    bad = []
    for k, lo, hi in (("vf", 0, 255), ("ad", 0, NV - 1), ("le", 0, NV - 1), ("z0", 0, 255), ("cb", 0, B - 1), ("ka", 0, 4095), ("th", 0, 4080)):
        x = np.asarray(d[k]); x = x.astype(np.float32) if k in ("vf", "z0") else x
        if not (np.min(x) >= lo and np.max(x) <= hi): bad.append("range of " + k)
        elif k in ("vf", "z0") and np.any(x != np.floor(x)): bad.append("whole numbers in " + k)
    return bad
def hashed(z):
    return np.add.reduce(z * (14 * np.arange(16) + 1)[:, None], axis=2) & 4095
def values(v, x):
    return np.take_along_axis(v, x.reshape(N, 8, 1, 16 * M), 3).reshape(N, 8, 16, 16, M)
def first(x):
    return np.argmax(x[:, :, :, None] == x[:, :, None, :], axis=3) == np.arange(M)
def reference(vf, ad, le, z0, cb, ka, th):
    v = vf.astype(np.float32).astype(np.int32).reshape(N, 8, 16, NV); dirs = ad.astype(np.int64).reshape(N, 8, 16, D); blk = le.astype(np.int64).reshape(N, 8, 16, B)
    z = z0.astype(np.float32).astype(np.int64).reshape(N, 8, 16, M); c = np.stack([gentries(x) for x in cb]).astype(np.int64)
    kap = ka.astype(np.int64).reshape(N, 8, 16, 1); lim = th.astype(np.int64).reshape(N, 8, 16, 1)
    count = np.zeros((N, 8, M), np.int64); u = hashed(z)
    for m in range(1, RO + 1):
        names = np.take_along_axis(blk, c[:, :, None, :], 3)
        a = ((u[:, :, None, :] * kap >> 5) + (37 * u + 613 * c)[:, :, None, :]) & (D - 1)
        n = np.take_along_axis(dirs, a, 3)
        s = values(v, names); y = values(v, n)
        e = np.add.reduce(np.abs(s - y), axis=2)
        ok = e <= lim + 32 * count[:, :, None, :]
        names = np.where(ok, names, n)
        squash = np.add.reduce(ok.astype(np.int64), axis=2) < Q
        hi = np.where(squash[:, :, None, :], np.maximum.reduce(y, axis=3), np.maximum.reduce(np.where(ok[:, :, None], s, -1), axis=3))
        lo = np.where(squash[:, :, None, :], np.minimum.reduce(y, axis=3), np.minimum.reduce(np.where(ok[:, :, None], s, 256), axis=3))
        z = np.abs(z - ((hi.astype(np.int64) + lo) >> 1)); u = hashed(z)
        new = 16 * np.arange(M) + (u & 15)
        np.put_along_axis(v, new[:, :, None, :], z.astype(np.int32), 3)
        r, g, t = np.nonzero(first(c)); blk[r, g, :, c[r, g, t]] = names[r, g, :, t]
        if m == RO: break
        k = np.argmax(e, axis=2)
        col = np.take_along_axis(a, k[:, :, None, :], 2)[:, :, 0]
        r, g, t = np.nonzero(first(col)); dirs[r, g, k[r, g, t], col[r, g, t]] = new[r, g, t]
        count = count + squash; c = (1103 * u >> 4) & (B - 1)
        src = (np.arange(N)[:, None] - np.arange(M) // (M // N) - m) % N
        z = np.take_along_axis(z, src[:, None, None, :], 0); u = np.take_along_axis(u, src[:, None, :], 0)
        c = np.take_along_axis(c, src[:, None, :], 0); count = np.take_along_axis(count, src[:, None, :], 0)
    return {"yv": v.reshape(N, 128, NV).astype(np.float32).astype(BF), "yl": blk.reshape(N, 128, B).astype(np.float32), "yz": z.reshape(N, 128, M).astype(np.float32).astype(BF)}

@@ -1,0 +1,798 @@
+import numpy as np
+from concourse.mybir import AluOpType as OP, ActivationFunctionType as AF
+
+F32, BF, F16, I32, U16 = "float32", "bfloat16", "float16", "int32", "uint16"
+STEPS = 4
+Q4 = ((0, 64), (64, 128), (128, 192), (192, 256))
+CFG = {
+    "selg": 16, "trig": 16, "si": 1000.0, "sl": 2800.0,
+    "raw1": 128,
+    "p1": Q4,
+    "adv": (0,),
+    "sv": (),
+    "abss": (2, 3),
+    "p3": Q4,
+    "vv": (),
+    "tail": ((0, 128), (128, 192), (192, 256)),
+    "s16": True, "dc": ((0, 128), (128, 256)), "da": ((0, 256),), "selv": 0, "nks": False, "q1late": True,
+    4: {"adv": (0, 1), "abss": ()},
+    "loads": "aav", "seed": 7, "noise": 800.0, "win": 0.0, "iters": 300, "temp": 300.0, "moves": 33000, "temp2": 200.0,
+    "alts": ({"g": 1.2, "sc": 2.5, "f": 1.4, "lat": 120.0, "pe": 0.55},),
+    "lg": ((0, 128), (128, 256)), "ad": ((0, 128), (128, 256)),
+    "g": 1.56, "sc": 3.8, "f": 1.2, "lat": 60.0, "pe": 0.42, "bw": 250.0,
+}
+
+_S = {
+    "VW1": (8192, BF), "VW0": (8192, BF), "ADi": (2048, I32), "AD": (4352, BF), "X16": (2048, F16), "H0": (2048, BF),
+    "LEi": (512, I32), "LE": (768, F32),
+    "CBi": (16, I32), "KAi": (8, I32), "THi": (8, I32), "COLS": (64, F32), "CI": (16, I32), "CBF": (16, F32), "CBL": (16, U16),
+    "IO": (144, BF), "MI": (256, BF), "MI2": (16, BF), "MSK": (256, BF), "MK1": (256, BF), "CE": (256, F16),
+    "ID32": (128, F32), "MID32": (128, F32), "DM": (128, F32),
+    "Z1": (144, BF), "Z32": (144, BF), "ZM16": (144, BF), "Z16": (144, BF),
+    "EQ": (16, F32), "EQ2": (16, F32), "LT": (16, F32),
+    "SEL": (2048, BF), "SELH": (2048, BF), "TRI": (2048, BF),
+    "T16": (256, BF), "RSD": (256, F32), "MSKC": (256, BF),
+    "RSN": (1024, BF), "RSP": (1024, BF), "RSK": (256, F32),
+    "XI": (256, I32), "A32": (256, I32), "A16": (256, U16), "CW16": (16, U16), "CWS": (256, F32),
+    "S16": (256, U16), "SF": (256, F32), "G16": (2048, F16), "GB": (4096, BF), "N16": (256, U16), "NS": (256, F32),
+    "DD": (4096, BF), "RR": (4096, BF), "NOK": (256, BF), "IND": (256, BF), "RL": (256, BF), "T1": (256, F32),
+    "T2": (256, F32), "P16": (256, U16), "M0": (256, F32), "M1": (256, F32), "VV": (4096, BF), "HI": (4096, BF), "LO": (4096, BF),
+    "KTT": (256, F32), "KSC": (256, F32), "MX": (256, F32), "IND2": (256, BF), "OHS": (256, BF), "OHA": (256, F16),
+    "COL": (256, F16), "COW16": (16, U16), "COWS": (256, F32), "COW2": (256, F32), "Q1": (256, BF), "Q2": (256, BF),
+    "QC": (4096, BF), "QA": (4096, BF), "DSC": (256, F32), "DSA": (256, F32),
+    "LOFF": (16, U16), "AOFF": (16, U16), "ZR": (256, F32), "QB": (256, BF), "FL": (256, F16), "WS": (256, F32),
+    "WW16": (16, U16), "TI": (256, I32), "C32": (256, I32),
+}
+_S.update({"ZN1": (256, BF), "AN1": (256, BF), "ZO": (256, BF), "UN": (256, F16), "CN0": (256, F16), "CN1": (256, F16)})
+for _m in range(1, STEPS):
+    _S["PO%d" % _m] = (512, BF)
+    _S["PN%d" % (_m + 1)] = (512, BF)
+_AL = {n: 128 * i for i, n in enumerate(
+    "ID BO WT W16 W16O ONES KT SU OHM OH2P OH2M IE IOD RA0 RA1 RB0 RB1 I16 MI1 MBO MIH IQ IM512 IM4096 ICH ICL KH KL DK "
+    "BM128 BM8192 B8192 BM384 B32 BP DF GI TMP TMP2 I4096 I8192 IM8192".split())}
+_S["CM"] = (128 * len(_AL), BF)
+SCRATCH = {k: ("sbuf", [128, w], d) for k, (w, d) in _S.items()}
+for _b in range(8):
+    SCRATCH["P%d" % _b] = ("psum", [128, 512], F32)
+SEMAPHORES = ["cv", "cs", "cp", "cg", "sent"] + ["d%d" % i for i in range(48)] + \
+             ["arr%d_%d" % (m, b) for m in range(1, STEPS) for b in range(4)]
+SEM = {"v": "cv", "s": "cs", "p": "cp", "g": "cg"}
+TWO = (BF, F16, U16)
+(cP, cK, cG, cG15, cW, cKL, cKH, cCP, cTHR, c16K, cK1, cE15, cTH, c15K, cPAR, cEV, cP2048, cE2048, cQ2, cK2, cPD,
+ cW16, cT, cK8, cNK) = range(25)
+
+
+def A(n, lo=0, hi=None, st=1):
+    if n in _AL:
+        return ("CM", _AL[n] + lo, _AL[n] + (128 if hi is None else hi), st)
+    return (n, lo, _S[n][0] if hi is None else hi, st)
+
+
+def col(i):
+    return ("COLS", i, i + 1, 1)
+
+
+def IND(win, off):
+    return ("*", win, off)
+
+
+def width(a):
+    if a[0] == "*":
+        return 16 * (a[2][2] - a[2][1])
+    return len(range(a[1], a[2], a[3]))
+
+
+def psum(a):
+    return len(a[0]) == 2 and a[0][0] == "P" and a[0][1].isdigit()
+
+
+def dty(a):
+    return F32 if psum(a) else _S[a[0]][1]
+
+
+SLOT = {"X": (2, 1), "q2": (2, 2), "cw": (2, 3), "colw": (2, 3), "col2": (6, 2), "val": (4, 0), "rr": (4, 0), "U16": (4, 0), "Y23": (4, 1), "ww": (4, 1), "Y1": (4, 2),
+        "oh2": (4, 2), "xA": (4, 3), "Xz": (4, 3), "dn": (6, 0), "D": (6, 1), "colr": (6, 1), "oh": (6, 2), "U": (6, 3), "uc": (6, 3)}
+
+
+def ps(role, a, b, st=1):
+    h = a // 128
+    if role == "n":
+        q = a // 64
+        return ("P%d" % (q & 1), (q >> 1) * 64 + a % 64, (q >> 1) * 64 + a % 64 + b - a, st)
+    if role == "key":
+        return ("P%d" % (2 + h), a % 128, a % 128 + b - a, st)
+    if role == "dedA":
+        return ("P0", 256 + a, 256 + b, st)
+    if role == "dedC":
+        return ("P1", 256 + a, 256 + b, st)
+    if role == "rel":
+        return ("P%d" % (4 + (a // 512) % 3), 0, b - a, st)
+    if role == "crep":
+        return ("P7", a, b, st)
+    o = SLOT[role][1] * 128 + a % 128
+    return ("P%d" % (SLOT[role][0] + h), o, o + b - a, st)
+
+
+def plan(cfg):
+    ops = []
+    cyc = 0.83 * cfg["f"]
+    nks = cfg["nks"]; cfg0 = cfg
+
+    def add(eng, kind, args, rd, wr, cost, lat=0.0, xfer=0.0):
+        R, W = [], []
+        for x in rd:
+            if isinstance(x, tuple):
+                R += [x[1], x[2]] if x[0] == "*" else [x]
+        for x in wr:
+            if x[0] == "*":
+                W.append(x[1]); R.append(x[2])
+            else:
+                W.append(x)
+        ops.append({"e": eng, "k": kind, "a": args, "r": R, "w": W, "c": cost, "l": lat, "x": xfer})
+
+    def vcost(out, ins, tt=False):
+        n = width(out)
+        if out[0] == "*":
+            return 50 + n * cfg["sc"] * 0.83
+        if ins[0][0] == "*":
+            return 50 + n * cfg["g"] * 0.83
+        if tt:
+            return max(64, n * (1 if any(psum(x) for x in ins) else 2)) * cyc
+        two = all(dty(x) in TWO for x in [out] + ins)
+        return max(64, n * (0.5 if two else 1)) * cyc
+
+    def ts(out, i, s1, op0, s2=None, op1=None):
+        add("v", "ts", (out, i, s1, s2, op0, op1), [i, s1, s2], [out], vcost(out, [i]))
+
+    def cp(out, i):
+        add("v", "cp", (out, i), [i], [out], vcost(out, [i]))
+
+    def tt(out, a, b, op):
+        add("v", "tt", (out, a, b, op), [a, b], [out], vcost(out, [a, b], True))
+
+    def ms(out, v):
+        add("v", "ms", (out, v), [], [out], vcost(out, [out]))
+
+    def scan(out, d0, d1, op1, op0=OP.add, init=0.0):
+        add("v", "scan", (out, d0, d1, op1, op0, init), [d0, d1], [out], vcost(out, [d0, d1]))
+
+    def tr(out, i):
+        add("v", "tr", (out, i), [i], [out], vcost(out, [i]))
+
+    def act(out, i, f=AF.Identity, bias=0.0, scale=1.0):
+        n = width(out)
+        c = 65 + n * cfg["g"] * 0.83 if i[0] == "*" else max(64, n) * cyc
+        add("s", "act", (out, i, f, bias, scale), [i, bias, scale], [out], c)
+
+    def mm(items):
+        c = sum(max(64, width(o)) * (4 if dty(r) == F32 else 1) for o, l, r in items) * cfg["pe"] * cfg["f"] + 60
+        add("p", "mm", items, [x for o, l, r in items for x in (l, r)], [o for o, l, r in items], c)
+
+    def dma(out, i, nbytes, rd, wr):
+        add("y", "dma", (out, i), rd, wr, 60.0, 2000.0, nbytes / cfg["bw"])
+
+    def iota(out, pat, base, cm):
+        add("g", "iota", (out, pat, base, cm), [], [out], 130 + 2 * width(out) * cyc)
+
+    def asel(out, i, pat, op, base, cm):
+        add("g", "asel", (out, i, pat, op, base, cm), [i], [out], 170 + 2 * width(out) * cyc)
+
+    def load(name, src, lo=0, hi=None):
+        at = 4096 if name == "VW1" else 0
+        o = A(name, at + lo, None if hi is None else at + hi)
+        dma(o, ("in", src, lo, o[2] - at), 128 * width(o) * (2 if dty(o) in TWO else 4), [], [o])
+
+    def blk(n, k):
+        return A(n, 128 * k, 128 * k + 128)
+
+    def zw(n, k):
+        return A(n, 15 - k, 143 - k)
+
+    load("ZN1", "z0"); load("KAi", "ka", 0, 1); load("CBi", "cb"); load("THi", "th", 0, 1)
+    big = {"a": [("ADi", "ad", 0, 1024), ("ADi", "ad", 1024, 2048)],
+           "v": [("LEi", "le", 0, 512), ("VW1", "vf", 0, 2048), ("VW1", "vf", 2048, 4096)]}
+    for x in (big["a"] + big["v"] if cfg["loads"] == "aav" else big["v"] + big["a"]):
+        load(*x)
+    iota(A("CI", 0, 1), [[0, 1]], 0, 1)
+    iota(A("DF"), [[1, 128]], 0, -1); iota(A("GI"), [[16, 8], [0, 16]], 0, 0); iota(A("MI"), [[0, 16], [1, 16]], 0, 0)
+    iota(A("IO"), [[1, 144]], 0, 0); iota(A("MI2"), [[2, 8], [0, 2]], 0, 0); iota(A("T16"), [[16, 256]], 0, 0)
+    ci = lambda i: A("CI", i, i + 1)
+
+    def aff(c, src, mul, plus):
+        act(col(c), col(src), bias=plus, scale=mul)
+
+    ts(ci(1), ci(0), 15, OP.bitwise_and); cp(col(cK), ci(1)); tt(col(cG), ci(0), ci(1), OP.subtract)
+    ts(ci(4), ci(0), 1, OP.bitwise_and); cp(col(cPAR), ci(4))
+    aff(cG15, cG, 1.0, 15.0); aff(cW, cK, 14.0, 1.0); aff(c16K, cK, -1.0, 16.0); aff(cK1, cK, 1.0, 1.0)
+    aff(c15K, cK, -1.0, 15.0); aff(cEV, cPAR, -1.0, 1.0); aff(cP2048, cPAR, 2048.0, 0.0); aff(cE2048, cPAR, -2048.0, 2048.0)
+    aff(cQ2, cPAR, 24576.0, -8192.0); aff(cPD, cPAR, 4096.0, -2048.0)
+    act(col(cK2), col(cPAR), bias=col(cK), scale=-1.0); act(col(cE15), col(cK), AF.Relu, bias=-14.0)
+    aff(cT, cE15, 1.0, -1.0)
+    ts(ci(2), A("KAi", 0, 1), 1184.0, OP.add); ts(ci(3), ci(2), 31, OP.bitwise_and); cp(col(cKL), ci(3))
+    tt(col(cKH), ci(2), ci(3), OP.subtract); aff(cCP, cKL, 2048.0, 40960.0)
+    ts(col(cTH), A("THi", 0, 1), 16.0, OP.mult, -65536.0, OP.add); act(col(cTHR), col(cTH), bias=col(c15K))
+    ts(ci(5), ci(1), 14.0, OP.mult, 9.0, OP.add); ts(ci(6), ci(5), 15, OP.bitwise_and); ts(col(cW16), ci(6), -8.0, OP.add)
+    ms(A("ONES"), 1.0); ms(A("AN1"), 128.0)
+    if nks:
+        aff(cTHR, cTHR, -1.0, -0.5); aff(cK1, cK, 1.0, 9.0); aff(cK8, cK, 1.0, 8.0)
+    for n, v in (("ID", 1.0), ("I16", 8.0 if nks else 16.0), ("I4096", 4096.0), ("I8192", 8192.0), ("IM8192", -8192.0),
+                 ("MI1", -1.0), ("MIH", -0.5), ("IQ", 0.25), ("IM512", -512.0), ("IM4096", -4096.0),
+                 ("ICH", 19456.0), ("ICL", 160.0), ("KH", col(cKH)), ("KL", col(cKL)), ("DK", col(cK8 if nks else cK)), ("IE", col(cEV)),
+                 ("IOD", col(cPAR))):
+        ts(A(n), A("DF"), 0.0, OP.is_equal, v, OP.mult)
+    for n, v in (("BO", 1.0), ("WT", col(cW)), ("W16", col(cW16)), ("MBO", -1.0), ("BM128", -128.0), ("BM8192", -8192.0),
+                 ("B8192", 8192.0), ("BM384", -384.0), ("B32", 1.0 / (64 if nks else 32)), ("BP", col(cPD)), ("TMP", col(cE15))):
+        ts(A(n), A("GI"), col(cG), OP.is_equal, v, OP.mult)
+    act(A("ID32"), A("ID")); act(A("MID32"), A("ID"), scale=-1.0)
+    act(A("KT"), A("ONES"), scale=col(c15K))
+    tt(A("DM"), A("TMP"), A("ID"), OP.subtract)
+    for h in range(2):
+        sel = col(cPAR if h else cEV)
+        ts(A("RB%d" % h), A("DF"), 1.0 - h, OP.is_equal, sel, OP.mult)
+        ts(A("TMP2"), A("DF"), 0.0 - h, OP.is_equal, sel, OP.mult)
+        tt(A("RA%d" % h), A("TMP2"), A("RB%d" % h), OP.subtract)
+    ts(A("OHM"), A("DF"), 1.0, OP.is_equal, col(cT), OP.mult)
+    asel(A("SU"), A("BO"), [[-1, 128]], OP.is_ge, 0, 1)
+    asel(A("W16O"), A("W16"), [[0, 64], [1, 2]], OP.is_equal, -1, 0)
+    asel(A("OH2P"), A("B8192"), [[2, 64], [0, 2]], OP.is_equal, 1, -1)
+    asel(A("OH2M"), A("BM8192"), [[2, 64], [0, 2]], OP.is_equal, -1, -1)
+    ts(A("MSK"), A("MI"), col(cK), OP.not_equal, -4194304.0, OP.mult)
+    ts(A("MK1"), A("MI"), col(cK), OP.is_equal)
+    for n, v in (("Z1", 1.0), ("Z32", 32.0), ("ZM16", -16.0), ("Z16", 16.0)):
+        ts(A(n), A("IO"), col(cG15), OP.is_equal, v, OP.mult)
+    ts(A("LT"), A("MI", 0, 16), col(cK), OP.is_gt); ts(A("EQ2"), A("MI2"), col(cK2), OP.is_equal)
+    ts(A("EQ"), A("MI", 0, 16), col(cK), OP.is_equal)
+    for k in range(16):
+        if cfg["raw1"] and k < cfg["selg"]:
+            asel(blk("SEL", k), A("ID"), [[0, 8], [1, 16]], OP.is_equal, -k, 0)
+        elif cfg["raw1"]:
+            ts(blk("SEL", k), A("ID"), A("EQ", k, k + 1), OP.mult)
+        if k < cfg["selv"]:
+            ts(blk("SELH", k), zw("Z1", k), A("EQ2", k, k + 1), OP.mult)
+        else:
+            act(blk("SELH", k), zw("Z1", k), scale=A("EQ2", k, k + 1))
+        if k < cfg["trig"]:
+            asel(blk("TRI", k), A("BM8192"), [[16, 8], [0, 16]], OP.is_ge, k - 1, -1)
+        else:
+            act(blk("TRI", k), A("BM8192"), scale=A("LT", k, k + 1))
+    aff(cNK, cK, -1.0, -1.0); act(A("MSKC"), A("MSK"), bias=256.0)
+    act(A("RSD"), A("MSK"), bias=1.0e9, scale=0.0); act(A("RSD", 0, 256, 16), A("IO", 0, 16), bias=col(cNK), scale=-16.0)
+    ms(A("RSN"), 0.0); ms(A("RSN", 0, 1024, 16), -512.0); act(A("RSP"), A("RSN"), scale=-1.0)
+    ms(A("RSK"), 0.0); ms(A("RSK", 0, 256, 16), -3.0e7)
+    cp(A("LE", 256, 768), A("LEi"))
+    if cfg["q1late"]:
+        act(A("AD", 0, 256), A("MSK"), scale=0.0)
+    for a in range(0, 2048, 512):
+        x, hh = A("X16", a, a + 512), A("H0", a, a + 512)
+        ts(x, A("ADi", a, a + 512), -2048.0, OP.add); ts(hh, x, 201326592.0, OP.add, -201326592.0, OP.add)
+        for h in range(2):
+            y = ps("rel", 2 * a + 512 * h, 2 * a + 512 * h + 512)
+            mm([(y, A("RA%d" % h), hh), (y, A("RB%d" % h), x)])
+            act(A("AD", 256 + 2048 * h + a, 256 + 2048 * h + a + 512), y, bias=col(cE2048))
+    HALF = ((0, 128), (128, 256))
+
+    def segs(m, side, part, a, b):
+        if side == "N" and m == 1:
+            return [(a, b, A("AN1" if part else "ZN1", a, b))]
+        out = []
+        for bb in range(a // 64, (b + 63) // 64):
+            x0, x1 = max(a, 64 * bb), min(b, 64 * bb + 64)
+            n = "PN%d" % m if side == "N" else "PO%d" % m if (bb + m) % 4 else "PN%d" % (m + 1)
+            out.append((x0, x1, A(n, 64 * (bb + part) + x0, 64 * (bb + part) + x1)))
+        return out
+
+    ts(A("CBF"), A("CBi"), -256.0, OP.add); cp(A("CBL"), A("IO", 0, 16))
+    tt(A("CE"), IND(A("CBF"), A("CBL")), A("MK1"), OP.mult)
+    mm([(ps("crep", 0, 256), A("BO"), A("CE"))])
+    cp(A("CN1"), ps("crep", 0, 256))
+
+    def wrap(out, p, a, b):
+        scan(A(out, a, b), A("RSK", 0, b - a), p, OP.max)
+
+    def dedupe(rep, wf, own, q, ds, r1, msk, off, a, b):
+        ja, jb = a // 16, b // 16
+        it = [(ps(r1, a, b), A("ID"), A(msk, a, b))] + [(ps(r1, a, b), l, r) for l, r in own]
+        for j in range(ja if q == "QC" else 0, jb):
+            lo = max(a, 16 * j)
+            ts(A(q, 240 * j + lo, 240 * j + b), A(rep, lo, b), wf(j), OP.is_equal)
+            lo = max(a, 16 * j + 16)
+            if lo < b:
+                it.append((ps(r1, lo, b), A("BM8192"), A(q, 240 * j + lo, 240 * j + b)))
+        mm(it + [(ps(r1, a + k, b, 16), blk("TRI", k), A(q, 256 * ja + k, 256 * jb, 256)) for k in range(16)])
+        scan(A(ds, a, b), A("RSD", a, b), ps(r1, a, b), OP.max, OP.min, 1.0e6)
+        ts(A(off, ja, jb), A(ds, a + 15, b, 16), 256.0, OP.add)
+
+    ADW, LEW = A("AD", 256, 4352), A("LE", 256, 768)
+    for m in range(1, STEPS + 1):
+        last = m == STEPS
+        cfg = dict(cfg0); cfg.update(cfg0.get(m, {}))
+        U, C = "UN", "CN%d" % (m % 2)
+        VW, VN = "VW%d" % (m % 2), "VW%d" % ((m + 1) % 2)
+        VF = A(VW, 4096, 8192)
+        for h in range(2, 4):
+            x, y = A(VN, 2048 * h, 2048 * h + 2048), A(VW, 2048 * h, 2048 * h + 2048)
+            dma(x, y, 128 * 4096, [y], [x])
+        for a, b in cfg["ad"]:
+            zs = segs(m, "N", 0, a, b)
+            for x0, x1, z in zs:
+                mm([(ps("U", x0, x1), A("WT"), z)])
+            act(A("QB", a, b), ps("U", a, b), bias=135.5 + 2.0 ** -13, scale=2.0 ** -12)
+            mm([(ps("uc", a, b), A("IM4096"), A("QB", a, b))] + [(ps("uc", x0, x1), A("WT"), z) for x0, x1, z in zs])
+            ts(A(U, a, b), ps("uc", a, b), 4096.0 * 136 - 2048, OP.add)
+            if m > 1:
+                ts(A("TI", a, b), ps("uc", a, b), 4096.0 * 136, OP.add, 1103.0, OP.mult)
+                ts(A("C32", a, b), A("TI", a, b), 4, OP.arith_shift_right, 511, OP.bitwise_and)
+                ts(A(C, a, b), A("C32", a, b), -256.0, OP.add)
+            x = ps("X", a, b)
+            mm([(x, A("KH"), A(U, a, b)), (x, A("KL"), A(U, a, b)), (x, A("ICH"), A(C, a, b)), (x, A("ICL"), A(C, a, b))])
+            ts(A("XI", a, b), x, col(cCP), OP.add)
+            ts(A("A32", a, b), A("XI", a, b), 5, OP.arith_shift_right, 2047, OP.bitwise_and)
+            r = min(b, max(a, cfg["raw1"])) if m == 1 else a
+            if r > a:
+                cp(A("A16", a, r), A("A32", a, r))
+            if r < b:
+                ts(A("A16", r, b), A("A32", r, b), col(cP2048), OP.add)
+            ja, jb = a // 16, b // 16
+            if m == 1:
+                cp(A("CW16", ja, jb), A("CBi", ja, jb))
+            else:
+                mm([(ps("cw", a, b), A("ID"), A("MSK", a, b)), (ps("cw", a, b), A("ID"), A(C, a, b))])
+                wrap("CWS", ps("cw", a, b), a, b)
+                ts(A("CW16", ja, jb), A("CWS", a + 15, b, 16), 256.0, OP.add)
+            act(A("SF", a, b), IND(LEW, A("CW16", ja, jb)))
+            cp(A("S16", a, b), A("SF", a, b) if cfg["s16"] else IND(LEW, A("CW16", ja, jb)))
+        for q, (a, b) in enumerate(cfg["p1"]):
+            lo, hi = 16 * a, 16 * b
+            if m == 1 and a < cfg["raw1"]:
+                ts(A("G16", lo, hi), IND(A("ADi"), A("A16", a, b)), -2048.0, OP.add); gb, sel, off = "G16", "SEL", 2048.0
+            else:
+                (cp if q in cfg["adv"] else act)(A("GB", lo, hi), IND(ADW, A("A16", a, b)))
+                gb, sel, off = "GB", "SELH", 0.0
+            mm([(ps("n", a, b), blk(sel, k), A(gb, lo + k, hi, 16)) for k in range(16)])
+            ts(A("N16", a, b), ps("n", a, b), off, OP.add)
+            act(A("NS", a, b), ps("n", a, b), bias=off)
+            sv = A(VW, (lo + 2048) % 4096, (lo + 2048) % 4096 + hi - lo)
+            (cp if q in cfg["sv"] else act)(sv, IND(VF, A("S16", a, b)))
+            tt(A("DD", lo, hi), IND(VF, A("N16", a, b)), sv, OP.subtract)
+            key = ps("key", a, b)
+            it = [(key, A("ID"), A("KT", 0, b - a)), (key, A("IM512"), segs(m, "N", 1, a, b)[0][2])]
+            if q in cfg["abss"]:
+                act(A("RR", lo, hi), A("DD", lo, hi), AF.Abs)
+                it += [(key, zw("Z16", k), A("RR", lo + k, hi, 16)) for k in range(16)]
+            else:
+                ts(A("RR", lo, hi), A("DD", lo, hi), 0.0, OP.max)
+                it += [(key, zw("ZM16", k), A("DD", lo + k, hi, 16)) for k in range(16)]
+                it += [(key, zw("Z32", k), A("RR", lo + k, hi, 16)) for k in range(16)]
+            mm(it)
+        cw = (lambda j: A("CBF", j, j + 1)) if m == 1 else (lambda j: A("CWS", 16 * j + 15, 16 * j + 16))
+        for a, b in cfg["dc"]:
+            dedupe(C, cw, [(A("ID"), A(C, a, b))], "QC", "DSC", "dedC", "MSKC", "LOFF", a, b)
+        for a, b in cfg["lg"]:
+            ja, jb = a // 16, b // 16
+            nok, one = A("NOK", a, b), A("ONES", 0, b - a)
+            if nks:
+                act(nok, ps("key", a, b), AF.Sign, bias=col(cTHR))
+            else:
+                ts(nok, ps("key", a, b), col(cTHR), OP.is_gt)
+            mm([(ps("val", a, b), A("SU"), nok)])
+            act(A("IND", a, b), ps("val", a, b), AF.Sign, bias=col(c16K), scale=-1.0)
+            an = segs(m, "N", 1, a, b)
+            ao = [(a, b, A("Q2", a, b))] if last else segs(m, "O", 1, a, b)
+            mm([(ps("xA", a, b), A("B32"), nok)] + [(ps("xA", x0, x1), A("ID"), x) for x0, x1, x in an])
+            for x0, x1, x in ao:
+                act(x, ps("xA", x0, x1), bias=0.421875 if nks else 0.171875)
+            mm([(ps("rr", a, b), A("I16"), nok), (ps("rr", a, b), A("MBO"), A("IND", a, b))])
+            act(A("RL", a, b), ps("rr", a, b), AF.Relu, bias=col(cK1))
+            y = ps("Y23", a, b)
+            h = a // 128
+            mm([(y, A("ID"), A("T16", a, b)), (y, A("DK"), one), (y, A("BM384" if h else "BM128"), one), (y, A("I16"), nok)] +
+               [(ps("Y23", x0, x1), A("IM8192"), x) for x0, x1, x in an] + [(ps("Y23", x0, x1), A("I8192"), x) for x0, x1, x in ao] +
+               [(y, A("MI1"), A("RL", a, b))])
+            tt(A("T2", a, b), y, A("NS", a, b), OP.min)
+            ts(A("P16", a, b), A("T2", a, b), 2048.0 * (h + 1), OP.add)
+            if nks:
+                mm([(ps("dn", a, b), A("ID32"), A("SF", a, b)), (ps("dn", a, b), A("IM4096"), nok)])
+                act(A("M0", a, b), ps("dn", a, b), AF.Relu, bias=-4096.0)
+                mm([(ps("uc", a, b), A("ID32"), A("NS", a, b)), (ps("uc", a, b), A("I4096"), nok)])
+                act(A("M1", a, b), ps("uc", a, b), AF.Relu, bias=-4096.0)
+            else:
+                mm([(ps("dn", a, b), A("ID32"), A("NS", a, b)), (ps("dn", a, b), A("MID32"), A("SF", a, b))])
+                tt(A("M1", a, b), ps("dn", a, b), nok, OP.mult)
+            if not last:
+                tr(A("KTT", a, b), ps("key", a, b))
+                scan(A("KSC", a, b), A("RSK", 0, b - a), A("KTT", a, b), OP.max)
+                tr(A("MX", a, b), A("KSC", a, b))
+                mm([(ps("D", a, b), A("DM"), A("MX", a, b))])
+                act(A("IND2", a, b), ps("D", a, b), AF.Relu, bias=1.0, scale=-1.0)
+                i2, oha, msk = A("IND2", a, b), A("OHA", a, b), A("MSK", a, b)
+                mm([(ps("oh", a, b), A("ID"), i2), (ps("oh", a, b), A("OHM"), i2)])
+                tt(oha, ps("oh", a, b), A("A32", a, b), OP.mult)
+                mm([(ps("oh2", a, b), A("OH2P"), i2), (ps("oh2", a, b), A("OH2M"), i2)])
+                act(A("OHS", a, b), ps("oh2", a, b), bias=1.0, scale=-1.0 / 8192)
+                mm([(ps("colr", a, b), A("BO"), oha)])
+                cp(A("COL", a, b), ps("colr", a, b))
+                mm([(ps("colw", a, b), A("ID"), msk), (ps("colw", a, b), A("BO"), oha)])
+                wrap("COWS", ps("colw", a, b), a, b)
+                if not cfg["q1late"]:
+                    mm([(ps("col2", a, b), A("ID"), msk), (ps("col2", a, b), A("BP"), i2), (ps("col2", a, b), A("BO"), oha)])
+                    wrap("COW2", ps("col2", a, b), a, b)
+                    cp(A("COW16", ja, jb), A("COW2", a + 15, b, 16))
+                    tt(A("Q1", a, b), IND(ADW, A("COW16", ja, jb)), A("OHS", a, b), OP.mult)
+        for a, b in reversed(cfg["dc"]):
+            tt(IND(A("LE"), A("LOFF", a // 16, b // 16)), A("M0" if nks else "SF", a, b), A("M1", a, b), OP.add)
+        if last:
+            dma(("out", "yl", 0, 512), LEW, 128 * 2048, [LEW], [])
+        else:
+            for a, b in cfg["da"]:
+                dedupe("COL", lambda j: A("COWS", 16 * j + 15, 16 * j + 16), [(A("BP"), A("IND2", a, b)), (A("BO"), A("OHA", a, b))],
+                       "QA", "DSA", "dedA", "MSK", "AOFF", a, b)
+            for a, b in cfg["da"] if cfg["q1late"] else ():
+                tt(A("Q1", a, b), IND(A("AD"), A("AOFF", a // 16, b // 16)), A("OHS", a, b), OP.mult)
+        for q, (a, b) in enumerate(cfg["p3"]):
+            lo, hi = 16 * a, 16 * b
+            src = IND(A(VW, 2048 if a < 128 else 0, 8192), A("P16", a, b))
+            (cp if q in cfg["vv"] else act)(A("VV", lo, hi), src)
+            scan(A("HI", lo, hi), A("RSN", 0, hi - lo), A("VV", lo, hi), OP.max)
+            scan(A("LO", lo, hi), A("RSP", 0, hi - lo), A("VV", lo, hi), OP.min)
+        for a, b in cfg["tail"]:
+            ja, jb, lo, hi = a // 16, b // 16, 16 * a, 16 * b
+            zo = A("ZO", a, b)
+            x = ps("Xz", a, b)
+            mm([(x, A("IQ"), A("ONES", 0, b - a))] + [(ps("Xz", x0, x1), A("ID"), z) for x0, x1, z in segs(m, "N", 0, a, b)] +
+               [(x, A("MIH"), A("HI", lo + 15, hi, 16)), (x, A("MIH"), A("LO", lo + 15, hi, 16))])
+            act(A("ZR", a, b), x, bias=12582912.0)
+            act(zo, A("ZR", a, b), AF.Abs, bias=-12582912.0)
+            mm([(ps("U16", a, b), A("W16"), zo)])
+            ts(A("FL", a, b), ps("U16", a, b), -1.0, OP.mult, -24568.5, OP.add)
+            w = ps("ww", a, b)
+            mm([(w, A("ID"), A("T16", a, b)), (w, A("ID"), A("MSK", 0, b - a)), (w, A("W16"), zo), (w, A("ID"), A("FL", a, b))])
+            wrap("WS", w, a, b)
+            ts(A("WW16", ja, jb), A("WS", a + 15, b, 16), 24576.0 - lo, OP.add)
+            yv = A(VN, 4096 + lo, 4096 + hi)
+            cp(IND(yv, A("WW16", ja, jb)), zo)
+            if last:
+                dma(("out", "yv", lo, hi), yv, 4096 * (b - a), [yv], [])
+                dma(("out", "yz", a, b), zo, 256 * (b - a), [zo], [])
+                continue
+            y = ps("q2", a, b)
+            mm([(y, A("IE"), A("T16", a, b)), (y, A("OH2P"), A("IND2", a, b)), (y, A("OH2M"), A("IND2", a, b)),
+                (y, A("W16O"), zo), (y, A("IOD"), A("FL", a, b))])
+            act(A("Q2", a, b), y, AF.Relu, bias=col(cQ2))
+            for x0, x1, pk in segs(m, "O", 0, a, b):
+                act(pk, A("ZR", x0, x1), AF.Abs, bias=-12582912.0)
+            for bb in range(4):
+                if a < 64 * bb + 64 <= b and (bb + m) % 4:
+                    src, dst = A("PO%d" % m, 128 * bb, 128 * bb + 128), A("PN%d" % (m + 1), 128 * bb, 128 * bb + 128)
+                    add("g", "send", (m, bb, src, dst), [src], [dst], cfg["si"], cfg["sl"])
+        if not last:
+            for a, b in cfg["tail"]:
+                ja, jb = a // 16, b // 16
+                tt(IND(A("AD"), A("AOFF", ja, jb)), A("Q1", a, b), A("Q2", a, b), OP.add)
+    used = [(x[1], x[2]) for o in ops for x in o["r"] if x[0] == "CM"]
+    names = {x[0] for o in ops for x in o["r"]}
+    return [o for o in ops if not o["w"] or (o["w"][0][0] in names and (o["w"][0][0] != "CM" or any(
+        lo < o["w"][0][2] and o["w"][0][1] < hi for lo, hi in used)))]
+
+
+def schedule(ops, cfg):
+    n = len(ops)
+    hist = {}
+    for i, o in enumerate(ops):
+        d = set()
+        for accs, w in ((o["r"], False), (o["w"], True)):
+            for x in accs:
+                for j, lo, hi, jw in hist.get(x[0], ()):
+                    if (w or jw) and lo < x[2] and x[1] < hi and j != i:
+                        d.add(j)
+        for accs, w in ((o["r"], False), (o["w"], True)):
+            for x in accs:
+                h = hist.setdefault(x[0], [])
+                if w and x[3] == 1:
+                    h[:] = [y for y in h if not (x[1] <= y[1] and y[2] <= x[2])]
+                h.append((i, x[1], x[2], w))
+        o["d"] = d
+        o["b"] = {x[0] for x in o["r"] + o["w"] if psum(x)}
+    succ = [[] for _ in ops]
+    for i, o in enumerate(ops):
+        for j in o["d"]:
+            succ[j].append(i)
+    lat = cfg["lat"]
+    eng = [o["e"] for o in ops]; cost = [o["c"] for o in ops]; after = [o["l"] for o in ops]; xf = [o["x"] for o in ops]
+    banks = [sorted(o["b"]) for o in ops]; deps = [sorted(o["d"]) for o in ops]
+
+    def run(pr, win):
+        left = [len(d) for d in deps]
+        base = [0.0] * n
+        ready = {e: [] for e in "vspgy"}
+        for i in range(n):
+            if left[i] == 0:
+                ready[eng[i]].append(i)
+        free = {e: 0.0 for e in "vspgyx"}; fin = [0.0] * n; start = [0.0] * n; bank = {}; order = []; extra = [()] * n
+        for _ in range(n):
+            best = None
+            for e, rl in ready.items():
+                if not rl:
+                    continue
+                es = []
+                for i in rl:
+                    t = base[i] if base[i] > free[e] else free[e]
+                    for b in banks[i]:
+                        for e2, j in bank.get(b, {}).items():
+                            if e2 != e and fin[j] + lat > t:
+                                t = fin[j] + lat
+                    es.append(t)
+                t0 = min(es)
+                if best is None or t0 < best[0]:
+                    best = (t0, e, es)
+            t0, e, es = best
+            rl = ready[e]
+            if e == "y":
+                x = min((rl[x], x) for x in range(len(rl)) if es[x] <= t0 + 1.0)[1]
+            else:
+                x = max((pr[rl[x]], x) for x in range(len(rl)) if es[x] <= t0 + win[rl[x]])[1]
+            i = rl.pop(x)
+            ex = []
+            for b in banks[i]:
+                ex += [j for e2, j in bank.get(b, {}).items() if e2 != e]
+                bank.setdefault(b, {})[e] = i
+            extra[i] = ex; start[i] = es[x]
+            free[e] = es[x] + cost[i]; fin[i] = free[e] + after[i]
+            if xf[i]:
+                fin[i] = free["x"] = max(fin[i], free["x"]) + xf[i]
+            order.append(i)
+            for j in succ[i]:
+                left[j] -= 1
+                if fin[i] + lat > base[j]:
+                    base[j] = fin[i] + lat
+                if left[j] == 0:
+                    ready[eng[j]].append(j)
+        return max(fin), order, extra, start
+
+    def levels(order, extra, w):
+        pr = [0.0] * n; nxt = {}
+        for i in reversed(order):
+            t = max([pr[j] + lat for j in succ[i]] + [0.0]) + after[i] + xf[i]
+            j = nxt.get(eng[i])
+            if j is not None and w:
+                t = max(t, t + w * (pr[j] - t))
+            pr[i] = cost[i] + t; nxt[eng[i]] = i
+        return pr
+
+    def score(r):
+        tot = r[0]
+        for c2, l2 in alts:
+            free = {e: 0.0 for e in "vspgyx"}; fin = [0.0] * n
+            for i in r[1]:
+                t = free[eng[i]]
+                for j in deps[i]:
+                    if fin[j] + l2 > t:
+                        t = fin[j] + l2
+                for j in r[2][i]:
+                    if fin[j] + l2 > t:
+                        t = fin[j] + l2
+                free[eng[i]] = t + c2[i]; fin[i] = t + c2[i] + after[i]
+                if xf[i]:
+                    fin[i] = free["x"] = max(fin[i], free["x"]) + xf[i]
+            tot += max(fin)
+        return tot
+
+    alts = []
+    if cfg["iters"] or cfg["moves"]:
+        for alt in cfg["alts"]:
+            c2 = dict(cfg); c2.update(alt)
+            alts.append(([o["c"] for o in plan(c2)], c2["lat"]))
+    rng = np.random.RandomState(cfg["seed"])
+    pr = levels(list(range(n)), None, 0.0); win = [cfg["win"]] * n
+    best = run(pr, win); bs = score(best); top = (bs, best)
+    for it in range(cfg["iters"]):
+        p2, w2 = list(pr), list(win)
+        u = rng.uniform()
+        if u < 0.15:
+            lv = levels(best[1], best[2], float(rng.uniform(0.2, 1.0))); a = float(rng.uniform(0.1, 1.0))
+            p2 = [(1 - a) * x + a * y for x, y in zip(pr, lv)]
+        else:
+            t0 = rng.uniform(0, best[0]); sp = rng.uniform(2000, 12000)
+            for i in range(n):
+                if t0 <= best[3][i] < t0 + sp and rng.uniform() < 0.3:
+                    p2[i] += float(rng.normal(0, cfg["noise"]))
+                    if rng.uniform() < 0.3:
+                        w2[i] = float(rng.choice([0.0, 70.0, 200.0, 500.0]))
+        r = run(p2, w2); s = score(r)
+        if s <= bs + cfg["temp"] * (1.0 - it / cfg["iters"]) * rng.exponential():
+            best, bs, pr, win = r, s, p2, w2
+            if s < top[0]:
+                top = (s, r)
+    order = list(top[1][1])
+    E = {e: x for x, e in enumerate("vspgy")}
+    en = [E[e] for e in eng]; bk = [[int(b[1:]) for b in bs_] for bs_ in banks]
+    sets = [(cost, lat)] + alts
+
+    if cfg.get("order"):
+        order = [(ord(cfg["order"][2 * x]) - 48) * 40 + ord(cfg["order"][2 * x + 1]) - 48 for x in range(n)]
+
+    def timed(order, c2, l2, old=None, lo=0):
+        if old is None:
+            x0 = 0; snaps = []
+            free = [0.0] * 5; prev = [-1] * 5; fin = [0.0] * n; why = [-1] * n; xfree = 0.0
+            lastb = [[-1, -1, -1] for _ in range(8)]
+        else:
+            x0 = lo >> 5; snaps = old[3][:x0]; sn = old[3][x0]; x0 <<= 5
+            free = list(sn[0]); prev = list(sn[1]); xfree = sn[2]; lastb = [list(y) for y in sn[3]]
+            fin = list(old[1]); why = list(old[2])
+        for x in range(x0, n):
+            if not x & 31:
+                snaps.append((list(free), list(prev), xfree, [list(y) for y in lastb]))
+            i = order[x]
+            e = en[i]; t = free[e]; w = prev[e]
+            for j in deps[i]:
+                if fin[j] > t:
+                    t = fin[j]; w = j
+            for b in bk[i]:
+                lb = lastb[b]
+                for e2 in (0, 1, 2):
+                    j = lb[e2]
+                    if j >= 0 and e2 != e and fin[j] > t:
+                        t = fin[j]; w = j
+                lb[e] = i
+            why[i] = w; prev[e] = i
+            t += c2[i]; free[e] = t; t += after[i]
+            if xf[i]:
+                t = xfree = (t if t > xfree else xfree) + xf[i]
+            fin[i] = t + l2
+        end = max(fin)
+        return end - l2, fin, why, snaps
+
+    def total(order, olds=None, lo=0):
+        rs = [timed(order, c2, l2, olds[x] if olds else None, lo) for x, (c2, l2) in enumerate(sets)]
+        return sum(r[0] for r in rs), rs
+
+    dset = [set(d) for d in deps]
+    cur, rs = total(order); keep = (cur, list(order))
+    for it in range(cfg["moves"]):
+        pos = [0] * n
+        for x, i in enumerate(order):
+            pos[i] = x
+        r = rs[rng.randint(len(rs))]
+        i = r[1].index(max(r[1])); pairs = []
+        while r[2][i] >= 0:
+            j = r[2][i]
+            if j not in dset[i] and en[i] != 4:
+                pairs.append((j, i))
+            i = j
+        j, i = pairs[rng.randint(len(pairs))]
+        u = rng.uniform()
+        new = list(order)
+        if u < 0.45:
+            lo = max(0, pos[j] - (rng.randint(30) if rng.uniform() < 0.4 else 0)); grp = {i}
+            for x in range(pos[i] - 1, lo - 1, -1):
+                if en[order[x]] != 4 and any(k in grp for k in succ[order[x]]):
+                    grp.add(order[x])
+                elif any(k in grp for k in succ[order[x]]):
+                    lo = x + 1
+                    break
+            seg = order[lo:pos[i] + 1]
+            new[lo:pos[i] + 1] = [k for k in seg if k in grp] + [k for k in seg if k not in grp]
+        elif u < 0.9:
+            hi = min(n - 1, pos[i] + (rng.randint(30) if rng.uniform() < 0.4 else 0)); grp = {j}
+            for x in range(pos[j] + 1, hi + 1):
+                if any(k in grp for k in deps[order[x]]):
+                    grp.add(order[x])
+            seg = order[pos[j]:hi + 1]
+            new[pos[j]:hi + 1] = [k for k in seg if k not in grp] + [k for k in seg if k in grp]
+        else:
+            i = rng.randint(n)
+            lo = max([pos[k] for k in deps[i]] + [-1]) + 1; hi = min([pos[k] for k in succ[i]] + [n]) - 1
+            new.pop(pos[i]); new.insert(rng.randint(max(lo, pos[i] - 60), min(hi, pos[i] + 60) + 1), i)
+        if new == order:
+            continue
+        s, r2 = total(new, rs, next(x for x in range(n) if new[x] != order[x]))
+        if s <= cur + cfg["temp2"] * (1.0 - it / cfg["moves"]) * rng.exponential():
+            order, cur, rs = new, s, r2
+            if s < keep[0]:
+                keep = (s, list(order))
+    order = keep[1]
+    end, fin = timed(order, cost, lat)[:2]
+    lastb = {}
+    for i in order:
+        o = ops[i]
+        o["d"] = set(deps[i]); o["t"] = fin[i] - lat - cost[i] - after[i] - xf[i]
+        for b in bk[i]:
+            o["d"] |= {j for e2, j in lastb.get(b, {}).items() if e2 != en[i]}
+            lastb.setdefault(b, {})[en[i]] = i
+    return order, end
+
+
+_PLAN = {}
+
+
+def rank_program(g, core, T, topo):
+    rank = T.rank_of(core)
+    if rank is None:
+        return
+    if not _PLAN:
+        ops_ = plan(CFG)
+        _PLAN["ops"] = ops_; _PLAN["order"] = schedule(ops_, CFG)[0]
+    ops, order = _PLAN["ops"], _PLAN["order"]
+    Q = {"v": g.vector, "s": g.scalar, "p": g.tensor, "g": g, "y": g.sync}
+    N = len(T.cores)
+
+    def X(a):
+        if not isinstance(a, tuple):
+            return a
+        if a[0] == "*":
+            return X(a[1]).indirect(X(a[2]))
+        if a[0] in ("in", "out"):
+            t = T[a[1]]
+            return t[:] if a[3] - a[2] == t.shape[1] else t[:, a[2]:a[3]]
+        return T[a[0]][:, a[1]:a[2]] if a[3] == 1 else T[a[0]][:, a[1]:a[2]:a[3]]
+
+    count = {}; done = {}; seen = {}; ndma = [0]; final = []; sent = [0]
+
+    known = {}; rank_in = {i: x for x, i in enumerate(order)}
+
+    def wait(e, sem, val):
+        mine = seen.setdefault(e, {})
+        if mine.get(sem, 0) < val:
+            mine[sem] = val
+            Q[e].wait_ge(T.sem[sem], val)
+
+    for i in order:
+        o = ops[i]; e = o["e"]; k = o["k"]; a = o["a"]; q = Q[e]
+        mine = seen.setdefault(e, {})
+        for j in sorted(o["d"], key=lambda j: -rank_in[j]):
+            if mine.get(done[j][0], 0) < done[j][1]:
+                wait(e, *done[j])
+                for s, v in known[j].items():
+                    if mine.get(s, 0) < v:
+                        mine[s] = v
+        known[i] = {} if k == "send" else dict(mine)
+        if k == "dma":
+            s = "d%d" % ndma[0]; ndma[0] += 1
+            q.dma_start(X(a[0]), X(a[1])).then_inc(T.sem[s], 16)
+            done[i] = (s, 16); final.append((s, 16))
+            continue
+        if k == "send":
+            m, b, src4, dst4 = a
+            dst = T.cores[(rank + b + m) % N]
+            rid, pid = topo.addr(dst)[:2]
+            en = topo.engines(core, dst)
+            s = "arr%d_%d" % (m, b)
+            g.remote_dma(X(dst4), X(src4), T.sem[s], T.sem.sent, pid, rid, sum(1 << x for x in en[:8]))
+            sent[0] += 8
+            done[i] = (s, 8); final.append((s, 8))
+            continue
+        if k == "ts":
+            if a[3] is None:
+                ins = q.tensor_scalar(X(a[0]), X(a[1]), X(a[2]), None, a[4])
+            else:
+                ins = q.tensor_scalar(X(a[0]), X(a[1]), X(a[2]), X(a[3]), a[4], a[5])
+        elif k == "cp":
+            ins = q.tensor_copy(X(a[0]), X(a[1]))
+        elif k == "tt":
+            ins = q.tensor_tensor(X(a[0]), X(a[1]), X(a[2]), a[3])
+        elif k == "ms":
+            ins = q.memset(X(a[0]), a[1])
+        elif k == "scan":
+            ins = q.tensor_tensor_scan(X(a[0]), X(a[1]), X(a[2]), a[5], a[4], a[3])
+        elif k == "tr":
+            ins = q.transpose(X(a[0]), X(a[1]))
+        elif k == "act":
+            ins = q.activation(X(a[0]), X(a[1]), a[2], bias=X(a[3]), scale=X(a[4]))
+        elif k == "iota":
+            if dty(a[0]) == I32:
+                ins = q.iota(X(a[0]), a[1], a[2], a[3])
+            else:
+                ins = q.iota(X(a[0]), a[1], a[2], a[3], allow_small_or_imprecise_dtypes=True)
+        elif k == "asel":
+            ins = q.affine_select(X(a[0]), X(a[1]), a[2], a[3], 0.0, a[4], a[5])
+        else:
+            for x, (po, l, r) in enumerate(a):
+                ins = q.matmul(X(po), X(l), X(r), x == 0, x == len(a) - 1)
+        count[e] = count.get(e, 0) + 1
+        ins.then_inc(T.sem[SEM[e]], 1)
+        done[i] = (SEM[e], count[e])
+    for e, c in count.items():
+        wait("y", SEM[e], c)
+    wait("y", "sent", sent[0])
+    for s, v in final:
+        wait("y", s, v)

@@ -3,43 +3,46 @@ from concourse.mybir import AluOpType as OP, ActivationFunctionType as AF
 
 F32, BF, F16, I32, U16 = "float32", "bfloat16", "float16", "int32", "uint16"
 STEPS = 4
-Q4 = ((0, 64), (64, 128), (128, 192), (192, 256))
+Q4 = ((192, 256), (128, 192), (64, 128), (0, 64))
+H2 = ((128, 256), (0, 128))
+T3 = ((128, 256), (64, 128), (0, 64))
 CFG = {
-    "selg": 16, "trig": 16, "si": 1000.0, "sl": 2800.0,
-    "raw1": 128,
+    "si": 1000.0, "sl": 2800.0,
     "p1": Q4,
     "adv": (0,),
     "sv": (),
-    "abss": (2, 3),
+    "abss": (3,),
     "p3": Q4,
     "vv": (),
-    "tail": ((0, 128), (128, 192), (192, 256)),
-    "s16": True, "dc": ((0, 128), (128, 256)), "da": ((0, 256),), "selv": 0, "nks": False, "q1late": True,
-    4: {"adv": (0, 1), "abss": ()},
-    "loads": "aav", "seed": 7, "noise": 800.0, "win": 0.0, "iters": 300, "temp": 300.0, "moves": 33000, "temp2": 200.0,
-    "alts": ({"g": 1.2, "sc": 2.5, "f": 1.4, "lat": 120.0, "pe": 0.55},),
-    "lg": ((0, 128), (128, 256)), "ad": ((0, 128), (128, 256)),
-    "g": 1.56, "sc": 3.8, "f": 1.2, "lat": 60.0, "pe": 0.42, "bw": 250.0,
+    "tail": T3,
+    "lg": T3, "ad": H2, "dc": ((0, 256),), "da": ((0, 256),),
+    "nks": True, "q1s": True, "cvt": True, "les": False, "t2s": False, "selg": 8,
+    "s": ("NH",), "tiu": False, "flip": 0.3,
+    1: {"adv": (0, 1, 2, 3)},
+    4: {"adv": (0, 1)},
+    "seed": 7, "iters": 22000, "temp": 120.0, "moves": 4000, "temp2": 60.0,
+    "alts": ({"g": 1.6, "sc": 4.0, "f": 1.3, "lat": 130.0},),
+    "g": 1.7, "sc": 4.2, "f": 1.1, "lat": 100.0, "pe": 0.42, "bw": 250.0, "vo": 55.0, "so": 72.0, "mn": 0, "po": 60.0,
 }
 
 _S = {
-    "VW1": (8192, BF), "VW0": (8192, BF), "ADi": (2048, I32), "AD": (4352, BF), "X16": (2048, F16), "H0": (2048, BF),
-    "LEi": (512, I32), "LE": (768, F32),
+    "VW1": (8192, BF), "VW0": (8192, BF), "ADi": (2048, I32), "AD": (2304, F32), "RUN": (64, U16),
+    "LEi": (512, I32), "LE": (768, F32), "YL": (512, F32),
     "CBi": (16, I32), "KAi": (8, I32), "THi": (8, I32), "COLS": (64, F32), "CI": (16, I32), "CBF": (16, F32), "CBL": (16, U16),
-    "IO": (144, BF), "MI": (256, BF), "MI2": (16, BF), "MSK": (256, BF), "MK1": (256, BF), "CE": (256, F16),
-    "ID32": (128, F32), "MID32": (128, F32), "DM": (128, F32),
-    "Z1": (144, BF), "Z32": (144, BF), "ZM16": (144, BF), "Z16": (144, BF),
-    "EQ": (16, F32), "EQ2": (16, F32), "LT": (16, F32),
-    "SEL": (2048, BF), "SELH": (2048, BF), "TRI": (2048, BF),
-    "T16": (256, BF), "RSD": (256, F32), "MSKC": (256, BF),
-    "RSN": (1024, BF), "RSP": (1024, BF), "RSK": (256, F32),
-    "XI": (256, I32), "A32": (256, I32), "A16": (256, U16), "CW16": (16, U16), "CWS": (256, F32),
-    "S16": (256, U16), "SF": (256, F32), "G16": (2048, F16), "GB": (4096, BF), "N16": (256, U16), "NS": (256, F32),
-    "DD": (4096, BF), "RR": (4096, BF), "NOK": (256, BF), "IND": (256, BF), "RL": (256, BF), "T1": (256, F32),
+    "IO": (144, BF), "MI": (256, BF), "MSK": (256, BF), "MK1": (256, BF), "CE": (256, F16), "HD": (256, BF),
+    "ID32": (128, F32), "MID32": (128, F32), "DM": (128, F32), "IC16": (128, F16), "DF": (144, BF), "IDW": (144, BF),
+    "Z1": (144, BF), "Z2": (144, BF), "ZM1": (144, BF), "EQ": (16, F32),
+    "SEL": (2048, BF), "BC": (128, F16), "MBC": (128, F16), "MI16": (128, BF), "SH": (256, F16), "NH": (256, F16),
+    "T16": (256, BF), "T16M": (256, BF), "T16K": (256, F16), "RSD": (256, F32), "MSKC": (256, BF),
+    "RSN": (1024, BF), "RSP": (1024, BF), "RSK": (256, BF), "OFS": (1024, BF), "OFI": (256, BF), "OF2": (256, BF),
+    "XI": (256, I32), "A32": (256, I32), "A16": (256, U16), "CW16": (16, U16), "HC": (256, F16),
+    "S16": (256, U16), "SF": (256, F32), "G16": (4096, F16), "N16": (256, U16), "NS": (256, F32),
+    "DD": (4096, BF), "RR": (4096, BF), "NOK": (256, BF), "IND": (256, BF), "RL": (256, BF),
     "T2": (256, F32), "P16": (256, U16), "M0": (256, F32), "M1": (256, F32), "VV": (4096, BF), "HI": (4096, BF), "LO": (4096, BF),
-    "KTT": (256, F32), "KSC": (256, F32), "MX": (256, F32), "IND2": (256, BF), "OHS": (256, BF), "OHA": (256, F16),
-    "COL": (256, F16), "COW16": (16, U16), "COWS": (256, F32), "COW2": (256, F32), "Q1": (256, BF), "Q2": (256, BF),
-    "QC": (4096, BF), "QA": (4096, BF), "DSC": (256, F32), "DSA": (256, F32),
+    "HI2": (2048, F16), "LO2": (2048, F16),
+    "KTT": (256, F32), "KSC": (256, F32), "MX": (256, F32), "IND2": (256, BF), "OHS": (256, F32), "OHA": (256, F16),
+    "Q0": (256, F32), "Q1": (256, F32), "Q2": (256, F32), "AO": (256, BF),
+    "HA": (256, F16), "QC": (512, BF), "QA": (512, BF), "DSC": (256, F32), "DSA": (256, F32),
     "LOFF": (16, U16), "AOFF": (16, U16), "ZR": (256, F32), "QB": (256, BF), "FL": (256, F16), "WS": (256, F32),
     "WW16": (16, U16), "TI": (256, I32), "C32": (256, I32),
 }
@@ -48,8 +51,7 @@ for _m in range(1, STEPS):
     _S["PO%d" % _m] = (512, BF)
     _S["PN%d" % (_m + 1)] = (512, BF)
 _AL = {n: 128 * i for i, n in enumerate(
-    "ID BO WT W16 W16O ONES KT SU OHM OH2P OH2M IE IOD RA0 RA1 RB0 RB1 I16 MI1 MBO MIH IQ IM512 IM4096 ICH ICL KH KL DK "
-    "BM128 BM8192 B8192 BM384 B32 BP DF GI TMP TMP2 I4096 I8192 IM8192".split())}
+    "BO WT W16 ONES SU OHM OH OH8 MOH8 I16 MI1 MBO MIH IQ IM32 IM4096 KH KL BM128 BM8192 B32 GI TMP I4096 I8192 IM8192".split())}
 _S["CM"] = (128 * len(_AL), BF)
 SCRATCH = {k: ("sbuf", [128, w], d) for k, (w, d) in _S.items()}
 for _b in range(8):
@@ -58,14 +60,20 @@ SEMAPHORES = ["cv", "cs", "cp", "cg", "sent"] + ["d%d" % i for i in range(48)] +
              ["arr%d_%d" % (m, b) for m in range(1, STEPS) for b in range(4)]
 SEM = {"v": "cv", "s": "cs", "p": "cp", "g": "cg"}
 TWO = (BF, F16, U16)
-(cP, cK, cG, cG15, cW, cKL, cKH, cCP, cTHR, c16K, cK1, cE15, cTH, c15K, cPAR, cEV, cP2048, cE2048, cQ2, cK2, cPD,
- cW16, cT, cK8, cNK) = range(25)
+(cK, cG, cG15, cW, cKL, cKH, cCP, cTHR, c16K, cK1, cE15, cPAR, cEV, cP2048, cE2048, cQ2, cP2, cPD,
+ cW16, cT, cNK, cKM, cMPAR, cMEV, cP32) = range(25)
 
 
 def A(n, lo=0, hi=None, st=1):
+    if n == "ID":
+        return ("IDW", 1 + lo, 1 + (128 if hi is None else hi), st)
     if n in _AL:
         return ("CM", _AL[n] + lo, _AL[n] + (128 if hi is None else hi), st)
     return (n, lo, _S[n][0] if hi is None else hi, st)
+
+
+def cols(a):
+    return slice(a[1], a[2], a[3]) if a[3] > 0 else slice(a[2] - 1, a[1] - 1 if a[1] else None, a[3])
 
 
 def col(i):
@@ -79,7 +87,7 @@ def IND(win, off):
 def width(a):
     if a[0] == "*":
         return 16 * (a[2][2] - a[2][1])
-    return len(range(a[1], a[2], a[3]))
+    return len(range(a[1], a[2], abs(a[3])))
 
 
 def psum(a):
@@ -90,8 +98,8 @@ def dty(a):
     return F32 if psum(a) else _S[a[0]][1]
 
 
-SLOT = {"X": (2, 1), "q2": (2, 2), "cw": (2, 3), "colw": (2, 3), "col2": (6, 2), "val": (4, 0), "rr": (4, 0), "U16": (4, 0), "Y23": (4, 1), "ww": (4, 1), "Y1": (4, 2),
-        "oh2": (4, 2), "xA": (4, 3), "Xz": (4, 3), "dn": (6, 0), "D": (6, 1), "colr": (6, 1), "oh": (6, 2), "U": (6, 3), "uc": (6, 3)}
+SLOT = {"X": (2, 1), "q2": (2, 2), "cw": (2, 3), "colw": (2, 3), "val": (4, 0), "rr": (4, 0), "U16": (4, 0), "Y23": (4, 1), "ww": (4, 1),
+        "oh2": (4, 2), "m1": (4, 2), "xA": (4, 3), "Xz": (4, 3), "dn": (6, 0), "D": (6, 1), "oh": (6, 2), "U": (6, 3), "uc": (6, 3)}
 
 
 def ps(role, a, b, st=1):
@@ -106,8 +114,8 @@ def ps(role, a, b, st=1):
     if role == "dedC":
         return ("P1", 256 + a, 256 + b, st)
     if role == "rel":
-        return ("P%d" % (4 + (a // 512) % 3), 0, b - a, st)
-    if role == "crep":
+        return ("P%d" % (4 + (a // 512) % 2), 0, b - a, st)
+    if role == "con":
         return ("P7", a, b, st)
     o = SLOT[role][1] * 128 + a % 128
     return ("P%d" % (SLOT[role][0] + h), o, o + b - a, st)
@@ -117,6 +125,7 @@ def plan(cfg):
     ops = []
     cyc = 0.83 * cfg["f"]
     nks = cfg["nks"]; cfg0 = cfg
+    les = 32.0 if cfg["les"] else 0.0
 
     def add(eng, kind, args, rd, wr, cost, lat=0.0, xfer=0.0):
         R, W = [], []
@@ -137,9 +146,9 @@ def plan(cfg):
         if ins[0][0] == "*":
             return 50 + n * cfg["g"] * 0.83
         if tt:
-            return max(64, n * (1 if any(psum(x) for x in ins) else 2)) * cyc
+            return cfg["vo"] + max(cfg["mn"], n * (1 if any(psum(x) for x in ins) else 2)) * cyc
         two = all(dty(x) in TWO for x in [out] + ins)
-        return max(64, n * (0.5 if two else 1)) * cyc
+        return cfg["vo"] + max(cfg["mn"], n * (0.5 if two else 1)) * cyc
 
     def ts(out, i, s1, op0, s2=None, op1=None):
         add("v", "ts", (out, i, s1, s2, op0, op1), [i, s1, s2], [out], vcost(out, [i]))
@@ -159,13 +168,25 @@ def plan(cfg):
     def tr(out, i):
         add("v", "tr", (out, i), [i], [out], vcost(out, [i]))
 
-    def act(out, i, f=AF.Identity, bias=0.0, scale=1.0):
+    def act(out, i, f=AF.Identity, bias=0.0, scale=1.0, other=None, vec=False):
         n = width(out)
-        c = 65 + n * cfg["g"] * 0.83 if i[0] == "*" else max(64, n) * cyc
+        c = 65 + n * cfg["g"] * 0.83 if i[0] == "*" else 65 + n * cfg["sc"] * 0.83 if out[0] == "*" else cfg["so"] + max(cfg["mn"], n) * cyc
         add("s", "act", (out, i, f, bias, scale), [i, bias, scale], [out], c)
+        if f == AF.Identity:
+            other = (scale, OP.mult, bias, OP.add) if scale != 1.0 else (bias, OP.add, None, None)
+        elif f == AF.Relu and scale == 1.0:
+            other = (bias, OP.add, 0.0, OP.max)
+        if other:
+            o = ops[-1]
+            o["m"] = [("s", "act", o["a"], c), ("v", "ts", (out, i, other[0], other[2], other[1], other[3]), vcost(out, [i]))]
+            if f == AF.Identity and scale == 1.0 and bias == 0.0 and i[0] != "*" and not psum(i) and dty(out) == U16:
+                o["m"].append(("g", "asel", (out, i, [[0, n]], OP.is_ge, 0, 0), 170 + 2 * n * cyc))
+            if vec:
+                o["m"][:2] = o["m"][1::-1]
+                o["e"], o["k"], o["a"], o["c"] = o["m"][0]
 
     def mm(items):
-        c = sum(max(64, width(o)) * (4 if dty(r) == F32 else 1) for o, l, r in items) * cfg["pe"] * cfg["f"] + 60
+        c = sum(max(64, width(o)) * (4 if dty(r) == F32 else 1) for o, l, r in items) * cfg["pe"] * cfg["f"] + cfg["po"]
         add("p", "mm", items, [x for o, l, r in items for x in (l, r)], [o for o, l, r in items], c)
 
     def dma(out, i, nbytes, rd, wr):
@@ -176,6 +197,9 @@ def plan(cfg):
 
     def asel(out, i, pat, op, base, cm):
         add("g", "asel", (out, i, pat, op, base, cm), [i], [out], 170 + 2 * width(out) * cyc)
+
+    def lin(out, i, plus, mul=1.0):
+        act(out, i, bias=plus, scale=mul, vec=out[0].rstrip("01") not in cfg["s"])
 
     def load(name, src, lo=0, hi=None):
         at = 4096 if name == "VW1" else 0
@@ -189,87 +213,79 @@ def plan(cfg):
         return A(n, 15 - k, 143 - k)
 
     load("ZN1", "z0"); load("KAi", "ka", 0, 1); load("CBi", "cb"); load("THi", "th", 0, 1)
-    big = {"a": [("ADi", "ad", 0, 1024), ("ADi", "ad", 1024, 2048)],
-           "v": [("LEi", "le", 0, 512), ("VW1", "vf", 0, 2048), ("VW1", "vf", 2048, 4096)]}
-    for x in (big["a"] + big["v"] if cfg["loads"] == "aav" else big["v"] + big["a"]):
+    for x in (("ADi", "ad", 0, 1024), ("ADi", "ad", 1024, 2048), ("LEi", "le", 0, 512), ("VW1", "vf", 0, 2048), ("VW1", "vf", 2048, 4096)):
         load(*x)
     iota(A("CI", 0, 1), [[0, 1]], 0, 1)
-    iota(A("DF"), [[1, 128]], 0, -1); iota(A("GI"), [[16, 8], [0, 16]], 0, 0); iota(A("MI"), [[0, 16], [1, 16]], 0, 0)
-    iota(A("IO"), [[1, 144]], 0, 0); iota(A("MI2"), [[2, 8], [0, 2]], 0, 0); iota(A("T16"), [[16, 256]], 0, 0)
+    iota(A("GI"), [[16, 8], [0, 16]], 0, 0); iota(A("DF"), [[1, 144]], -1, -1); iota(A("MI"), [[0, 16], [1, 16]], 0, 0)
+    iota(A("IO"), [[1, 144]], 0, 0); iota(A("T16"), [[16, 256]], 0, 0)
+    iota(A("RSN"), [[0, 64], [256, 16]], 0, 0); iota(A("RSP"), [[0, 64], [-256, 16]], 256, 0)
+    iota(A("OFS"), [[0, 4], [256, 16], [0, 16]], -2048, 0); iota(A("OFI"), [[0, 16], [32, 16]], -256, 0)
     ci = lambda i: A("CI", i, i + 1)
+    ID = A("ID")
+    nsum = [0]
 
     def aff(c, src, mul, plus):
         act(col(c), col(src), bias=plus, scale=mul)
 
+    def msum(out, x, y):
+        p = ps("con", 128 * (nsum[0] % 3), 128 * (nsum[0] % 3) + 128); nsum[0] += 1
+        mm([(p, ID, x), (p, ID, y)]); act(out, p)
+
     ts(ci(1), ci(0), 15, OP.bitwise_and); cp(col(cK), ci(1)); tt(col(cG), ci(0), ci(1), OP.subtract)
     ts(ci(4), ci(0), 1, OP.bitwise_and); cp(col(cPAR), ci(4))
-    aff(cG15, cG, 1.0, 15.0); aff(cW, cK, 14.0, 1.0); aff(c16K, cK, -1.0, 16.0); aff(cK1, cK, 1.0, 1.0)
-    aff(c15K, cK, -1.0, 15.0); aff(cEV, cPAR, -1.0, 1.0); aff(cP2048, cPAR, 2048.0, 0.0); aff(cE2048, cPAR, -2048.0, 2048.0)
-    aff(cQ2, cPAR, 24576.0, -8192.0); aff(cPD, cPAR, 4096.0, -2048.0)
-    act(col(cK2), col(cPAR), bias=col(cK), scale=-1.0); act(col(cE15), col(cK), AF.Relu, bias=-14.0)
-    aff(cT, cE15, 1.0, -1.0)
+    aff(cG15, cG, 1.0, 15.0); aff(cW, cK, 14.0, 1.0); aff(c16K, cK, -1.0, 16.0); aff(cK1, cK, 1.0, 9.0 if nks else 1.0)
+    aff(cEV, cPAR, -1.0, 1.0); aff(cP32, cPAR, 1.0 / 32, 0.0)
+    act(col(cE15), col(cK), AF.Relu, bias=-14.0)
+    aff(cT, cE15, 1.0, -1.0); aff(cNK, cK, -1.0, -1.0); aff(cKM, cK, 1.0, -2048.0)
     ts(ci(2), A("KAi", 0, 1), 1184.0, OP.add); ts(ci(3), ci(2), 31, OP.bitwise_and); cp(col(cKL), ci(3))
     tt(col(cKH), ci(2), ci(3), OP.subtract); aff(cCP, cKL, 2048.0, 40960.0)
-    ts(col(cTH), A("THi", 0, 1), 16.0, OP.mult, -65536.0, OP.add); act(col(cTHR), col(cTH), bias=col(c15K))
-    ts(ci(5), ci(1), 14.0, OP.mult, 9.0, OP.add); ts(ci(6), ci(5), 15, OP.bitwise_and); ts(col(cW16), ci(6), -8.0, OP.add)
-    ms(A("ONES"), 1.0); ms(A("AN1"), 128.0)
     if nks:
-        aff(cTHR, cTHR, -1.0, -0.5); aff(cK1, cK, 1.0, 9.0); aff(cK8, cK, 1.0, 8.0)
-    for n, v in (("ID", 1.0), ("I16", 8.0 if nks else 16.0), ("I4096", 4096.0), ("I8192", 8192.0), ("IM8192", -8192.0),
-                 ("MI1", -1.0), ("MIH", -0.5), ("IQ", 0.25), ("IM512", -512.0), ("IM4096", -4096.0),
-                 ("ICH", 19456.0), ("ICL", 160.0), ("KH", col(cKH)), ("KL", col(cKL)), ("DK", col(cK8 if nks else cK)), ("IE", col(cEV)),
-                 ("IOD", col(cPAR))):
-        ts(A(n), A("DF"), 0.0, OP.is_equal, v, OP.mult)
-    for n, v in (("BO", 1.0), ("WT", col(cW)), ("W16", col(cW16)), ("MBO", -1.0), ("BM128", -128.0), ("BM8192", -8192.0),
-                 ("B8192", 8192.0), ("BM384", -384.0), ("B32", 1.0 / (64 if nks else 32)), ("BP", col(cPD)), ("TMP", col(cE15))):
-        ts(A(n), A("GI"), col(cG), OP.is_equal, v, OP.mult)
-    act(A("ID32"), A("ID")); act(A("MID32"), A("ID"), scale=-1.0)
-    act(A("KT"), A("ONES"), scale=col(c15K))
-    tt(A("DM"), A("TMP"), A("ID"), OP.subtract)
-    for h in range(2):
-        sel = col(cPAR if h else cEV)
-        ts(A("RB%d" % h), A("DF"), 1.0 - h, OP.is_equal, sel, OP.mult)
-        ts(A("TMP2"), A("DF"), 0.0 - h, OP.is_equal, sel, OP.mult)
-        tt(A("RA%d" % h), A("TMP2"), A("RB%d" % h), OP.subtract)
-    ts(A("OHM"), A("DF"), 1.0, OP.is_equal, col(cT), OP.mult)
+        ts(col(cTHR), A("THi", 0, 1), -1.0, OP.mult, 4095.5, OP.add)
+    else:
+        ts(col(cTHR), A("THi", 0, 1), -4096.0, OP.add)
+    ts(ci(5), ci(1), 14.0, OP.mult, 9.0, OP.add); ts(ci(6), ci(5), 15, OP.bitwise_and); ts(col(cW16), ci(6), -8.0, OP.add)
+    ms(A("AN1"), 128.0)
+    ts(A("IDW"), A("DF"), 0.0, OP.is_equal); ts(A("BO"), A("GI"), col(cG), OP.is_equal)
+    ts(A("IC16"), ID, 19616.0, OP.mult); ts(A("Z1"), A("IO"), col(cG15), OP.is_equal)
+    act(A("ONES"), ID, bias=1.0, scale=0.0)
+    for n, v in (("I16", 8.0 if nks else 16.0), ("I4096", 4096.0), ("I8192", 8192.0), ("IM8192", -8192.0),
+                 ("MI1", -1.0), ("MIH", -0.5), ("IQ", 0.25), ("IM32", -32.0), ("IM4096", -4096.0),
+                 ("KH", col(cKH)), ("KL", col(cKL)), ("ID32", 1.0), ("MID32", -1.0)):
+        act(A(n), ID, scale=v)
+    for n, v in (("WT", col(cW)), ("W16", col(cW16)), ("MBO", -1.0), ("BM128", -128.0), ("BM8192", -8192.0),
+                 ("B32", 1.0 / (64 if nks else 32)), ("TMP", col(cE15))):
+        act(A(n), A("BO"), scale=v)
+    act(A("BC"), A("BO"), scale=-255.5); act(A("MBC"), A("BO"), scale=255.5); act(A("MI16"), ID, scale=-8.0)
+    act(A("Z2"), A("Z1"), scale=2.0); act(A("ZM1"), A("Z1"), scale=-1.0)
+    msum(A("DM"), A("TMP"), A("MI1"))
+    act(A("OHM"), A("IDW", 0, 128), scale=col(cT)); msum(A("OH"), ID, A("OHM"))
+    act(A("OH8"), A("OH"), scale=8192.0); act(A("MOH8"), A("OH"), scale=-8192.0)
     asel(A("SU"), A("BO"), [[-1, 128]], OP.is_ge, 0, 1)
-    asel(A("W16O"), A("W16"), [[0, 64], [1, 2]], OP.is_equal, -1, 0)
-    asel(A("OH2P"), A("B8192"), [[2, 64], [0, 2]], OP.is_equal, 1, -1)
-    asel(A("OH2M"), A("BM8192"), [[2, 64], [0, 2]], OP.is_equal, -1, -1)
     ts(A("MSK"), A("MI"), col(cK), OP.not_equal, -4194304.0, OP.mult)
     ts(A("MK1"), A("MI"), col(cK), OP.is_equal)
-    for n, v in (("Z1", 1.0), ("Z32", 32.0), ("ZM16", -16.0), ("Z16", 16.0)):
-        ts(A(n), A("IO"), col(cG15), OP.is_equal, v, OP.mult)
-    ts(A("LT"), A("MI", 0, 16), col(cK), OP.is_gt); ts(A("EQ2"), A("MI2"), col(cK2), OP.is_equal)
     ts(A("EQ"), A("MI", 0, 16), col(cK), OP.is_equal)
+    ts(A("T16K"), A("T16"), col(cKM), OP.add)
     for k in range(16):
-        if cfg["raw1"] and k < cfg["selg"]:
-            asel(blk("SEL", k), A("ID"), [[0, 8], [1, 16]], OP.is_equal, -k, 0)
-        elif cfg["raw1"]:
-            ts(blk("SEL", k), A("ID"), A("EQ", k, k + 1), OP.mult)
-        if k < cfg["selv"]:
-            ts(blk("SELH", k), zw("Z1", k), A("EQ2", k, k + 1), OP.mult)
+        if k < cfg["selg"]:
+            asel(blk("SEL", k), ID, [[0, 8], [1, 16]], OP.is_equal, -k, 0)
         else:
-            act(blk("SELH", k), zw("Z1", k), scale=A("EQ2", k, k + 1))
-        if k < cfg["trig"]:
-            asel(blk("TRI", k), A("BM8192"), [[16, 8], [0, 16]], OP.is_ge, k - 1, -1)
-        else:
-            act(blk("TRI", k), A("BM8192"), scale=A("LT", k, k + 1))
-    aff(cNK, cK, -1.0, -1.0); act(A("MSKC"), A("MSK"), bias=256.0)
+            act(blk("SEL", k), ID, scale=A("EQ", k, k + 1))
+    p = ps("con", 0, 256)
+    mm([(p, ID, A("T16")), (p, ID, A("MSK"))]); act(A("T16M"), p)
+    act(A("MSKC"), A("MSK"), bias=256.0); act(A("HD"), A("MSK"), bias=-2097152.0, scale=-1.0)
     act(A("RSD"), A("MSK"), bias=1.0e9, scale=0.0); act(A("RSD", 0, 256, 16), A("IO", 0, 16), bias=col(cNK), scale=-16.0)
-    ms(A("RSN"), 0.0); ms(A("RSN", 0, 1024, 16), -512.0); act(A("RSP"), A("RSN"), scale=-1.0)
-    ms(A("RSK"), 0.0); ms(A("RSK", 0, 256, 16), -3.0e7)
-    cp(A("LE", 256, 768), A("LEi"))
-    if cfg["q1late"]:
-        act(A("AD", 0, 256), A("MSK"), scale=0.0)
-    for a in range(0, 2048, 512):
-        x, hh = A("X16", a, a + 512), A("H0", a, a + 512)
-        ts(x, A("ADi", a, a + 512), -2048.0, OP.add); ts(hh, x, 201326592.0, OP.add, -201326592.0, OP.add)
-        for h in range(2):
-            y = ps("rel", 2 * a + 512 * h, 2 * a + 512 * h + 512)
-            mm([(y, A("RA%d" % h), hh), (y, A("RB%d" % h), x)])
-            act(A("AD", 256 + 2048 * h + a, 256 + 2048 * h + a + 512), y, bias=col(cE2048))
-    HALF = ((0, 128), (128, 256))
+    act(A("RSK"), A("MSK"), scale=0.0); act(A("RSK", 0, 256, 16), A("IO", 0, 16), bias=-3.0e7, scale=0.0)
+    act(A("OF2"), A("OFI"), bias=col(cP32), scale=col(cEV))
+    act(A("AD", 0, 256), A("MSK"), scale=0.0)
+    if cfg["cvt"]:
+        act(A("LE", 256, 768), A("LEi"), bias=les)
+        for a in (0, 1024):
+            act(A("AD", 256 + a, 1280 + a), A("ADi", a, a + 1024))
+    else:
+        ts(A("RUN"), A("T16", 0, 64), col(cK), OP.add)
+        act(A("LE", 256, 768), IND(A("LEi"), A("RUN", 0, 32)), bias=les)
+        for a in (0, 1024):
+            act(A("AD", 256 + a, 1280 + a), IND(A("ADi", a, a + 1024), A("RUN")))
 
     def segs(m, side, part, a, b):
         if side == "N" and m == 1:
@@ -283,26 +299,32 @@ def plan(cfg):
 
     ts(A("CBF"), A("CBi"), -256.0, OP.add); cp(A("CBL"), A("IO", 0, 16))
     tt(A("CE"), IND(A("CBF"), A("CBL")), A("MK1"), OP.mult)
-    mm([(ps("crep", 0, 256), A("BO"), A("CE"))])
-    cp(A("CN1"), ps("crep", 0, 256))
+    mm([(ps("dedC", 0, 256), A("BO"), A("CE"))])
+    cp(A("CN1"), ps("dedC", 0, 256))
 
     def wrap(out, p, a, b):
         scan(A(out, a, b), A("RSK", 0, b - a), p, OP.max)
 
-    def dedupe(rep, wf, own, q, ds, r1, msk, off, a, b):
-        ja, jb = a // 16, b // 16
-        it = [(ps(r1, a, b), A("ID"), A(msk, a, b))] + [(ps(r1, a, b), l, r) for l, r in own]
-        for j in range(ja if q == "QC" else 0, jb):
-            lo = max(a, 16 * j)
-            ts(A(q, 240 * j + lo, 240 * j + b), A(rep, lo, b), wf(j), OP.is_equal)
-            lo = max(a, 16 * j + 16)
-            if lo < b:
-                it.append((ps(r1, lo, b), A("BM8192"), A(q, 240 * j + lo, 240 * j + b)))
-        mm(it + [(ps(r1, a + k, b, 16), blk("TRI", k), A(q, 256 * ja + k, 256 * jb, 256)) for k in range(16)])
-        scan(A(ds, a, b), A("RSD", a, b), ps(r1, a, b), OP.max, OP.min, 1.0e6)
-        ts(A(off, ja, jb), A(ds, a + 15, b, 16), 256.0, OP.add)
+    def hold(out, p, a, b):
+        scan(A(out, a, b), A("HD", 0, b - a), p, OP.max, OP.min, -30000.0)
 
-    ADW, LEW = A("AD", 256, 4352), A("LE", 256, 768)
+    def places(it, ds, r1, off, a, b):
+        mm(it)
+        scan(A(ds, a, b), A("RSD", a, b), ps(r1, a, b), OP.max, OP.min, 1.0e6)
+        lin(A(off, a // 16, b // 16), A(ds, a + 15, b, 16), 256.0)
+
+    def first_of_32(l, r, made, held, q, msk, ds, r1, off, a, b):
+        p = ps(r1, a, b)
+        if not made:
+            mm([(p, l, A(r, a, b))])
+        it = [(p, ID, A(msk, a, b)), (p, l, A(r, a, b))]
+        for x, d in enumerate((1, 17)):
+            eq = A(q, 256 * x + a + d, 256 * x + b)
+            tt(eq, A(held, a, b - d), ps(r1, a + d, b), OP.is_equal)
+            it.append((ps(r1, a + d, b), A("BM8192"), eq))
+        places(it, ds, r1, off, a, b)
+
+    ADW, LEW = A("AD", 256, 2304), A("LE", 256, 768)
     for m in range(1, STEPS + 1):
         last = m == STEPS
         cfg = dict(cfg0); cfg.update(cfg0.get(m, {}))
@@ -318,83 +340,97 @@ def plan(cfg):
                 mm([(ps("U", x0, x1), A("WT"), z)])
             act(A("QB", a, b), ps("U", a, b), bias=135.5 + 2.0 ** -13, scale=2.0 ** -12)
             mm([(ps("uc", a, b), A("IM4096"), A("QB", a, b))] + [(ps("uc", x0, x1), A("WT"), z) for x0, x1, z in zs])
-            ts(A(U, a, b), ps("uc", a, b), 4096.0 * 136 - 2048, OP.add)
+            lin(A(U, a, b), ps("uc", a, b), 4096.0 * 136 - 2048)
             if m > 1:
-                ts(A("TI", a, b), ps("uc", a, b), 4096.0 * 136, OP.add, 1103.0, OP.mult)
+                if cfg["tiu"]:
+                    lin(A("TI", a, b), A(U, a, b), 1103.0 * 2048, 1103.0)
+                else:
+                    ts(A("TI", a, b), ps("uc", a, b), 4096.0 * 136, OP.add, 1103.0, OP.mult)
                 ts(A("C32", a, b), A("TI", a, b), 4, OP.arith_shift_right, 511, OP.bitwise_and)
-                ts(A(C, a, b), A("C32", a, b), -256.0, OP.add)
+                lin(A(C, a, b), A("C32", a, b), -256.0)
             x = ps("X", a, b)
-            mm([(x, A("KH"), A(U, a, b)), (x, A("KL"), A(U, a, b)), (x, A("ICH"), A(C, a, b)), (x, A("ICL"), A(C, a, b))])
-            ts(A("XI", a, b), x, col(cCP), OP.add)
+            mm([(x, A("KH"), A(U, a, b)), (x, A("KL"), A(U, a, b)), (x, A("IC16"), A(C, a, b))])
+            lin(A("XI", a, b), x, col(cCP))
             ts(A("A32", a, b), A("XI", a, b), 5, OP.arith_shift_right, 2047, OP.bitwise_and)
-            r = min(b, max(a, cfg["raw1"])) if m == 1 else a
-            if r > a:
-                cp(A("A16", a, r), A("A32", a, r))
-            if r < b:
-                ts(A("A16", r, b), A("A32", r, b), col(cP2048), OP.add)
+            lin(A("A16", a, b), A("A32", a, b), 0.0)
             ja, jb = a // 16, b // 16
+            mm([(ps("cw", a, b), ID, A("MSK", a, b)), (ps("cw", a, b), ID, A(C, a, b))])
+            hold("HC", ps("cw", a, b), a, b)
             if m == 1:
                 cp(A("CW16", ja, jb), A("CBi", ja, jb))
             else:
-                mm([(ps("cw", a, b), A("ID"), A("MSK", a, b)), (ps("cw", a, b), A("ID"), A(C, a, b))])
-                wrap("CWS", ps("cw", a, b), a, b)
-                ts(A("CW16", ja, jb), A("CWS", a + 15, b, 16), 256.0, OP.add)
-            act(A("SF", a, b), IND(LEW, A("CW16", ja, jb)))
-            cp(A("S16", a, b), A("SF", a, b) if cfg["s16"] else IND(LEW, A("CW16", ja, jb)))
+                lin(A("CW16", ja, jb), A("HC", a + 15, b, 16), 256.0)
+            if nks:
+                act(A("SH", a, b), IND(LEW, A("CW16", ja, jb)), bias=-2048.0 - les)
+                lin(A("S16", a, b), A("SH", a, b), 2048.0)
+            else:
+                act(A("SF", a, b), IND(LEW, A("CW16", ja, jb)))
+                lin(A("S16", a, b), A("SF", a, b), 0.0)
         for q, (a, b) in enumerate(cfg["p1"]):
             lo, hi = 16 * a, 16 * b
-            if m == 1 and a < cfg["raw1"]:
-                ts(A("G16", lo, hi), IND(A("ADi"), A("A16", a, b)), -2048.0, OP.add); gb, sel, off = "G16", "SEL", 2048.0
+            src = IND(A("ADi") if m == 1 else ADW, A("A16", a, b))
+            act(A("G16", lo, hi), src, bias=-2048.0, vec=q in cfg["adv"])
+            mm([(ps("n", a, b), blk("SEL", k), A("G16", lo + k, hi, 16)) for k in range(16)])
+            lin(A("N16", a, b), ps("n", a, b), 2048.0)
+            if nks:
+                lin(A("NH", a, b), ps("n", a, b), 0.0)
             else:
-                (cp if q in cfg["adv"] else act)(A("GB", lo, hi), IND(ADW, A("A16", a, b)))
-                gb, sel, off = "GB", "SELH", 0.0
-            mm([(ps("n", a, b), blk(sel, k), A(gb, lo + k, hi, 16)) for k in range(16)])
-            ts(A("N16", a, b), ps("n", a, b), off, OP.add)
-            act(A("NS", a, b), ps("n", a, b), bias=off)
-            sv = A(VW, (lo + 2048) % 4096, (lo + 2048) % 4096 + hi - lo)
-            (cp if q in cfg["sv"] else act)(sv, IND(VF, A("S16", a, b)))
+                act(A("NS", a, b), ps("n", a, b), bias=2048.0)
+            sv = A(VW, lo, hi)
+            act(sv, IND(VF, A("S16", a, b)))
             tt(A("DD", lo, hi), IND(VF, A("N16", a, b)), sv, OP.subtract)
             key = ps("key", a, b)
-            it = [(key, A("ID"), A("KT", 0, b - a)), (key, A("IM512"), segs(m, "N", 1, a, b)[0][2])]
+            it = [(key, A("IM32"), segs(m, "N", 1, a, b)[0][2])]
             if q in cfg["abss"]:
                 act(A("RR", lo, hi), A("DD", lo, hi), AF.Abs)
-                it += [(key, zw("Z16", k), A("RR", lo + k, hi, 16)) for k in range(16)]
+                it += [(key, zw("Z1", k), A("RR", lo + k, hi, 16)) for k in range(16)]
             else:
                 ts(A("RR", lo, hi), A("DD", lo, hi), 0.0, OP.max)
-                it += [(key, zw("ZM16", k), A("DD", lo + k, hi, 16)) for k in range(16)]
-                it += [(key, zw("Z32", k), A("RR", lo + k, hi, 16)) for k in range(16)]
+                it += [(key, zw("ZM1", k), A("DD", lo + k, hi, 16)) for k in range(16)]
+                it += [(key, zw("Z2", k), A("RR", lo + k, hi, 16)) for k in range(16)]
             mm(it)
-        cw = (lambda j: A("CBF", j, j + 1)) if m == 1 else (lambda j: A("CWS", 16 * j + 15, 16 * j + 16))
         for a, b in cfg["dc"]:
-            dedupe(C, cw, [(A("ID"), A(C, a, b))], "QC", "DSC", "dedC", "MSKC", "LOFF", a, b)
+            first_of_32(ID, C, m == 1, "HC", "QC", "MSKC", "DSC", "dedC", "LOFF", a, b)
         for a, b in cfg["lg"]:
-            ja, jb = a // 16, b // 16
             nok, one = A("NOK", a, b), A("ONES", 0, b - a)
             if nks:
                 act(nok, ps("key", a, b), AF.Sign, bias=col(cTHR))
             else:
                 ts(nok, ps("key", a, b), col(cTHR), OP.is_gt)
             mm([(ps("val", a, b), A("SU"), nok)])
-            act(A("IND", a, b), ps("val", a, b), AF.Sign, bias=col(c16K), scale=-1.0)
+            act(A("IND", a, b), ps("val", a, b), AF.Sign, bias=col(c16K), scale=-1.0, other=(col(c16K), OP.is_lt, None, None))
             an = segs(m, "N", 1, a, b)
-            ao = [(a, b, A("Q2", a, b))] if last else segs(m, "O", 1, a, b)
-            mm([(ps("xA", a, b), A("B32"), nok)] + [(ps("xA", x0, x1), A("ID"), x) for x0, x1, x in an])
+            ao = [(a, b, A("AO", a, b))] if last else segs(m, "O", 1, a, b)
+            mm([(ps("xA", a, b), A("B32"), nok)] + [(ps("xA", x0, x1), ID, x) for x0, x1, x in an])
             for x0, x1, x in ao:
                 act(x, ps("xA", x0, x1), bias=0.421875 if nks else 0.171875)
             mm([(ps("rr", a, b), A("I16"), nok), (ps("rr", a, b), A("MBO"), A("IND", a, b))])
             act(A("RL", a, b), ps("rr", a, b), AF.Relu, bias=col(cK1))
             y = ps("Y23", a, b)
-            h = a // 128
-            mm([(y, A("ID"), A("T16", a, b)), (y, A("DK"), one), (y, A("BM384" if h else "BM128"), one), (y, A("I16"), nok)] +
-               [(ps("Y23", x0, x1), A("IM8192"), x) for x0, x1, x in an] + [(ps("Y23", x0, x1), A("I8192"), x) for x0, x1, x in ao] +
-               [(y, A("MI1"), A("RL", a, b))])
-            tt(A("T2", a, b), y, A("NS", a, b), OP.min)
-            ts(A("P16", a, b), A("T2", a, b), 2048.0 * (h + 1), OP.add)
-            if nks:
-                mm([(ps("dn", a, b), A("ID32"), A("SF", a, b)), (ps("dn", a, b), A("IM4096"), nok)])
-                act(A("M0", a, b), ps("dn", a, b), AF.Relu, bias=-4096.0)
-                mm([(ps("uc", a, b), A("ID32"), A("NS", a, b)), (ps("uc", a, b), A("I4096"), nok)])
-                act(A("M1", a, b), ps("uc", a, b), AF.Relu, bias=-4096.0)
+            nh, sh = A("NH", a, b), A("SH", a, b)
+            if cfg["t2s"]:
+                mm([(y, A("MI1"), A("T16K", a, b)), (y, A("MI16"), nok), (y, A("MBC"), one), (y, ID, nh)] +
+                   [(ps("Y23", x0, x1), A("I8192"), x) for x0, x1, x in an] + [(ps("Y23", x0, x1), A("IM8192"), x) for x0, x1, x in ao] +
+                   [(y, ID, A("RL", a, b))])
+                act(A("T2", a, b), y, AF.Relu)
+                mm([(y, ID, nh), (y, A("MID32"), A("T2", a, b))])
+                lin(A("P16", a, b), y, 6144.0 - 16 * a)
+            else:
+                mm([(y, ID, A("T16K", a, b)), (y, A("I16"), nok), (y, A("BC" if nks else "BM128"), one)] +
+                   [(ps("Y23", x0, x1), A("IM8192"), x) for x0, x1, x in an] + [(ps("Y23", x0, x1), A("I8192"), x) for x0, x1, x in ao] +
+                   [(y, A("MI1"), A("RL", a, b))])
+                tt(A("T2", a, b), y, nh if nks else A("NS", a, b), OP.min)
+                lin(A("P16", a, b), A("T2", a, b), (6144.0 if nks else 4096.0) - 16 * a)
+            if les:
+                mm([(ps("dn", a, b), ID, sh), (ps("dn", a, b), A("MI1"), nh), (ps("dn", a, b), A("IM8192"), nok)])
+                act(A("M0", a, b), ps("dn", a, b), AF.Relu)
+                mm([(ps("m1", a, b), ID, nh), (ps("m1", a, b), A("ID32"), A("M0", a, b)), (ps("m1", a, b), A("I4096"), nok)])
+                act(A("M1", a, b), ps("m1", a, b), bias=les - 2048.0)
+            elif nks:
+                mm([(ps("dn", a, b), ID, sh), (ps("dn", a, b), A("IM4096"), nok)])
+                act(A("M0", a, b), ps("dn", a, b), AF.Relu, bias=-2048.0)
+                mm([(ps("m1", a, b), ID, nh), (ps("m1", a, b), A("I4096"), nok)])
+                act(A("M1", a, b), ps("m1", a, b), AF.Relu, bias=-2048.0)
             else:
                 mm([(ps("dn", a, b), A("ID32"), A("NS", a, b)), (ps("dn", a, b), A("MID32"), A("SF", a, b))])
                 tt(A("M1", a, b), ps("dn", a, b), nok, OP.mult)
@@ -403,51 +439,71 @@ def plan(cfg):
                 scan(A("KSC", a, b), A("RSK", 0, b - a), A("KTT", a, b), OP.max)
                 tr(A("MX", a, b), A("KSC", a, b))
                 mm([(ps("D", a, b), A("DM"), A("MX", a, b))])
-                act(A("IND2", a, b), ps("D", a, b), AF.Relu, bias=1.0, scale=-1.0)
+                act(A("IND2", a, b), ps("D", a, b), AF.Relu, bias=1.0, scale=-1.0, other=(0.5, OP.is_lt, None, None))
                 i2, oha, msk = A("IND2", a, b), A("OHA", a, b), A("MSK", a, b)
-                mm([(ps("oh", a, b), A("ID"), i2), (ps("oh", a, b), A("OHM"), i2)])
+                mm([(ps("oh", a, b), A("OH"), i2)])
                 tt(oha, ps("oh", a, b), A("A32", a, b), OP.mult)
-                mm([(ps("oh2", a, b), A("OH2P"), i2), (ps("oh2", a, b), A("OH2M"), i2)])
-                act(A("OHS", a, b), ps("oh2", a, b), bias=1.0, scale=-1.0 / 8192)
-                mm([(ps("colr", a, b), A("BO"), oha)])
-                cp(A("COL", a, b), ps("colr", a, b))
-                mm([(ps("colw", a, b), A("ID"), msk), (ps("colw", a, b), A("BO"), oha)])
-                wrap("COWS", ps("colw", a, b), a, b)
-                if not cfg["q1late"]:
-                    mm([(ps("col2", a, b), A("ID"), msk), (ps("col2", a, b), A("BP"), i2), (ps("col2", a, b), A("BO"), oha)])
-                    wrap("COW2", ps("col2", a, b), a, b)
-                    cp(A("COW16", ja, jb), A("COW2", a + 15, b, 16))
-                    tt(A("Q1", a, b), IND(ADW, A("COW16", ja, jb)), A("OHS", a, b), OP.mult)
-        for a, b in reversed(cfg["dc"]):
-            tt(IND(A("LE"), A("LOFF", a // 16, b // 16)), A("M0" if nks else "SF", a, b), A("M1", a, b), OP.add)
+                if not cfg["q1s"]:
+                    act(A("OHS", a, b), ps("oh", a, b), bias=1.0, scale=-1.0)
+                mm([(ps("colw", a, b), ID, msk), (ps("colw", a, b), A("BO"), oha)])
+                hold("HA", ps("colw", a, b), a, b)
+        for a in range(224, -1, -32):
+            dst = IND(A("LE"), A("LOFF", a // 16, a // 16 + 2))
+            if les:
+                act(dst, A("M1", a, a + 32), AF.Silu)
+            else:
+                tt(dst, A("M0" if nks else "SF", a, a + 32), A("M1", a, a + 32), OP.add)
         if last:
-            dma(("out", "yl", 0, 512), LEW, 128 * 2048, [LEW], [])
+            yl = A("YL") if les else LEW
+            if les:
+                ts(yl, LEW, 12582912.0 - les, OP.add, -12582912.0, OP.add)
+            dma(("out", "yl", 0, 512), yl, 128 * 2048, [yl], [])
         else:
             for a, b in cfg["da"]:
-                dedupe("COL", lambda j: A("COWS", 16 * j + 15, 16 * j + 16), [(A("BP"), A("IND2", a, b)), (A("BO"), A("OHA", a, b))],
-                       "QA", "DSA", "dedA", "MSK", "AOFF", a, b)
-            for a, b in cfg["da"] if cfg["q1late"] else ():
-                tt(A("Q1", a, b), IND(A("AD"), A("AOFF", a // 16, b // 16)), A("OHS", a, b), OP.mult)
+                first_of_32(A("BO"), "OHA", False, "HA", "QA", "MSK", "DSA", "dedA", "AOFF", a, b)
+            for a, b in cfg["da"]:
+                src = IND(A("AD"), A("AOFF", a // 16, b // 16))
+                if not cfg["q1s"]:
+                    tt(A("Q1", a, b), src, A("OHS", a, b), OP.mult)
+                    continue
+                act(A("Q0", a, b), src)
+                for x0 in range(a, b, 128):
+                    x1 = min(b, x0 + 128)
+                    mm([(ps("oh2", x0, x1), A("ID32"), A("Q0", x0, x1)), (ps("oh2", x0, x1), A("MOH8"), A("IND2", x0, x1))])
+                    act(A("Q1", x0, x1), ps("oh2", x0, x1), AF.Relu)
+        two = set()
         for q, (a, b) in enumerate(cfg["p3"]):
             lo, hi = 16 * a, 16 * b
-            src = IND(A(VW, 2048 if a < 128 else 0, 8192), A("P16", a, b))
-            (cp if q in cfg["vv"] else act)(A("VV", lo, hi), src)
-            scan(A("HI", lo, hi), A("RSN", 0, hi - lo), A("VV", lo, hi), OP.max)
-            scan(A("LO", lo, hi), A("RSP", 0, hi - lo), A("VV", lo, hi), OP.min)
+            la = [x0 for x0, x1 in cfg["lg"] if x0 <= a < x1][0]
+            src = IND(A(VW, 16 * la, 8192), A("P16", a, b))
+            if q in cfg["vv"]:
+                two |= set(range(a, b))
+                tt(A("G16", lo, hi), src, A("OFS", 0, hi - lo), OP.add)
+                for c0 in range(lo, hi, 256):
+                    scan(A("HI2", c0 // 2, c0 // 2 + 128), A("G16", c0, c0 + 256, 2), A("G16", c0 + 1, c0 + 256, 2), OP.max, OP.max, -4096.0)
+                    scan(A("LO2", c0 // 2, c0 // 2 + 128, -1), A("G16", c0 + 1, c0 + 256, -2), A("G16", c0, c0 + 255, -2), OP.min, OP.min, 4096.0)
+                continue
+            act(A("VV", lo, hi), src)
+            scan(A("HI", lo, hi), A("RSN", 0, hi - lo), A("VV", lo, hi), OP.max, OP.min)
+            scan(A("LO", lo, hi), A("RSP", 0, hi - lo), A("VV", lo, hi), OP.min, OP.max)
         for a, b in cfg["tail"]:
             ja, jb, lo, hi = a // 16, b // 16, 16 * a, 16 * b
-            zo = A("ZO", a, b)
+            pk = [] if last else segs(m, "O", 0, a, b)
+            zo = pk.pop()[2] if len(pk) == 1 else A("ZO", a, b)
             x = ps("Xz", a, b)
-            mm([(x, A("IQ"), A("ONES", 0, b - a))] + [(ps("Xz", x0, x1), A("ID"), z) for x0, x1, z in segs(m, "N", 0, a, b)] +
-               [(x, A("MIH"), A("HI", lo + 15, hi, 16)), (x, A("MIH"), A("LO", lo + 15, hi, 16))])
+            if a in two:
+                it = [(x, A("BO"), A("OF2", a, b)), (x, A("MIH"), A("HI2", lo // 2 + 7, hi // 2, 8)), (x, A("MIH"), A("LO2", lo // 2, hi // 2, 8))]
+            else:
+                it = [(x, A("IQ"), A("ONES", 0, b - a)), (x, A("MIH"), A("HI", lo + 15, hi, 16)), (x, A("MIH"), A("LO", lo + 15, hi, 16))]
+            mm(it[:1] + [(ps("Xz", x0, x1), ID, z) for x0, x1, z in segs(m, "N", 0, a, b)] + it[1:])
             act(A("ZR", a, b), x, bias=12582912.0)
             act(zo, A("ZR", a, b), AF.Abs, bias=-12582912.0)
             mm([(ps("U16", a, b), A("W16"), zo)])
-            ts(A("FL", a, b), ps("U16", a, b), -1.0, OP.mult, -24568.5, OP.add)
+            lin(A("FL", a, b), ps("U16", a, b), -24568.5, -1.0)
             w = ps("ww", a, b)
-            mm([(w, A("ID"), A("T16", a, b)), (w, A("ID"), A("MSK", 0, b - a)), (w, A("W16"), zo), (w, A("ID"), A("FL", a, b))])
+            mm([(w, ID, A("T16M", a, b)), (w, A("W16"), zo), (w, ID, A("FL", a, b))])
             wrap("WS", w, a, b)
-            ts(A("WW16", ja, jb), A("WS", a + 15, b, 16), 24576.0 - lo, OP.add)
+            lin(A("WW16", ja, jb), A("WS", a + 15, b, 16), 24576.0 - lo)
             yv = A(VN, 4096 + lo, 4096 + hi)
             cp(IND(yv, A("WW16", ja, jb)), zo)
             if last:
@@ -455,23 +511,26 @@ def plan(cfg):
                 dma(("out", "yz", a, b), zo, 256 * (b - a), [zo], [])
                 continue
             y = ps("q2", a, b)
-            mm([(y, A("IE"), A("T16", a, b)), (y, A("OH2P"), A("IND2", a, b)), (y, A("OH2M"), A("IND2", a, b)),
-                (y, A("W16O"), zo), (y, A("IOD"), A("FL", a, b))])
-            act(A("Q2", a, b), y, AF.Relu, bias=col(cQ2))
-            for x0, x1, pk in segs(m, "O", 0, a, b):
-                act(pk, A("ZR", x0, x1), AF.Abs, bias=-12582912.0)
-            for bb in range(4):
-                if a < 64 * bb + 64 <= b and (bb + m) % 4:
+            mm([(y, ID, A("T16", a, b)), (y, A("OH8"), A("IND2", a, b)), (y, A("W16"), zo), (y, ID, A("FL", a, b))])
+            act(A("Q2", a, b), y, AF.Relu, bias=24576.0 - 8192)
+            for x0, x1, x in pk:
+                act(x, A("ZR", x0, x1), AF.Abs, bias=-12582912.0)
+            for bb in range(3, -1, -1):
+                if a <= 64 * bb < b and (bb + m) % 4:
                     src, dst = A("PO%d" % m, 128 * bb, 128 * bb + 128), A("PN%d" % (m + 1), 128 * bb, 128 * bb + 128)
                     add("g", "send", (m, bb, src, dst), [src], [dst], cfg["si"], cfg["sl"])
-        if not last:
-            for a, b in cfg["tail"]:
-                ja, jb = a // 16, b // 16
-                tt(IND(A("AD"), A("AOFF", ja, jb)), A("Q1", a, b), A("Q2", a, b), OP.add)
-    used = [(x[1], x[2]) for o in ops for x in o["r"] if x[0] == "CM"]
-    names = {x[0] for o in ops for x in o["r"]}
-    return [o for o in ops if not o["w"] or (o["w"][0][0] in names and (o["w"][0][0] != "CM" or any(
-        lo < o["w"][0][2] and o["w"][0][1] < hi for lo, hi in used)))]
+            for x0 in range(b - 32, a - 1, -32):
+                tt(IND(A("AD"), A("AOFF", x0 // 16, x0 // 16 + 2)), A("Q1", x0, x0 + 32), A("Q2", x0, x0 + 32), OP.add)
+    while True:
+        used = {}
+        for o in ops:
+            for x in o["r"]:
+                used.setdefault(x[0], []).append((x[1], x[2]))
+        keep = [o for o in ops if not o["w"] or o["k"] == "send" or any(
+            lo < o["w"][0][2] and o["w"][0][1] < hi for lo, hi in used.get(o["w"][0][0], ()))]
+        if len(keep) == len(ops):
+            return ops
+        ops[:] = keep
 
 
 def schedule(ops, cfg):
@@ -487,128 +546,146 @@ def schedule(ops, cfg):
         for accs, w in ((o["r"], False), (o["w"], True)):
             for x in accs:
                 h = hist.setdefault(x[0], [])
-                if w and x[3] == 1:
+                if w and abs(x[3]) == 1:
                     h[:] = [y for y in h if not (x[1] <= y[1] and y[2] <= x[2])]
                 h.append((i, x[1], x[2], w))
         o["d"] = d
         o["b"] = {x[0] for x in o["r"] + o["w"] if psum(x)}
+    anc = [0] * n
+    for i, o in enumerate(ops):
+        m = 0
+        for j in o["d"]:
+            m |= anc[j]
+        o["d"] = {j for j in o["d"] if not (m >> j) & 1}
+        for j in o["d"]:
+            m |= 1 << j
+        anc[i] = 0 if o["k"] == "send" else m
     succ = [[] for _ in ops]
     for i, o in enumerate(ops):
-        for j in o["d"]:
+        for j in sorted(o["d"]):
             succ[j].append(i)
     lat = cfg["lat"]
     eng = [o["e"] for o in ops]; cost = [o["c"] for o in ops]; after = [o["l"] for o in ops]; xf = [o["x"] for o in ops]
     banks = [sorted(o["b"]) for o in ops]; deps = [sorted(o["d"]) for o in ops]
 
-    def run(pr, win):
-        left = [len(d) for d in deps]
-        base = [0.0] * n
-        ready = {e: [] for e in "vspgy"}
-        for i in range(n):
-            if left[i] == 0:
-                ready[eng[i]].append(i)
-        free = {e: 0.0 for e in "vspgyx"}; fin = [0.0] * n; start = [0.0] * n; bank = {}; order = []; extra = [()] * n
-        for _ in range(n):
-            best = None
-            for e, rl in ready.items():
-                if not rl:
-                    continue
-                es = []
-                for i in rl:
-                    t = base[i] if base[i] > free[e] else free[e]
-                    for b in banks[i]:
-                        for e2, j in bank.get(b, {}).items():
-                            if e2 != e and fin[j] + lat > t:
-                                t = fin[j] + lat
-                    es.append(t)
-                t0 = min(es)
-                if best is None or t0 < best[0]:
-                    best = (t0, e, es)
-            t0, e, es = best
-            rl = ready[e]
-            if e == "y":
-                x = min((rl[x], x) for x in range(len(rl)) if es[x] <= t0 + 1.0)[1]
-            else:
-                x = max((pr[rl[x]], x) for x in range(len(rl)) if es[x] <= t0 + win[rl[x]])[1]
-            i = rl.pop(x)
-            ex = []
-            for b in banks[i]:
-                ex += [j for e2, j in bank.get(b, {}).items() if e2 != e]
-                bank.setdefault(b, {})[e] = i
-            extra[i] = ex; start[i] = es[x]
-            free[e] = es[x] + cost[i]; fin[i] = free[e] + after[i]
-            if xf[i]:
-                fin[i] = free["x"] = max(fin[i], free["x"]) + xf[i]
-            order.append(i)
-            for j in succ[i]:
-                left[j] -= 1
-                if fin[i] + lat > base[j]:
-                    base[j] = fin[i] + lat
-                if left[j] == 0:
-                    ready[eng[j]].append(j)
-        return max(fin), order, extra, start
-
-    def levels(order, extra, w):
-        pr = [0.0] * n; nxt = {}
-        for i in reversed(order):
-            t = max([pr[j] + lat for j in succ[i]] + [0.0]) + after[i] + xf[i]
-            j = nxt.get(eng[i])
-            if j is not None and w:
-                t = max(t, t + w * (pr[j] - t))
-            pr[i] = cost[i] + t; nxt[eng[i]] = i
-        return pr
-
-    def score(r):
-        tot = r[0]
-        for c2, l2 in alts:
-            free = {e: 0.0 for e in "vspgyx"}; fin = [0.0] * n
-            for i in r[1]:
-                t = free[eng[i]]
-                for j in deps[i]:
-                    if fin[j] + l2 > t:
-                        t = fin[j] + l2
-                for j in r[2][i]:
-                    if fin[j] + l2 > t:
-                        t = fin[j] + l2
-                free[eng[i]] = t + c2[i]; fin[i] = t + c2[i] + after[i]
-                if xf[i]:
-                    fin[i] = free["x"] = max(fin[i], free["x"]) + xf[i]
-            tot += max(fin)
-        return tot
-
-    alts = []
-    if cfg["iters"] or cfg["moves"]:
-        for alt in cfg["alts"]:
-            c2 = dict(cfg); c2.update(alt)
-            alts.append(([o["c"] for o in plan(c2)], c2["lat"]))
-    rng = np.random.RandomState(cfg["seed"])
-    pr = levels(list(range(n)), None, 0.0); win = [cfg["win"]] * n
-    best = run(pr, win); bs = score(best); top = (bs, best)
-    for it in range(cfg["iters"]):
-        p2, w2 = list(pr), list(win)
-        u = rng.uniform()
-        if u < 0.15:
-            lv = levels(best[1], best[2], float(rng.uniform(0.2, 1.0))); a = float(rng.uniform(0.1, 1.0))
-            p2 = [(1 - a) * x + a * y for x, y in zip(pr, lv)]
-        else:
-            t0 = rng.uniform(0, best[0]); sp = rng.uniform(2000, 12000)
-            for i in range(n):
-                if t0 <= best[3][i] < t0 + sp and rng.uniform() < 0.3:
-                    p2[i] += float(rng.normal(0, cfg["noise"]))
-                    if rng.uniform() < 0.3:
-                        w2[i] = float(rng.choice([0.0, 70.0, 200.0, 500.0]))
-        r = run(p2, w2); s = score(r)
-        if s <= bs + cfg["temp"] * (1.0 - it / cfg["iters"]) * rng.exponential():
-            best, bs, pr, win = r, s, p2, w2
-            if s < top[0]:
-                top = (s, r)
-    order = list(top[1][1])
     E = {e: x for x, e in enumerate("vspgy")}
     en = [E[e] for e in eng]; bk = [[int(b[1:]) for b in bs_] for bs_ in banks]
-    sets = [(cost, lat)] + alts
+    dur = [xf[i] or cost[i] for i in range(n)]
+    pre = [cost[i] + after[i] if xf[i] else 0.0 for i in range(n)]
+    post = [0.0 if xf[i] else after[i] for i in range(n)]
 
-    if cfg.get("order"):
-        order = [(ord(cfg["order"][2 * x]) - 48) * 40 + ord(cfg["order"][2 * x + 1]) - 48 for x in range(n)]
+    def place(seq, nxt, pre, post):
+        S = [[] for _ in range(5)]; F = [[] for _ in range(5)]
+        BS = [[] for _ in range(8)]; BF = [[] for _ in range(8)]; BE = [[] for _ in range(8)]
+        start = [0.0] * n; rdy = [0.0] * n; end = 0.0
+        for i in seq:
+            e = en[i]; c = dur[i]; t = rdy[i] + pre[i]
+            s = S[e]; f = F[e]; bs = bk[i]; m = len(s)
+            while True:
+                x = m
+                while x and f[x - 1] > t:
+                    x -= 1
+                while x < m and s[x] < t + c:
+                    t = f[x]; x += 1
+                t0 = t
+                for b in bs:
+                    ss = BS[b]; ff = BF[b]; ee = BE[b]
+                    y = mb = len(ss)
+                    while y and ff[y - 1] + lat > t:
+                        y -= 1
+                    while y < mb and ss[y] < t + c + lat:
+                        if ee[y] != e and ff[y] + lat > t:
+                            t = ff[y] + lat
+                        y += 1
+                if t == t0:
+                    break
+            s.insert(x, t); f.insert(x, t + c)
+            for b in bs:
+                ss = BS[b]; y = len(ss)
+                while y and ss[y - 1] > t:
+                    y -= 1
+                ss.insert(y, t); BF[b].insert(y, t + c); BE[b].insert(y, e)
+            start[i] = t
+            z = t + c + post[i]
+            if z > end:
+                end = z
+            z += lat
+            for j in nxt[i]:
+                if z > rdy[j]:
+                    rdy[j] = z
+        return end, start
+
+    def forward(key):
+        for i in range(n):
+            for j in deps[i]:
+                if key[j] >= key[i]:
+                    key[i] = key[j] + 0.01
+        return place(sorted(range(n), key=lambda i: key[i]), succ, pre, post)
+
+    def both(key):
+        r = forward(key)
+        s2 = place(sorted(range(n), key=lambda i: -r[1][i] - dur[i]), deps, post, pre)[1]
+        r3 = place(sorted(range(n), key=lambda i: -s2[i] - dur[i]), succ, pre, post)
+        return r3 if r3[0] <= r[0] else r
+
+    lv = [0.0] * n
+    for i in range(n - 1, -1, -1):
+        lv[i] = pre[i] + dur[i] + post[i] + max([lv[j] + lat for j in succ[i]] + [0.0])
+    rng = np.random.RandomState(cfg["seed"])
+    cur = best = both([-x for x in lv])
+    free = [i for i in range(n) if "m" in ops[i]]
+    mode = [0] * n; top = list(mode)
+    for it in range(cfg["iters"]):
+        key = list(cur[1]); undo = []
+        if rng.uniform() < cfg["flip"]:
+            for _ in range(1 + rng.randint(2)):
+                i = free[rng.randint(len(free))]; ms_ = ops[i]["m"]
+                undo.append((i, mode[i]))
+                mode[i] = (mode[i] + 1 + rng.randint(len(ms_) - 1)) % len(ms_)
+                en[i] = E[ms_[mode[i]][0]]; dur[i] = ms_[mode[i]][3]
+        elif rng.uniform() < 0.3:
+            a = rng.uniform(-3000, cur[0]); sp = rng.uniform(1000, 10000)
+            nz = (rng.normal(0, rng.choice([200.0, 600.0, 1500.0]), n) * (rng.uniform(size=n) < 0.4)).tolist()
+            for i in range(n):
+                if a <= key[i] < a + sp:
+                    key[i] += nz[i]
+        else:
+            for _ in range(1 + rng.randint(2)):
+                i = rng.randint(n); dl = rng.exponential(1500.0); st = [i]
+                if rng.uniform() < 0.5:
+                    key[i] -= dl
+                    while st:
+                        x = st.pop()
+                        for j in deps[x]:
+                            v = key[x] - dur[j] - pre[x] - post[j] - lat
+                            if key[j] > v:
+                                key[j] = v; st.append(j)
+                else:
+                    key[i] += dl
+                    while st:
+                        x = st.pop()
+                        for j in succ[x]:
+                            v = key[x] + dur[x] + pre[j] + post[x] + lat
+                            if key[j] < v:
+                                key[j] = v; st.append(j)
+        r = both(key) if rng.uniform() < 0.3 else forward(key)
+        if r[0] <= cur[0] + cfg["temp"] * (1.0 - it / cfg["iters"]) * rng.exponential():
+            cur = r
+            if r[0] < best[0]:
+                best = r; top = list(mode)
+        else:
+            for i, x in reversed(undo):
+                mode[i] = x; en[i] = E[ops[i]["m"][x][0]]; dur[i] = ops[i]["m"][x][3]
+    for i in free:
+        o = ops[i]
+        o["e"], o["k"], o["a"], o["c"] = o["m"][top[i]]
+        en[i] = E[o["e"]]; cost[i] = o["c"]; o["mode"] = top[i]
+    key = [best[1][i] - pre[i] for i in range(n)]
+    order = sorted(range(n), key=lambda i: key[i])
+    sets = [(cost, lat)]
+    for alt in cfg["alts"]:
+        c2 = dict(cfg); c2.update(alt)
+        sets.append(([o["m"][top[i]][3] if "m" in o else o["c"] for i, o in enumerate(plan(c2))], c2["lat"]))
 
     def timed(order, c2, l2, old=None, lo=0):
         if old is None:
@@ -724,7 +801,7 @@ def rank_program(g, core, T, topo):
         if a[0] in ("in", "out"):
             t = T[a[1]]
             return t[:] if a[3] - a[2] == t.shape[1] else t[:, a[2]:a[3]]
-        return T[a[0]][:, a[1]:a[2]] if a[3] == 1 else T[a[0]][:, a[1]:a[2]:a[3]]
+        return T[a[0]][:, a[1]:a[2]] if a[3] == 1 else T[a[0]][:, cols(a)]
 
     count = {}; done = {}; seen = {}; ndma = [0]; final = []; sent = [0]
 
@@ -777,7 +854,10 @@ def rank_program(g, core, T, topo):
         elif k == "tr":
             ins = q.transpose(X(a[0]), X(a[1]))
         elif k == "act":
-            ins = q.activation(X(a[0]), X(a[1]), a[2], bias=X(a[3]), scale=X(a[4]))
+            if a[0][0] == "*":
+                ins = q.activation(X(a[0]), X(a[1]), a[2])
+            else:
+                ins = q.activation(X(a[0]), X(a[1]), a[2], bias=X(a[3]), scale=X(a[4]))
         elif k == "iota":
             if dty(a[0]) == I32:
                 ins = q.iota(X(a[0]), a[1], a[2], a[3])

@@ -7,33 +7,35 @@ Q4 = ((192, 256), (128, 192), (64, 128), (0, 64))
 H2 = ((128, 256), (0, 128))
 T3 = ((128, 256), (64, 128), (0, 64))
 CFG = {
-    "si": 1000.0, "sl": 2800.0,
+    "si": 1000.0, "sl": 3600.0,
     "p1": Q4,
     "adv": (0,),
     "sv": (),
-    "abss": (3,),
+    "abss": (),
     "p3": Q4,
     "vv": (),
-    "tail": T3,
-    "lg": T3, "ad": H2, "dc": ((0, 256),), "da": ((0, 256),),
-    "nks": True, "q1s": True, "cvt": True, "les": False, "t2s": False, "selg": 8,
-    "s": ("NH",), "tiu": False, "flip": 0.3,
-    1: {"adv": (0, 1, 2, 3)},
-    4: {"adv": (0, 1)},
-    "seed": 7, "iters": 22000, "temp": 120.0, "moves": 4000, "temp2": 60.0,
-    "alts": ({"g": 1.6, "sc": 4.0, "f": 1.3, "lat": 130.0},),
-    "g": 1.7, "sc": 4.2, "f": 1.1, "lat": 100.0, "pe": 0.42, "bw": 250.0, "vo": 55.0, "so": 72.0, "mn": 0, "po": 60.0,
+    "tail": Q4,
+    "lg": T3, "ad": T3, "dc": ((0, 256),), "da": ((0, 256),),
+    "mr": H2, "am": H2, "q1s": True, "cvt": True, "les": False, "tl": False, "s1": 1000.0, "selg": 8,
+    "s": ("NH",), "both": 0.2, "flip": 0.3,
+    1: {"adv": (0, 1, 2, 3), "p1": ((224, 256), (192, 224)) + Q4[1:]},
+    4: {"tail": T3[:2] + ((32, 64), (0, 32)), "p3": Q4[:3] + ((32, 64), (0, 32))},
+    "seed": 7, "iters": 4000, "sweeps": 5, "its": 2500, "span": 24000.0, "temp": 120.0, "moves": 36000, "temp2": 60.0,
+    "alts": ({"lat": 140.0, "po": 100.0, "pe": 0.5, "sl": 4500.0, "bw": 200.0},
+             {"g": 1.3, "sc": 2.6, "bw": 350.0, "dl": 1500.0}, {"g": 2.2, "sc": 5.8}),
+    "g": 1.7, "sc": 4.2, "f": 1.1, "lat": 110.0, "pe": 0.42, "bw": 250.0, "dl": 2000.0, "vo": 55.0, "so": 72.0, "mn": 0, "po": 60.0,
 }
 
 _S = {
-    "VW1": (8192, BF), "VW0": (8192, BF), "ADi": (2048, I32), "AD": (2304, F32), "RUN": (64, U16),
-    "LEi": (512, I32), "LE": (768, F32), "YL": (512, F32),
+    "VW1": (8192, BF), "VW0": (8192, BF), "ADi": (2048, I32), "AD": (2080, F32),
+    "LEi": (512, I32), "LE": (544, F32), "YL": (512, F32),
     "CBi": (16, I32), "KAi": (8, I32), "THi": (8, I32), "COLS": (64, F32), "CI": (16, I32), "CBF": (16, F32), "CBL": (16, U16),
     "IO": (144, BF), "MI": (256, BF), "MSK": (256, BF), "MK1": (256, BF), "CE": (256, F16), "HD": (256, BF),
     "ID32": (128, F32), "MID32": (128, F32), "DM": (128, F32), "IC16": (128, F16), "DF": (144, BF), "IDW": (144, BF),
     "Z1": (144, BF), "Z2": (144, BF), "ZM1": (144, BF), "EQ": (16, F32),
-    "SEL": (2048, BF), "BC": (128, F16), "MBC": (128, F16), "MI16": (128, BF), "SH": (256, F16), "NH": (256, F16),
-    "T16": (256, BF), "T16M": (256, BF), "T16K": (256, F16), "RSD": (256, F32), "MSKC": (256, BF),
+    "SEL": (2048, BF), "TC": (256, BF), "QH": (256, F16), "I69": (128, F16), "KH1": (256, F16), "KH2": (256, F16),
+    "GZ1": (8, BF), "GZM": (8, BF), "GZ2": (8, BF), "SH": (256, F16), "NH": (256, F16),
+    "T16": (256, BF), "T16M": (256, BF), "T16K": (256, F16), "ZM8": (144, BF),
     "RSN": (1024, BF), "RSP": (1024, BF), "RSK": (256, BF), "OFS": (1024, BF), "OFI": (256, BF), "OF2": (256, BF),
     "XI": (256, I32), "A32": (256, I32), "A16": (256, U16), "CW16": (16, U16), "HC": (256, F16),
     "S16": (256, U16), "SF": (256, F32), "G16": (4096, F16), "N16": (256, U16), "NS": (256, F32),
@@ -51,7 +53,7 @@ for _m in range(1, STEPS):
     _S["PO%d" % _m] = (512, BF)
     _S["PN%d" % (_m + 1)] = (512, BF)
 _AL = {n: 128 * i for i, n in enumerate(
-    "BO WT W16 ONES SU OHM OH OH8 MOH8 I16 MI1 MBO MIH IQ IM32 IM4096 KH KL BM128 BM8192 B32 GI TMP I4096 I8192 IM8192".split())}
+    "BO WT W16 ONES SU OHM OH OH8 MOH8 MI8 MI1 MIH IQ IM32 IM4096 KH KL M256 K0 IM512 BM8192 B32 GI TMP I4096 I8192 IM8192".split())}
 _S["CM"] = (128 * len(_AL), BF)
 SCRATCH = {k: ("sbuf", [128, w], d) for k, (w, d) in _S.items()}
 for _b in range(8):
@@ -61,7 +63,7 @@ SEMAPHORES = ["cv", "cs", "cp", "cg", "sent"] + ["d%d" % i for i in range(48)] +
 SEM = {"v": "cv", "s": "cs", "p": "cp", "g": "cg"}
 TWO = (BF, F16, U16)
 (cK, cG, cG15, cW, cKL, cKH, cCP, cTHR, c16K, cK1, cE15, cPAR, cEV, cP2048, cE2048, cQ2, cP2, cPD,
- cW16, cT, cNK, cKM, cMPAR, cMEV, cP32) = range(25)
+ cW16, cT, cK16, cKM, cMPAR, cMEV, cP32) = range(25)
 
 
 def A(n, lo=0, hi=None, st=1):
@@ -124,7 +126,7 @@ def ps(role, a, b, st=1):
 def plan(cfg):
     ops = []
     cyc = 0.83 * cfg["f"]
-    nks = cfg["nks"]; cfg0 = cfg
+    cfg0 = cfg
     les = 32.0 if cfg["les"] else 0.0
 
     def add(eng, kind, args, rd, wr, cost, lat=0.0, xfer=0.0):
@@ -190,7 +192,7 @@ def plan(cfg):
         add("p", "mm", items, [x for o, l, r in items for x in (l, r)], [o for o, l, r in items], c)
 
     def dma(out, i, nbytes, rd, wr):
-        add("y", "dma", (out, i), rd, wr, 60.0, 2000.0, nbytes / cfg["bw"])
+        add("y", "dma", (out, i), rd, wr, 60.0, cfg["dl"], nbytes / cfg["bw"])
 
     def iota(out, pat, base, cm):
         add("g", "iota", (out, pat, base, cm), [], [out], 130 + 2 * width(out) * cyc)
@@ -202,9 +204,8 @@ def plan(cfg):
         act(out, i, bias=plus, scale=mul, vec=out[0].rstrip("01") not in cfg["s"])
 
     def load(name, src, lo=0, hi=None):
-        at = 4096 if name == "VW1" else 0
-        o = A(name, at + lo, None if hi is None else at + hi)
-        dma(o, ("in", src, lo, o[2] - at), 128 * width(o) * (2 if dty(o) in TWO else 4), [], [o])
+        o = A(name, lo, hi)
+        dma(o, ("in", src, lo, o[2]), 128 * width(o) * (2 if dty(o) in TWO else 4), [], [o])
 
     def blk(n, k):
         return A(n, 128 * k, 128 * k + 128)
@@ -233,29 +234,25 @@ def plan(cfg):
 
     ts(ci(1), ci(0), 15, OP.bitwise_and); cp(col(cK), ci(1)); tt(col(cG), ci(0), ci(1), OP.subtract)
     ts(ci(4), ci(0), 1, OP.bitwise_and); cp(col(cPAR), ci(4))
-    aff(cG15, cG, 1.0, 15.0); aff(cW, cK, 14.0, 1.0); aff(c16K, cK, -1.0, 16.0); aff(cK1, cK, 1.0, 9.0 if nks else 1.0)
+    aff(cG15, cG, 1.0, 15.0); aff(cW, cK, 14.0, 1.0); aff(c16K, cK, -1.0, 16.0); aff(cK1, cK, -1.0, -9.0)
     aff(cEV, cPAR, -1.0, 1.0); aff(cP32, cPAR, 1.0 / 32, 0.0)
     act(col(cE15), col(cK), AF.Relu, bias=-14.0)
-    aff(cT, cE15, 1.0, -1.0); aff(cNK, cK, -1.0, -1.0); aff(cKM, cK, 1.0, -2048.0)
+    aff(cT, cE15, 1.0, -1.0); aff(cK16, cK, 1.0, 16.0)
     ts(ci(2), A("KAi", 0, 1), 1184.0, OP.add); ts(ci(3), ci(2), 31, OP.bitwise_and); cp(col(cKL), ci(3))
     tt(col(cKH), ci(2), ci(3), OP.subtract); aff(cCP, cKL, 2048.0, 40960.0)
-    if nks:
-        ts(col(cTHR), A("THi", 0, 1), -1.0, OP.mult, 4095.5, OP.add)
-    else:
-        ts(col(cTHR), A("THi", 0, 1), -4096.0, OP.add)
+    act(col(cTHR), A("THi", 0, 1), bias=4095.5, scale=-1.0)
     ts(ci(5), ci(1), 14.0, OP.mult, 9.0, OP.add); ts(ci(6), ci(5), 15, OP.bitwise_and); ts(col(cW16), ci(6), -8.0, OP.add)
     ms(A("AN1"), 128.0)
     ts(A("IDW"), A("DF"), 0.0, OP.is_equal); ts(A("BO"), A("GI"), col(cG), OP.is_equal)
     ts(A("IC16"), ID, 19616.0, OP.mult); ts(A("Z1"), A("IO"), col(cG15), OP.is_equal)
-    act(A("ONES"), ID, bias=1.0, scale=0.0)
-    for n, v in (("I16", 8.0 if nks else 16.0), ("I4096", 4096.0), ("I8192", 8192.0), ("IM8192", -8192.0),
+    iota(A("ONES"), [[0, 128]], 1, 0); iota(A("M256"), [[0, 128]], -1536, 0)
+    for n, v in (("MI8", -8.0), ("I4096", 4096.0), ("I8192", 8192.0), ("IM8192", -8192.0),
                  ("MI1", -1.0), ("MIH", -0.5), ("IQ", 0.25), ("IM32", -32.0), ("IM4096", -4096.0),
                  ("KH", col(cKH)), ("KL", col(cKL)), ("ID32", 1.0), ("MID32", -1.0)):
         act(A(n), ID, scale=v)
-    for n, v in (("WT", col(cW)), ("W16", col(cW16)), ("MBO", -1.0), ("BM128", -128.0), ("BM8192", -8192.0),
-                 ("B32", 1.0 / (64 if nks else 32)), ("TMP", col(cE15))):
+    for n, v in (("WT", col(cW)), ("W16", col(cW16)), ("BM8192", -8192.0),
+                 ("B32", 1.0 / 64), ("TMP", col(cE15))):
         act(A(n), A("BO"), scale=v)
-    act(A("BC"), A("BO"), scale=-255.5); act(A("MBC"), A("BO"), scale=255.5); act(A("MI16"), ID, scale=-8.0)
     act(A("Z2"), A("Z1"), scale=2.0); act(A("ZM1"), A("Z1"), scale=-1.0)
     msum(A("DM"), A("TMP"), A("MI1"))
     act(A("OHM"), A("IDW", 0, 128), scale=col(cT)); msum(A("OH"), ID, A("OHM"))
@@ -264,7 +261,19 @@ def plan(cfg):
     ts(A("MSK"), A("MI"), col(cK), OP.not_equal, -4194304.0, OP.mult)
     ts(A("MK1"), A("MI"), col(cK), OP.is_equal)
     ts(A("EQ"), A("MI", 0, 16), col(cK), OP.is_equal)
-    ts(A("T16K"), A("T16"), col(cKM), OP.add)
+    act(A("K0"), ID, bias=-2040.0 / 128, scale=0.0)
+    for n, v in (("GZ1", 1.0), ("GZM", -1.0), ("GZ2", 2.0)):
+        act(A(n), A("BO", 0, 128, 16), scale=v)
+    act(A("I69"), ID, scale=1103.0 / 16); act(A("IM512"), ID, scale=-512.0); act(A("ZM8"), A("Z1"), scale=-8192.0)
+
+    def svo(t):
+        a, b = [x for x in cfg["lg"] if x[0] <= t < x[1]][0]
+        return 4096 + 16 * (256 - b) - 16 * a
+
+    act(col(cKM), A("EQ", 2, 3), scale=-1.0)
+    for x, (a, b) in enumerate(cfg["lg"]):
+        act(col(30 + x), A("EQ", 1, 2), bias=col(cKM), scale=float(svo(a)))
+        act(A("TC", a, b), A("T16", a, b), bias=col(30 + x), scale=A("EQ", 0, 1))
     for k in range(16):
         if k < cfg["selg"]:
             asel(blk("SEL", k), ID, [[0, 8], [1, 16]], OP.is_equal, -k, 0)
@@ -272,20 +281,14 @@ def plan(cfg):
             act(blk("SEL", k), ID, scale=A("EQ", k, k + 1))
     p = ps("con", 0, 256)
     mm([(p, ID, A("T16")), (p, ID, A("MSK"))]); act(A("T16M"), p)
-    act(A("MSKC"), A("MSK"), bias=256.0); act(A("HD"), A("MSK"), bias=-2097152.0, scale=-1.0)
-    act(A("RSD"), A("MSK"), bias=1.0e9, scale=0.0); act(A("RSD", 0, 256, 16), A("IO", 0, 16), bias=col(cNK), scale=-16.0)
-    act(A("RSK"), A("MSK"), scale=0.0); act(A("RSK", 0, 256, 16), A("IO", 0, 16), bias=-3.0e7, scale=0.0)
+    act(A("HD"), A("MSK"), bias=-2097152.0, scale=-1.0)
+    iota(A("RSK"), [[0, 16], [32767, 16]], -30000, 0)
     act(A("OF2"), A("OFI"), bias=col(cP32), scale=col(cEV))
-    act(A("AD", 0, 256), A("MSK"), scale=0.0)
-    if cfg["cvt"]:
-        act(A("LE", 256, 768), A("LEi"), bias=les)
-        for a in (0, 1024):
-            act(A("AD", 256 + a, 1280 + a), A("ADi", a, a + 1024))
-    else:
-        ts(A("RUN"), A("T16", 0, 64), col(cK), OP.add)
-        act(A("LE", 256, 768), IND(A("LEi"), A("RUN", 0, 32)), bias=les)
-        for a in (0, 1024):
-            act(A("AD", 256 + a, 1280 + a), IND(A("ADi", a, a + 1024), A("RUN")))
+    ms(A("AD", 0, 32), 0.0)
+    act(A("LE", 32, 544), A("LEi"), AF.Silu if les else AF.Identity, bias=les)
+    ops[-1]["c"] += 1300.0 * cfg["f"] if les else 0.0
+    for a in (0, 1024):
+        act(A("AD", 32 + a, 1056 + a), A("ADi", a, a + 1024))
 
     def segs(m, side, part, a, b):
         if side == "N" and m == 1:
@@ -293,45 +296,44 @@ def plan(cfg):
         out = []
         for bb in range(a // 64, (b + 63) // 64):
             x0, x1 = max(a, 64 * bb), min(b, 64 * bb + 64)
-            n = "PN%d" % m if side == "N" else "PO%d" % m if (bb + m) % 4 else "PN%d" % (m + 1)
-            out.append((x0, x1, A(n, 64 * (bb + part) + x0, 64 * (bb + part) + x1)))
+            n = "PO%d" % m if side == "O" else "PN%d" % m if (bb + m - 1) % 4 else "PO%d" % (m - 1)
+            o = 128 * (bb // 2) + (64 if part == 0 else 128 * (bb % 2))
+            if out and out[-1][2][0] == n and out[-1][2][2] == o + x0:
+                out[-1] = (out[-1][0], x1, A(n, out[-1][2][1], o + x1))
+            else:
+                out.append((x0, x1, A(n, o + x0, o + x1)))
         return out
 
-    ts(A("CBF"), A("CBi"), -256.0, OP.add); cp(A("CBL"), A("IO", 0, 16))
-    tt(A("CE"), IND(A("CBF"), A("CBL")), A("MK1"), OP.mult)
+    cp(A("CBL"), A("IO", 0, 16))
+    tt(A("CE"), IND(A("CBi"), A("CBL")), A("MK1"), OP.mult)
     mm([(ps("dedC", 0, 256), A("BO"), A("CE"))])
-    cp(A("CN1"), ps("dedC", 0, 256))
+    lin(A("CN1"), ps("dedC", 0, 256), 1280.0)
 
     def wrap(out, p, a, b):
-        scan(A(out, a, b), A("RSK", 0, b - a), p, OP.max)
+        scan(A(out, a, b), A("RSK", 0, b - a), p, OP.max, OP.min)
 
     def hold(out, p, a, b):
         scan(A(out, a, b), A("HD", 0, b - a), p, OP.max, OP.min, -30000.0)
 
-    def places(it, ds, r1, off, a, b):
-        mm(it)
-        scan(A(ds, a, b), A("RSD", a, b), ps(r1, a, b), OP.max, OP.min, 1.0e6)
-        lin(A(off, a // 16, b // 16), A(ds, a + 15, b, 16), 256.0)
-
-    def first_of_32(l, r, made, held, q, msk, ds, r1, off, a, b):
-        p = ps(r1, a, b)
-        if not made:
-            mm([(p, l, A(r, a, b))])
-        it = [(p, ID, A(msk, a, b)), (p, l, A(r, a, b))]
+    def first_of_32(l, r, held, q, r1, off, plus):
+        mm([(ps(r1, 0, 256), l, A(r))])
         for x, d in enumerate((1, 17)):
-            eq = A(q, 256 * x + a + d, 256 * x + b)
-            tt(eq, A(held, a, b - d), ps(r1, a + d, b), OP.is_equal)
-            it.append((ps(r1, a + d, b), A("BM8192"), eq))
-        places(it, ds, r1, off, a, b)
+            tt(A(q, 256 * x + d, 256 * x + 256), A(held, 0, 256 - d), ps(r1, d, 256), OP.is_equal)
+        p = ps(r1, 0, 16)
+        mm([(p, ID, A(held, 15, 256, 16))] + [(p, zw("ZM8", k), A(q, 256 * x + k, 256 * x + 256, 16)) for x in range(2) for k in range(16)])
+        for x in range(2):
+            ts(A(off, x, 16, 2), ps(r1, x, 16, 2), 32.0 + plus, OP.add, col(cK16 if x else cK), OP.max)
 
-    ADW, LEW = A("AD", 256, 2304), A("LE", 256, 768)
+    for q in ("QC", "QA"):
+        ms(A(q, 0, 16), 0.0); ms(A(q, 256, 288), 0.0)
+    ADW, LEW = A("AD", 32, 2080), A("LE", 32, 544)
     for m in range(1, STEPS + 1):
         last = m == STEPS
         cfg = dict(cfg0); cfg.update(cfg0.get(m, {}))
         U, C = "UN", "CN%d" % (m % 2)
         VW, VN = "VW%d" % (m % 2), "VW%d" % ((m + 1) % 2)
-        VF = A(VW, 4096, 8192)
-        for h in range(2, 4):
+        VF = A(VW, 0, 4096)
+        for h in range(2):
             x, y = A(VN, 2048 * h, 2048 * h + 2048), A(VW, 2048 * h, 2048 * h + 2048)
             dma(x, y, 128 * 4096, [y], [x])
         for a, b in cfg["ad"]:
@@ -342,14 +344,11 @@ def plan(cfg):
             mm([(ps("uc", a, b), A("IM4096"), A("QB", a, b))] + [(ps("uc", x0, x1), A("WT"), z) for x0, x1, z in zs])
             lin(A(U, a, b), ps("uc", a, b), 4096.0 * 136 - 2048)
             if m > 1:
-                if cfg["tiu"]:
-                    lin(A("TI", a, b), A(U, a, b), 1103.0 * 2048, 1103.0)
-                else:
-                    ts(A("TI", a, b), ps("uc", a, b), 4096.0 * 136, OP.add, 1103.0, OP.mult)
-                ts(A("C32", a, b), A("TI", a, b), 4, OP.arith_shift_right, 511, OP.bitwise_and)
-                lin(A(C, a, b), A("C32", a, b), -256.0)
+                lin(A("QH", a, b), A(U, a, b), 1555.25, 1103.0 / 8192)
+                mm([(ps("X", a, b), A("I69"), A(U, a, b)), (ps("X", a, b), A("IM512"), A("QH", a, b))])
+                ts(A(C, a, b), ps("X", a, b), 796544.0, OP.add, 1279.53125, OP.add)
             x = ps("X", a, b)
-            mm([(x, A("KH"), A(U, a, b)), (x, A("KL"), A(U, a, b)), (x, A("IC16"), A(C, a, b))])
+            mm([(x, A("IC16"), A(C, a, b)), (x, A("IC16"), A("M256", 0, b - a)), (x, A("KH"), A(U, a, b)), (x, A("KL"), A(U, a, b))])
             lin(A("XI", a, b), x, col(cCP))
             ts(A("A32", a, b), A("XI", a, b), 5, OP.arith_shift_right, 2047, OP.bitwise_and)
             lin(A("A16", a, b), A("A32", a, b), 0.0)
@@ -359,24 +358,16 @@ def plan(cfg):
             if m == 1:
                 cp(A("CW16", ja, jb), A("CBi", ja, jb))
             else:
-                lin(A("CW16", ja, jb), A("HC", a + 15, b, 16), 256.0)
-            if nks:
-                act(A("SH", a, b), IND(LEW, A("CW16", ja, jb)), bias=-2048.0 - les)
-                lin(A("S16", a, b), A("SH", a, b), 2048.0)
-            else:
-                act(A("SF", a, b), IND(LEW, A("CW16", ja, jb)))
-                lin(A("S16", a, b), A("SF", a, b), 0.0)
+                lin(A("CW16", ja, jb), A("HC", a + 15, b, 16), -1280.0)
+            act(A("SH", a, b), IND(LEW, A("CW16", ja, jb)), bias=-2048.0 - les)
+            lin(A("S16", a, b), A("SH", a, b), 2048.0)
         for q, (a, b) in enumerate(cfg["p1"]):
             lo, hi = 16 * a, 16 * b
             src = IND(A("ADi") if m == 1 else ADW, A("A16", a, b))
             act(A("G16", lo, hi), src, bias=-2048.0, vec=q in cfg["adv"])
             mm([(ps("n", a, b), blk("SEL", k), A("G16", lo + k, hi, 16)) for k in range(16)])
             lin(A("N16", a, b), ps("n", a, b), 2048.0)
-            if nks:
-                lin(A("NH", a, b), ps("n", a, b), 0.0)
-            else:
-                act(A("NS", a, b), ps("n", a, b), bias=2048.0)
-            sv = A(VW, lo, hi)
+            sv = A(VW, svo(a) + lo, svo(a) + hi)
             act(sv, IND(VF, A("S16", a, b)))
             tt(A("DD", lo, hi), IND(VF, A("N16", a, b)), sv, OP.subtract)
             key = ps("key", a, b)
@@ -389,56 +380,54 @@ def plan(cfg):
                 it += [(key, zw("ZM1", k), A("DD", lo + k, hi, 16)) for k in range(16)]
                 it += [(key, zw("Z2", k), A("RR", lo + k, hi, 16)) for k in range(16)]
             mm(it)
-        for a, b in cfg["dc"]:
-            first_of_32(ID, C, m == 1, "HC", "QC", "MSKC", "DSC", "dedC", "LOFF", a, b)
+        first_of_32(ID, C, "HC", "QC", "dedC", "LOFF", -1280.0)
         for a, b in cfg["lg"]:
-            nok, one = A("NOK", a, b), A("ONES", 0, b - a)
-            if nks:
-                act(nok, ps("key", a, b), AF.Sign, bias=col(cTHR))
-            else:
-                ts(nok, ps("key", a, b), col(cTHR), OP.is_gt)
+            nok = A("NOK", a, b)
+            act(nok, ps("key", a, b), AF.Sign, bias=col(cTHR))
             mm([(ps("val", a, b), A("SU"), nok)])
             act(A("IND", a, b), ps("val", a, b), AF.Sign, bias=col(c16K), scale=-1.0, other=(col(c16K), OP.is_lt, None, None))
             an = segs(m, "N", 1, a, b)
             ao = [(a, b, A("AO", a, b))] if last else segs(m, "O", 1, a, b)
             mm([(ps("xA", a, b), A("B32"), nok)] + [(ps("xA", x0, x1), ID, x) for x0, x1, x in an])
             for x0, x1, x in ao:
-                act(x, ps("xA", x0, x1), bias=0.421875 if nks else 0.171875)
-            mm([(ps("rr", a, b), A("I16"), nok), (ps("rr", a, b), A("MBO"), A("IND", a, b))])
+                act(x, ps("xA", x0, x1), bias=0.421875)
+            mm([(ps("rr", a, b), A("MI8"), nok), (ps("rr", a, b), A("BO"), A("IND", a, b))])
             act(A("RL", a, b), ps("rr", a, b), AF.Relu, bias=col(cK1))
             y = ps("Y23", a, b)
-            nh, sh = A("NH", a, b), A("SH", a, b)
-            if cfg["t2s"]:
-                mm([(y, A("MI1"), A("T16K", a, b)), (y, A("MI16"), nok), (y, A("MBC"), one), (y, ID, nh)] +
-                   [(ps("Y23", x0, x1), A("I8192"), x) for x0, x1, x in an] + [(ps("Y23", x0, x1), A("IM8192"), x) for x0, x1, x in ao] +
-                   [(y, ID, A("RL", a, b))])
-                act(A("T2", a, b), y, AF.Relu)
-                mm([(y, ID, nh), (y, A("MID32"), A("T2", a, b))])
-                lin(A("P16", a, b), y, 6144.0 - 16 * a)
-            else:
-                mm([(y, ID, A("T16K", a, b)), (y, A("I16"), nok), (y, A("BC" if nks else "BM128"), one)] +
-                   [(ps("Y23", x0, x1), A("IM8192"), x) for x0, x1, x in an] + [(ps("Y23", x0, x1), A("I8192"), x) for x0, x1, x in ao] +
-                   [(y, A("MI1"), A("RL", a, b))])
-                tt(A("T2", a, b), y, nh if nks else A("NS", a, b), OP.min)
-                lin(A("P16", a, b), A("T2", a, b), (6144.0 if nks else 4096.0) - 16 * a)
+            mm([(y, A("BO"), A("TC", a, b)), (y, A("BO"), A("IND", a, b))] +
+               [(ps("Y23", x0, x1), A("I8192"), x) for x0, x1, x in an] + [(ps("Y23", x0, x1), A("IM8192"), x) for x0, x1, x in ao] +
+               [(y, A("MI1"), A("RL", a, b))])
+            tt(A("P16", a, b), y, A("N16", a, b), OP.max)
+        for a, b in cfg["mr"]:
+            nok, nh, sh = A("NOK", a, b), A("NH", a, b), A("SH", a, b)
+            lin(nh, A("N16", a, b), -2048.0)
             if les:
                 mm([(ps("dn", a, b), ID, sh), (ps("dn", a, b), A("MI1"), nh), (ps("dn", a, b), A("IM8192"), nok)])
                 act(A("M0", a, b), ps("dn", a, b), AF.Relu)
                 mm([(ps("m1", a, b), ID, nh), (ps("m1", a, b), A("ID32"), A("M0", a, b)), (ps("m1", a, b), A("I4096"), nok)])
                 act(A("M1", a, b), ps("m1", a, b), bias=les - 2048.0)
-            elif nks:
+            else:
                 mm([(ps("dn", a, b), ID, sh), (ps("dn", a, b), A("IM4096"), nok)])
                 act(A("M0", a, b), ps("dn", a, b), AF.Relu, bias=-2048.0)
                 mm([(ps("m1", a, b), ID, nh), (ps("m1", a, b), A("I4096"), nok)])
                 act(A("M1", a, b), ps("m1", a, b), AF.Relu, bias=-2048.0)
-            else:
-                mm([(ps("dn", a, b), A("ID32"), A("NS", a, b)), (ps("dn", a, b), A("MID32"), A("SF", a, b))])
-                tt(A("M1", a, b), ps("dn", a, b), nok, OP.mult)
+        for a, b in cfg["am"]:
+            absd = [q in cfg["abss"] for q, (x0, x1) in enumerate(cfg["p1"]) if x0 == a][0]
             if not last:
-                tr(A("KTT", a, b), ps("key", a, b))
-                scan(A("KSC", a, b), A("RSK", 0, b - a), A("KTT", a, b), OP.max)
-                tr(A("MX", a, b), A("KSC", a, b))
-                mm([(ps("D", a, b), A("DM"), A("MX", a, b))])
+                if cfg["tl"]:
+                    y = ps("oh", a, b)
+                    it = [(y, A("ONES"), A("K0"))]
+                    for src, w in (("RR", "GZ1"),) if absd else (("DD", "GZM"), ("RR", "GZ2")):
+                        it += [(ps("oh", a + k, b, 16), A(src, 16 * a + k, 16 * b, 16), A(w)) for k in range(16)]
+                    mm(it)
+                    scan(A("KH1", a, b), A("RSK", 0, 128), y, OP.max, OP.min)
+                    scan(A("KH2", a, b, -1), A("RSK", 0, 128), A("KH1", a, b, -1), OP.max, OP.min)
+                    mm([(ps("D", a, b), A("KH2", a, b), ID), (ps("D", a, b), A("KH1", a, b), A("MI1"))])
+                else:
+                    tr(A("KTT", a, b), ps("key", a, b))
+                    scan(A("KSC", a, b), A("RSK", 0, b - a), A("KTT", a, b), OP.max, OP.min)
+                    tr(A("MX", a, b), A("KSC", a, b))
+                    mm([(ps("D", a, b), A("DM"), A("MX", a, b))])
                 act(A("IND2", a, b), ps("D", a, b), AF.Relu, bias=1.0, scale=-1.0, other=(0.5, OP.is_lt, None, None))
                 i2, oha, msk = A("IND2", a, b), A("OHA", a, b), A("MSK", a, b)
                 mm([(ps("oh", a, b), A("OH"), i2)])
@@ -452,15 +441,14 @@ def plan(cfg):
             if les:
                 act(dst, A("M1", a, a + 32), AF.Silu)
             else:
-                tt(dst, A("M0" if nks else "SF", a, a + 32), A("M1", a, a + 32), OP.add)
+                tt(dst, A("M0", a, a + 32), A("M1", a, a + 32), OP.add)
         if last:
             yl = A("YL") if les else LEW
             if les:
                 ts(yl, LEW, 12582912.0 - les, OP.add, -12582912.0, OP.add)
             dma(("out", "yl", 0, 512), yl, 128 * 2048, [yl], [])
         else:
-            for a, b in cfg["da"]:
-                first_of_32(A("BO"), "OHA", False, "HA", "QA", "MSK", "DSA", "dedA", "AOFF", a, b)
+            first_of_32(A("BO"), "OHA", "HA", "QA", "dedA", "AOFF", 0.0)
             for a, b in cfg["da"]:
                 src = IND(A("AD"), A("AOFF", a // 16, b // 16))
                 if not cfg["q1s"]:
@@ -474,8 +462,8 @@ def plan(cfg):
         two = set()
         for q, (a, b) in enumerate(cfg["p3"]):
             lo, hi = 16 * a, 16 * b
-            la = [x0 for x0, x1 in cfg["lg"] if x0 <= a < x1][0]
-            src = IND(A(VW, 16 * la, 8192), A("P16", a, b))
+            lb = [x1 for x0, x1 in cfg["lg"] if x0 <= a < x1][0]
+            src = IND(A(VW, 0, svo(a) + 16 * lb), A("P16", a, b))
             if q in cfg["vv"]:
                 two |= set(range(a, b))
                 tt(A("G16", lo, hi), src, A("OFS", 0, hi - lo), OP.add)
@@ -488,8 +476,7 @@ def plan(cfg):
             scan(A("LO", lo, hi), A("RSP", 0, hi - lo), A("VV", lo, hi), OP.min, OP.max)
         for a, b in cfg["tail"]:
             ja, jb, lo, hi = a // 16, b // 16, 16 * a, 16 * b
-            pk = [] if last else segs(m, "O", 0, a, b)
-            zo = pk.pop()[2] if len(pk) == 1 else A("ZO", a, b)
+            zo = A("ZO", a, b) if last else segs(m, "O", 0, a, b)[0][2]
             x = ps("Xz", a, b)
             if a in two:
                 it = [(x, A("BO"), A("OF2", a, b)), (x, A("MIH"), A("HI2", lo // 2 + 7, hi // 2, 8)), (x, A("MIH"), A("LO2", lo // 2, hi // 2, 8))]
@@ -504,7 +491,7 @@ def plan(cfg):
             mm([(w, ID, A("T16M", a, b)), (w, A("W16"), zo), (w, ID, A("FL", a, b))])
             wrap("WS", w, a, b)
             lin(A("WW16", ja, jb), A("WS", a + 15, b, 16), 24576.0 - lo)
-            yv = A(VN, 4096 + lo, 4096 + hi)
+            yv = A(VN, lo, hi)
             cp(IND(yv, A("WW16", ja, jb)), zo)
             if last:
                 dma(("out", "yv", lo, hi), yv, 4096 * (b - a), [yv], [])
@@ -513,12 +500,10 @@ def plan(cfg):
             y = ps("q2", a, b)
             mm([(y, ID, A("T16", a, b)), (y, A("OH8"), A("IND2", a, b)), (y, A("W16"), zo), (y, ID, A("FL", a, b))])
             act(A("Q2", a, b), y, AF.Relu, bias=24576.0 - 8192)
-            for x0, x1, x in pk:
-                act(x, A("ZR", x0, x1), AF.Abs, bias=-12582912.0)
             for bb in range(3, -1, -1):
                 if a <= 64 * bb < b and (bb + m) % 4:
                     src, dst = A("PO%d" % m, 128 * bb, 128 * bb + 128), A("PN%d" % (m + 1), 128 * bb, 128 * bb + 128)
-                    add("g", "send", (m, bb, src, dst), [src], [dst], cfg["si"], cfg["sl"])
+                    add("g", "send", (m, bb, src, dst), [src], [dst], cfg["si"] + (cfg["s1"] if (m, bb) == (1, 2) else 0.0), cfg["sl"])
             for x0 in range(b - 32, a - 1, -32):
                 tt(IND(A("AD"), A("AOFF", x0 // 16, x0 // 16 + 2)), A("Q1", x0, x0 + 32), A("Q2", x0, x0 + 32), OP.add)
     while True:
@@ -574,19 +559,24 @@ def schedule(ops, cfg):
     pre = [cost[i] + after[i] if xf[i] else 0.0 for i in range(n)]
     post = [0.0 if xf[i] else after[i] for i in range(n)]
 
-    def place(seq, nxt, pre, post):
-        S = [[] for _ in range(5)]; F = [[] for _ in range(5)]
-        BS = [[] for _ in range(8)]; BF = [[] for _ in range(8)]; BE = [[] for _ in range(8)]
-        start = [0.0] * n; rdy = [0.0] * n; end = 0.0
+    nothing = ([[]] * 13, [0.0] * n, [0.0] * n, [0.0] * 5, [0.0] * n)
+
+    def place(seq, nxt, pre, post, fixed=nothing):
+        S = [[y[0] for y in x] for x in fixed[0]]; F = [[y[1] for y in x] for x in fixed[0]]
+        BS, BF, BE = S[5:], F[5:], [[y[2] for y in x] for x in fixed[0][5:]]
+        rdy = list(fixed[1]); out = fixed[2]; start = list(fixed[4]); end = 0.0
         for i in seq:
             e = en[i]; c = dur[i]; t = rdy[i] + pre[i]
-            s = S[e]; f = F[e]; bs = bk[i]; m = len(s)
+            s = S[e]; f = F[e]; bs = bk[i]; m = x = len(s)
+            while x and f[x - 1] > t:
+                x -= 1
             while True:
-                x = m
-                while x and f[x - 1] > t:
-                    x -= 1
                 while x < m and s[x] < t + c:
-                    t = f[x]; x += 1
+                    if f[x] > t:
+                        t = f[x]
+                    x += 1
+                if not bs:
+                    break
                 t0 = t
                 for b in bs:
                     ss = BS[b]; ff = BF[b]; ee = BE[b]
@@ -607,87 +597,133 @@ def schedule(ops, cfg):
                 ss.insert(y, t); BF[b].insert(y, t + c); BE[b].insert(y, e)
             start[i] = t
             z = t + c + post[i]
-            if z > end:
-                end = z
+            if z + out[i] > end:
+                end = z + out[i]
             z += lat
             for j in nxt[i]:
                 if z > rdy[j]:
                     rdy[j] = z
-        return end, start
+        return max([end] + [F[e][-1] + fixed[3][e] for e in range(5) if F[e]]), start
 
     def forward(key):
-        for i in range(n):
-            for j in deps[i]:
-                if key[j] >= key[i]:
-                    key[i] = key[j] + 0.01
-        return place(sorted(range(n), key=lambda i: key[i]), succ, pre, post)
+        return place(np.argsort(key, kind="stable").tolist(), succ, pre, post)
 
     def both(key):
         r = forward(key)
-        s2 = place(sorted(range(n), key=lambda i: -r[1][i] - dur[i]), deps, post, pre)[1]
-        r3 = place(sorted(range(n), key=lambda i: -s2[i] - dur[i]), succ, pre, post)
+        s2 = place(np.argsort(-np.add(r[1], dur), kind="stable").tolist(), deps, post, pre)[1]
+        r3 = forward(-np.add(s2, dur))
         return r3 if r3[0] <= r[0] else r
 
     lv = [0.0] * n
     for i in range(n - 1, -1, -1):
         lv[i] = pre[i] + dur[i] + post[i] + max([lv[j] + lat for j in succ[i]] + [0.0])
     rng = np.random.RandomState(cfg["seed"])
-    cur = best = both([-x for x in lv])
-    free = [i for i in range(n) if "m" in ops[i]]
-    mode = [0] * n; top = list(mode)
-    for it in range(cfg["iters"]):
-        key = list(cur[1]); undo = []
-        if rng.uniform() < cfg["flip"]:
-            for _ in range(1 + rng.randint(2)):
-                i = free[rng.randint(len(free))]; ms_ = ops[i]["m"]
-                undo.append((i, mode[i]))
-                mode[i] = (mode[i] + 1 + rng.randint(len(ms_) - 1)) % len(ms_)
-                en[i] = E[ms_[mode[i]][0]]; dur[i] = ms_[mode[i]][3]
-        elif rng.uniform() < 0.3:
-            a = rng.uniform(-3000, cur[0]); sp = rng.uniform(1000, 10000)
-            nz = (rng.normal(0, rng.choice([200.0, 600.0, 1500.0]), n) * (rng.uniform(size=n) < 0.4)).tolist()
-            for i in range(n):
-                if a <= key[i] < a + sp:
-                    key[i] += nz[i]
-        else:
-            for _ in range(1 + rng.randint(2)):
-                i = rng.randint(n); dl = rng.exponential(1500.0); st = [i]
-                if rng.uniform() < 0.5:
-                    key[i] -= dl
-                    while st:
-                        x = st.pop()
-                        for j in deps[x]:
-                            v = key[x] - dur[j] - pre[x] - post[j] - lat
-                            if key[j] > v:
-                                key[j] = v; st.append(j)
-                else:
-                    key[i] += dl
-                    while st:
-                        x = st.pop()
-                        for j in succ[x]:
-                            v = key[x] + dur[x] + pre[j] + post[x] + lat
-                            if key[j] < v:
-                                key[j] = v; st.append(j)
-        r = both(key) if rng.uniform() < 0.3 else forward(key)
-        if r[0] <= cur[0] + cfg["temp"] * (1.0 - it / cfg["iters"]) * rng.exponential():
-            cur = r
-            if r[0] < best[0]:
-                best = r; top = list(mode)
-        else:
-            for i, x in reversed(undo):
-                mode[i] = x; en[i] = E[ops[i]["m"][x][0]]; dur[i] = ops[i]["m"][x][3]
-    for i in free:
-        o = ops[i]
-        o["e"], o["k"], o["a"], o["c"] = o["m"][top[i]]
-        en[i] = E[o["e"]]; cost[i] = o["c"]; o["mode"] = top[i]
+    mode = [0] * n
+
+    def setmode(i, x):
+        mode[i] = x; en[i] = E[ops[i]["m"][x][0]]; dur[i] = ops[i]["m"][x][3]
+
+    def anneal(W, cur, value, iters, temp):
+        free = [i for i in W if "m" in ops[i]]
+        inside = [False] * n
+        for i in W:
+            inside[i] = True
+        up = [[j for j in deps[i] if inside[j]] for i in range(n)]; down = [[j for j in succ[i] if inside[j]] for i in range(n)]
+        best = cur; top = list(mode); t0, t1 = min(cur[1][i] for i in W), max(cur[1][i] for i in W)
+        for it in range(iters):
+            key = list(cur[1]); undo = []
+            if rng.uniform() < cfg["flip"]:
+                for _ in range(1 + rng.randint(2)):
+                    i = free[rng.randint(len(free))]; k = len(ops[i]["m"])
+                    undo.append((i, mode[i]))
+                    setmode(i, (mode[i] + 1 + rng.randint(k - 1)) % k)
+            elif rng.uniform() < 0.3:
+                a = rng.uniform(t0 - 3000, t1); sp = rng.uniform(1000, 10000)
+                nz = (rng.normal(0, rng.choice([200.0, 600.0, 1500.0]), n) * (rng.uniform(size=n) < 0.4)).tolist()
+                for i in W:
+                    if a <= key[i] < a + sp:
+                        key[i] += nz[i]
+                    for j in up[i]:
+                        if key[j] >= key[i]:
+                            key[i] = key[j] + 0.01
+            else:
+                for _ in range(1 + rng.randint(2)):
+                    i = W[rng.randint(len(W))]; dl = rng.exponential(1500.0); st = [i]
+                    if rng.uniform() < 0.5:
+                        key[i] -= dl
+                        while st:
+                            x = st.pop()
+                            for j in up[x]:
+                                v = key[x] - dur[j] - pre[x] - post[j] - lat
+                                if key[j] > v:
+                                    key[j] = v; st.append(j)
+                    else:
+                        key[i] += dl
+                        while st:
+                            x = st.pop()
+                            for j in down[x]:
+                                v = key[x] + dur[x] + pre[j] + post[x] + lat
+                                if key[j] < v:
+                                    key[j] = v; st.append(j)
+            r = value(key)
+            if r[0] <= cur[0] + temp * (1.0 - it / iters) * rng.exponential():
+                cur = r
+                if r[0] < best[0]:
+                    best = r; top = list(mode)
+            else:
+                for i, x in reversed(undo):
+                    setmode(i, x)
+        for i in free:
+            setmode(i, top[i])
+        return best
+
+    best = anneal(list(range(n)), both([-x for x in lv]), lambda key: both(key) if rng.uniform() < cfg["both"] else forward(key),
+                  cfg["iters"], cfg["temp"])
+    for sweep in range(cfg["sweeps"]):
+        t0 = -rng.uniform(0, cfg["span"] / 2)
+        while t0 < best[0] - 5000:
+            st = best[1]; t1 = t0 + cfg["span"]
+            back = place(np.argsort(-np.add(st, dur), kind="stable").tolist(), deps, post, pre)[1]
+            W = [i for i in range(n) if t0 <= st[i] - pre[i] < t1]
+            rdy = [max(t0 - 2000, 0.0)] * n; out = [0.0] * n; last = [0.0] * 5
+            S = [[] for _ in range(13)]
+            for i in sorted(range(n), key=lambda i: st[i]):
+                if st[i] - pre[i] >= t1:
+                    last[en[i]] = max(last[en[i]], back[i] + dur[i])
+                    for j in deps[i]:
+                        out[j] = max(out[j], lat + pre[i] + back[i] + dur[i])
+                elif st[i] - pre[i] < t0:
+                    for j in succ[i]:
+                        rdy[j] = max(rdy[j], st[i] + dur[i] + post[i] + lat)
+                    if st[i] + dur[i] > t0 - 2500:
+                        for x in [en[i]] + [5 + b for b in bk[i]]:
+                            S[x].append((st[i], st[i] + dur[i], en[i]))
+            fixed = (S, rdy, out, last, st)
+            old = list(mode)
+
+            def value(key):
+                return place(sorted(W, key=lambda i: key[i]), succ, pre, post, fixed)
+            r = anneal(W, value(st), value, cfg["its"], cfg["temp"] * (1.0 - sweep / cfg["sweeps"]))
+            r = both([r[1][i] if st[i] - pre[i] < t1 else r[0] - back[i] - dur[i] for i in range(n)])
+            if r[0] <= best[0]:
+                best = r
+            else:
+                for i in W:
+                    if mode[i] != old[i]:
+                        setmode(i, old[i])
+            t0 += cfg["span"] / 2
+    for i in range(n):
+        if "m" in ops[i]:
+            cost[i] = dur[i]
     key = [best[1][i] - pre[i] for i in range(n)]
     order = sorted(range(n), key=lambda i: key[i])
-    sets = [(cost, lat)]
+    sets = [(cost, lat, after, xf)]; plans = [ops]
     for alt in cfg["alts"]:
-        c2 = dict(cfg); c2.update(alt)
-        sets.append(([o["m"][top[i]][3] if "m" in o else o["c"] for i, o in enumerate(plan(c2))], c2["lat"]))
+        c2 = dict(cfg); c2.update(alt); p2 = plan(c2); plans.append(p2)
+        sets.append(([o["m"][mode[i]][3] if "m" in o else o["c"] for i, o in enumerate(p2)], c2["lat"], [o["l"] for o in p2], [o["x"] for o in p2]))
 
-    def timed(order, c2, l2, old=None, lo=0):
+    def timed(order, costs, old=None, lo=0):
+        c2, l2, after, xf = costs
         if old is None:
             x0 = 0; snaps = []
             free = [0.0] * 5; prev = [-1] * 5; fin = [0.0] * n; why = [-1] * n; xfree = 0.0
@@ -720,11 +756,11 @@ def schedule(ops, cfg):
         return end - l2, fin, why, snaps
 
     def total(order, olds=None, lo=0):
-        rs = [timed(order, c2, l2, olds[x] if olds else None, lo) for x, (c2, l2) in enumerate(sets)]
+        rs = [timed(order, costs, olds[x] if olds else None, lo) for x, costs in enumerate(sets)]
         return sum(r[0] for r in rs), rs
 
     dset = [set(d) for d in deps]
-    cur, rs = total(order); keep = (cur, list(order))
+    cur, rs = total(order); keep = (cur, list(order), list(mode))
     for it in range(cfg["moves"]):
         pos = [0] * n
         for x, i in enumerate(order):
@@ -739,6 +775,21 @@ def schedule(ops, cfg):
         j, i = pairs[rng.randint(len(pairs))]
         u = rng.uniform()
         new = list(order)
+        if u > 0.8 and "m" in ops[i]:
+            was = mode[i]; to = (was + 1 + rng.randint(len(ops[i]["m"]) - 1)) % len(ops[i]["m"])
+            for x in (to, was):
+                setmode(i, x)
+                for c2, p2 in zip(sets, plans):
+                    c2[0][i] = p2[i]["m"][x][3]
+                if x == was:
+                    break
+                s, r2 = total(order, rs, pos[i])
+                if s <= cur:
+                    cur, rs = s, r2
+                    if s < keep[0]:
+                        keep = (s, list(order), list(mode))
+                    break
+            continue
         if u < 0.45:
             lo = max(0, pos[j] - (rng.randint(30) if rng.uniform() < 0.4 else 0)); grp = {i}
             for x in range(pos[i] - 1, lo - 1, -1):
@@ -766,9 +817,17 @@ def schedule(ops, cfg):
         if s <= cur + cfg["temp2"] * (1.0 - it / cfg["moves"]) * rng.exponential():
             order, cur, rs = new, s, r2
             if s < keep[0]:
-                keep = (s, list(order))
+                keep = (s, list(order), list(mode))
     order = keep[1]
-    end, fin = timed(order, cost, lat)[:2]
+    for i in range(n):
+        o = ops[i]
+        if "m" in o:
+            setmode(i, keep[2][i])
+            o["e"], o["k"], o["a"], o["c"] = o["m"][mode[i]]
+            for c2, p2 in zip(sets, plans):
+                c2[0][i] = p2[i]["m"][mode[i]][3]
+    end, fin = timed(order, sets[0])[:2]
+    cfg["ends"] = [int(timed(order, x)[0]) for x in sets]
     lastb = {}
     for i in order:
         o = ops[i]

import numpy as np
from concourse.mybir import AluOpType as OP, ActivationFunctionType as AF

F32, BF, F16, I32, U16 = "float32", "bfloat16", "float16", "int32", "uint16"
STEPS = 4
Q4 = ((192, 256), (128, 192), (64, 128), (0, 64))
H2 = ((128, 256), (0, 128))
T3 = ((128, 256), (64, 128), (0, 64))
CFG = {
    "si": 1000.0, "sl": 3600.0,
    "p1": Q4,
    "adv": (0,),
    "sv": (),
    "abss": (),
    "p3": Q4,
    "vv": (),
    "tail": Q4,
    "lg": T3, "ad": T3, "dc": ((0, 256),), "da": ((0, 256),),
    "mr": H2, "am": H2, "q1s": True, "cvt": True, "les": False, "tl": False, "s1": 1000.0, "selg": 8,
    "s": ("NH",), "both": 0.2, "flip": 0.3,
    1: {"adv": (0, 1, 2, 3), "p1": ((224, 256), (192, 224)) + Q4[1:]},
    4: {"tail": T3[:2] + ((32, 64), (0, 32)), "p3": Q4[:3] + ((32, 64), (0, 32))},
    "seed": 7, "iters": 4000, "sweeps": 5, "its": 2500, "span": 24000.0, "temp": 120.0, "moves": 36000, "temp2": 60.0,
    "alts": ({"lat": 140.0, "po": 100.0, "pe": 0.5, "sl": 4500.0, "bw": 200.0},
             {"g": 1.3, "sc": 2.6, "bw": 350.0, "dl": 1500.0}, {"g": 2.2, "sc": 5.8}),
    "g": 1.7, "sc": 4.2, "f": 1.1, "lat": 110.0, "pe": 0.42, "bw": 250.0, "dl": 2000.0, "vo": 55.0, "so": 72.0, "mn": 0, "po": 60.0,
}

_S = {
    "VW1": (8192, BF), "VW0": (8192, BF), "ADi": (2048, I32), "AD": (2080, F32),
    "LEi": (512, I32), "LE": (544, F32), "YL": (512, F32),
    "CBi": (16, I32), "KAi": (8, I32), "THi": (8, I32), "COLS": (64, F32), "CI": (16, I32), "CBF": (16, F32), "CBL": (16, U16),
    "IO": (144, BF), "MI": (256, BF), "MSK": (256, BF), "MK1": (256, BF), "CE": (256, F16), "HD": (256, BF),
    "ID32": (128, F32), "MID32": (128, F32), "DM": (128, F32), "IC16": (128, F16), "DF": (144, BF), "IDW": (144, BF),
    "Z1": (144, BF), "Z2": (144, BF), "ZM1": (144, BF), "EQ": (16, F32),
    "SEL": (2048, BF), "TC": (256, BF), "QH": (256, F16), "I69": (128, F16), "KH1": (256, F16), "KH2": (256, F16),
    "GZ1": (8, BF), "GZM": (8, BF), "GZ2": (8, BF), "SH": (256, F16), "NH": (256, F16),
    "T16": (256, BF), "T16M": (256, BF), "T16K": (256, F16), "ZM8": (144, BF),
    "RSN": (1024, BF), "RSP": (1024, BF), "RSK": (256, BF), "OFS": (1024, BF), "OFI": (256, BF), "OF2": (256, BF),
    "XI": (256, I32), "A32": (256, I32), "A16": (256, U16), "CW16": (16, U16), "HC": (256, F16),
    "S16": (256, U16), "SF": (256, F32), "G16": (4096, F16), "N16": (256, U16), "NS": (256, F32),
    "DD": (4096, BF), "RR": (4096, BF), "NOK": (256, BF), "IND": (256, BF), "RL": (256, BF),
    "T2": (256, F32), "P16": (256, U16), "M0": (256, F32), "M1": (256, F32), "VV": (4096, BF), "HI": (4096, BF), "LO": (4096, BF),
    "HI2": (2048, F16), "LO2": (2048, F16),
    "KTT": (256, F32), "KSC": (256, F32), "MX": (256, F32), "IND2": (256, BF), "OHS": (256, F32), "OHA": (256, F16),
    "Q0": (256, F32), "Q1": (256, F32), "Q2": (256, F32), "AO": (256, BF),
    "HA": (256, F16), "QC": (512, BF), "QA": (512, BF), "DSC": (256, F32), "DSA": (256, F32),
    "LOFF": (16, U16), "AOFF": (16, U16), "ZR": (256, F32), "QB": (256, BF), "FL": (256, F16), "WS": (256, F32),
    "WW16": (16, U16), "TI": (256, I32), "C32": (256, I32),
}
_S.update({"ZN1": (256, BF), "AN1": (256, BF), "ZO": (256, BF), "UN": (256, F16), "CN0": (256, F16), "CN1": (256, F16)})
for _m in range(1, STEPS):
    _S["PO%d" % _m] = (512, BF)
    _S["PN%d" % (_m + 1)] = (512, BF)
_AL = {n: 128 * i for i, n in enumerate(
    "BO WT W16 ONES SU OHM OH OH8 MOH8 MI8 MI1 MIH IQ IM32 IM4096 KH KL M256 K0 IM512 BM8192 B32 GI TMP I4096 I8192 IM8192".split())}
_S["CM"] = (128 * len(_AL), BF)
SCRATCH = {k: ("sbuf", [128, w], d) for k, (w, d) in _S.items()}
for _b in range(8):
    SCRATCH["P%d" % _b] = ("psum", [128, 512], F32)
SEMAPHORES = ["cv", "cs", "cp", "cg", "sent"] + ["d%d" % i for i in range(48)] + \
             ["arr%d_%d" % (m, b) for m in range(1, STEPS) for b in range(4)]
SEM = {"v": "cv", "s": "cs", "p": "cp", "g": "cg"}
TWO = (BF, F16, U16)
(cK, cG, cG15, cW, cKL, cKH, cCP, cTHR, c16K, cK1, cE15, cPAR, cEV, cP2048, cE2048, cQ2, cP2, cPD,
 cW16, cT, cK16, cKM, cMPAR, cMEV, cP32) = range(25)


def A(n, lo=0, hi=None, st=1):
    if n == "ID":
        return ("IDW", 1 + lo, 1 + (128 if hi is None else hi), st)
    if n in _AL:
        return ("CM", _AL[n] + lo, _AL[n] + (128 if hi is None else hi), st)
    return (n, lo, _S[n][0] if hi is None else hi, st)


def cols(a):
    return slice(a[1], a[2], a[3]) if a[3] > 0 else slice(a[2] - 1, a[1] - 1 if a[1] else None, a[3])


def col(i):
    return ("COLS", i, i + 1, 1)


def IND(win, off):
    return ("*", win, off)


def width(a):
    if a[0] == "*":
        return 16 * (a[2][2] - a[2][1])
    return len(range(a[1], a[2], abs(a[3])))


def psum(a):
    return len(a[0]) == 2 and a[0][0] == "P" and a[0][1].isdigit()


def dty(a):
    return F32 if psum(a) else _S[a[0]][1]


SLOT = {"X": (2, 1), "q2": (2, 2), "cw": (2, 3), "colw": (2, 3), "val": (4, 0), "rr": (4, 0), "U16": (4, 0), "Y23": (4, 1), "ww": (4, 1),
        "oh2": (4, 2), "m1": (4, 2), "xA": (4, 3), "Xz": (4, 3), "dn": (6, 0), "D": (6, 1), "oh": (6, 2), "U": (6, 3), "uc": (6, 3)}


def ps(role, a, b, st=1):
    h = a // 128
    if role == "n":
        q = a // 64
        return ("P%d" % (q & 1), (q >> 1) * 64 + a % 64, (q >> 1) * 64 + a % 64 + b - a, st)
    if role == "key":
        return ("P%d" % (2 + h), a % 128, a % 128 + b - a, st)
    if role == "dedA":
        return ("P0", 256 + a, 256 + b, st)
    if role == "dedC":
        return ("P1", 256 + a, 256 + b, st)
    if role == "rel":
        return ("P%d" % (4 + (a // 512) % 2), 0, b - a, st)
    if role == "con":
        return ("P7", a, b, st)
    o = SLOT[role][1] * 128 + a % 128
    return ("P%d" % (SLOT[role][0] + h), o, o + b - a, st)


def plan(cfg):
    ops = []
    cyc = 0.83 * cfg["f"]
    cfg0 = cfg
    les = 32.0 if cfg["les"] else 0.0

    def add(eng, kind, args, rd, wr, cost, lat=0.0, xfer=0.0):
        R, W = [], []
        for x in rd:
            if isinstance(x, tuple):
                R += [x[1], x[2]] if x[0] == "*" else [x]
        for x in wr:
            if x[0] == "*":
                W.append(x[1]); R.append(x[2])
            else:
                W.append(x)
        ops.append({"e": eng, "k": kind, "a": args, "r": R, "w": W, "c": cost, "l": lat, "x": xfer})

    def vcost(out, ins, tt=False):
        n = width(out)
        if out[0] == "*":
            return 50 + n * cfg["sc"] * 0.83
        if ins[0][0] == "*":
            return 50 + n * cfg["g"] * 0.83
        if tt:
            return cfg["vo"] + max(cfg["mn"], n * (1 if any(psum(x) for x in ins) else 2)) * cyc
        two = all(dty(x) in TWO for x in [out] + ins)
        return cfg["vo"] + max(cfg["mn"], n * (0.5 if two else 1)) * cyc

    def ts(out, i, s1, op0, s2=None, op1=None):
        add("v", "ts", (out, i, s1, s2, op0, op1), [i, s1, s2], [out], vcost(out, [i]))

    def cp(out, i):
        add("v", "cp", (out, i), [i], [out], vcost(out, [i]))

    def tt(out, a, b, op):
        add("v", "tt", (out, a, b, op), [a, b], [out], vcost(out, [a, b], True))

    def ms(out, v):
        add("v", "ms", (out, v), [], [out], vcost(out, [out]))

    def scan(out, d0, d1, op1, op0=OP.add, init=0.0):
        add("v", "scan", (out, d0, d1, op1, op0, init), [d0, d1], [out], vcost(out, [d0, d1]))

    def tr(out, i):
        add("v", "tr", (out, i), [i], [out], vcost(out, [i]))

    def act(out, i, f=AF.Identity, bias=0.0, scale=1.0, other=None, vec=False):
        n = width(out)
        c = 65 + n * cfg["g"] * 0.83 if i[0] == "*" else 65 + n * cfg["sc"] * 0.83 if out[0] == "*" else cfg["so"] + max(cfg["mn"], n) * cyc
        add("s", "act", (out, i, f, bias, scale), [i, bias, scale], [out], c)
        if f == AF.Identity:
            other = (scale, OP.mult, bias, OP.add) if scale != 1.0 else (bias, OP.add, None, None)
        elif f == AF.Relu and scale == 1.0:
            other = (bias, OP.add, 0.0, OP.max)
        if other:
            o = ops[-1]
            o["m"] = [("s", "act", o["a"], c), ("v", "ts", (out, i, other[0], other[2], other[1], other[3]), vcost(out, [i]))]
            if f == AF.Identity and scale == 1.0 and bias == 0.0 and i[0] != "*" and not psum(i) and dty(out) == U16:
                o["m"].append(("g", "asel", (out, i, [[0, n]], OP.is_ge, 0, 0), 170 + 2 * n * cyc))
            if vec:
                o["m"][:2] = o["m"][1::-1]
                o["e"], o["k"], o["a"], o["c"] = o["m"][0]

    def mm(items):
        c = sum(max(64, width(o)) * (4 if dty(r) == F32 else 1) for o, l, r in items) * cfg["pe"] * cfg["f"] + cfg["po"]
        add("p", "mm", items, [x for o, l, r in items for x in (l, r)], [o for o, l, r in items], c)

    def dma(out, i, nbytes, rd, wr):
        add("y", "dma", (out, i), rd, wr, 60.0, cfg["dl"], nbytes / cfg["bw"])

    def iota(out, pat, base, cm):
        add("g", "iota", (out, pat, base, cm), [], [out], 130 + 2 * width(out) * cyc)

    def asel(out, i, pat, op, base, cm):
        add("g", "asel", (out, i, pat, op, base, cm), [i], [out], 170 + 2 * width(out) * cyc)

    def lin(out, i, plus, mul=1.0):
        act(out, i, bias=plus, scale=mul, vec=out[0].rstrip("01") not in cfg["s"])

    def load(name, src, lo=0, hi=None):
        o = A(name, lo, hi)
        dma(o, ("in", src, lo, o[2]), 128 * width(o) * (2 if dty(o) in TWO else 4), [], [o])

    def blk(n, k):
        return A(n, 128 * k, 128 * k + 128)

    def zw(n, k):
        return A(n, 15 - k, 143 - k)

    load("ZN1", "z0"); load("KAi", "ka", 0, 1); load("CBi", "cb"); load("THi", "th", 0, 1)
    for x in (("ADi", "ad", 0, 1024), ("ADi", "ad", 1024, 2048), ("LEi", "le", 0, 512), ("VW1", "vf", 0, 2048), ("VW1", "vf", 2048, 4096)):
        load(*x)
    iota(A("CI", 0, 1), [[0, 1]], 0, 1)
    iota(A("GI"), [[16, 8], [0, 16]], 0, 0); iota(A("DF"), [[1, 144]], -1, -1); iota(A("MI"), [[0, 16], [1, 16]], 0, 0)
    iota(A("IO"), [[1, 144]], 0, 0); iota(A("T16"), [[16, 256]], 0, 0)
    iota(A("RSN"), [[0, 64], [256, 16]], 0, 0); iota(A("RSP"), [[0, 64], [-256, 16]], 256, 0)
    iota(A("OFS"), [[0, 4], [256, 16], [0, 16]], -2048, 0); iota(A("OFI"), [[0, 16], [32, 16]], -256, 0)
    ci = lambda i: A("CI", i, i + 1)
    ID = A("ID")
    nsum = [0]

    def aff(c, src, mul, plus):
        act(col(c), col(src), bias=plus, scale=mul)

    def msum(out, x, y):
        p = ps("con", 128 * (nsum[0] % 3), 128 * (nsum[0] % 3) + 128); nsum[0] += 1
        mm([(p, ID, x), (p, ID, y)]); act(out, p)

    ts(ci(1), ci(0), 15, OP.bitwise_and); cp(col(cK), ci(1)); tt(col(cG), ci(0), ci(1), OP.subtract)
    ts(ci(4), ci(0), 1, OP.bitwise_and); cp(col(cPAR), ci(4))
    aff(cG15, cG, 1.0, 15.0); aff(cW, cK, 14.0, 1.0); aff(c16K, cK, -1.0, 16.0); aff(cK1, cK, -1.0, -9.0)
    aff(cEV, cPAR, -1.0, 1.0); aff(cP32, cPAR, 1.0 / 32, 0.0)
    act(col(cE15), col(cK), AF.Relu, bias=-14.0)
    aff(cT, cE15, 1.0, -1.0); aff(cK16, cK, 1.0, 16.0)
    ts(ci(2), A("KAi", 0, 1), 1184.0, OP.add); ts(ci(3), ci(2), 31, OP.bitwise_and); cp(col(cKL), ci(3))
    tt(col(cKH), ci(2), ci(3), OP.subtract); aff(cCP, cKL, 2048.0, 40960.0)
    act(col(cTHR), A("THi", 0, 1), bias=4095.5, scale=-1.0)
    ts(ci(5), ci(1), 14.0, OP.mult, 9.0, OP.add); ts(ci(6), ci(5), 15, OP.bitwise_and); ts(col(cW16), ci(6), -8.0, OP.add)
    ms(A("AN1"), 128.0)
    ts(A("IDW"), A("DF"), 0.0, OP.is_equal); ts(A("BO"), A("GI"), col(cG), OP.is_equal)
    ts(A("IC16"), ID, 19616.0, OP.mult); ts(A("Z1"), A("IO"), col(cG15), OP.is_equal)
    iota(A("ONES"), [[0, 128]], 1, 0); iota(A("M256"), [[0, 128]], -1536, 0)
    for n, v in (("MI8", -8.0), ("I4096", 4096.0), ("I8192", 8192.0), ("IM8192", -8192.0),
                 ("MI1", -1.0), ("MIH", -0.5), ("IQ", 0.25), ("IM32", -32.0), ("IM4096", -4096.0),
                 ("KH", col(cKH)), ("KL", col(cKL)), ("ID32", 1.0), ("MID32", -1.0)):
        act(A(n), ID, scale=v)
    for n, v in (("WT", col(cW)), ("W16", col(cW16)), ("BM8192", -8192.0),
                 ("B32", 1.0 / 64), ("TMP", col(cE15))):
        act(A(n), A("BO"), scale=v)
    act(A("Z2"), A("Z1"), scale=2.0); act(A("ZM1"), A("Z1"), scale=-1.0)
    msum(A("DM"), A("TMP"), A("MI1"))
    act(A("OHM"), A("IDW", 0, 128), scale=col(cT)); msum(A("OH"), ID, A("OHM"))
    act(A("OH8"), A("OH"), scale=8192.0); act(A("MOH8"), A("OH"), scale=-8192.0)
    asel(A("SU"), A("BO"), [[-1, 128]], OP.is_ge, 0, 1)
    ts(A("MSK"), A("MI"), col(cK), OP.not_equal, -4194304.0, OP.mult)
    ts(A("MK1"), A("MI"), col(cK), OP.is_equal)
    ts(A("EQ"), A("MI", 0, 16), col(cK), OP.is_equal)
    act(A("K0"), ID, bias=-2040.0 / 128, scale=0.0)
    for n, v in (("GZ1", 1.0), ("GZM", -1.0), ("GZ2", 2.0)):
        act(A(n), A("BO", 0, 128, 16), scale=v)
    act(A("I69"), ID, scale=1103.0 / 16); act(A("IM512"), ID, scale=-512.0); act(A("ZM8"), A("Z1"), scale=-8192.0)

    def svo(t):
        a, b = [x for x in cfg["lg"] if x[0] <= t < x[1]][0]
        return 4096 + 16 * (256 - b) - 16 * a

    act(col(cKM), A("EQ", 2, 3), scale=-1.0)
    for x, (a, b) in enumerate(cfg["lg"]):
        act(col(30 + x), A("EQ", 1, 2), bias=col(cKM), scale=float(svo(a)))
        act(A("TC", a, b), A("T16", a, b), bias=col(30 + x), scale=A("EQ", 0, 1))
    for k in range(16):
        if k < cfg["selg"]:
            asel(blk("SEL", k), ID, [[0, 8], [1, 16]], OP.is_equal, -k, 0)
        else:
            act(blk("SEL", k), ID, scale=A("EQ", k, k + 1))
    p = ps("con", 0, 256)
    mm([(p, ID, A("T16")), (p, ID, A("MSK"))]); act(A("T16M"), p)
    act(A("HD"), A("MSK"), bias=-2097152.0, scale=-1.0)
    iota(A("RSK"), [[0, 16], [32767, 16]], -30000, 0)
    act(A("OF2"), A("OFI"), bias=col(cP32), scale=col(cEV))
    ms(A("AD", 0, 32), 0.0)
    act(A("LE", 32, 544), A("LEi"), AF.Silu if les else AF.Identity, bias=les)
    ops[-1]["c"] += 1300.0 * cfg["f"] if les else 0.0
    for a in (0, 1024):
        act(A("AD", 32 + a, 1056 + a), A("ADi", a, a + 1024))

    def segs(m, side, part, a, b):
        if side == "N" and m == 1:
            return [(a, b, A("AN1" if part else "ZN1", a, b))]
        out = []
        for bb in range(a // 64, (b + 63) // 64):
            x0, x1 = max(a, 64 * bb), min(b, 64 * bb + 64)
            n = "PO%d" % m if side == "O" else "PN%d" % m if (bb + m - 1) % 4 else "PO%d" % (m - 1)
            o = 128 * (bb // 2) + (64 if part == 0 else 128 * (bb % 2))
            if out and out[-1][2][0] == n and out[-1][2][2] == o + x0:
                out[-1] = (out[-1][0], x1, A(n, out[-1][2][1], o + x1))
            else:
                out.append((x0, x1, A(n, o + x0, o + x1)))
        return out

    cp(A("CBL"), A("IO", 0, 16))
    tt(A("CE"), IND(A("CBi"), A("CBL")), A("MK1"), OP.mult)
    mm([(ps("dedC", 0, 256), A("BO"), A("CE"))])
    lin(A("CN1"), ps("dedC", 0, 256), 1280.0)

    def wrap(out, p, a, b):
        scan(A(out, a, b), A("RSK", 0, b - a), p, OP.max, OP.min)

    def hold(out, p, a, b):
        scan(A(out, a, b), A("HD", 0, b - a), p, OP.max, OP.min, -30000.0)

    def first_of_32(l, r, held, q, r1, off, plus):
        mm([(ps(r1, 0, 256), l, A(r))])
        for x, d in enumerate((1, 17)):
            tt(A(q, 256 * x + d, 256 * x + 256), A(held, 0, 256 - d), ps(r1, d, 256), OP.is_equal)
        p = ps(r1, 0, 16)
        mm([(p, ID, A(held, 15, 256, 16))] + [(p, zw("ZM8", k), A(q, 256 * x + k, 256 * x + 256, 16)) for x in range(2) for k in range(16)])
        for x in range(2):
            ts(A(off, x, 16, 2), ps(r1, x, 16, 2), 32.0 + plus, OP.add, col(cK16 if x else cK), OP.max)

    for q in ("QC", "QA"):
        ms(A(q, 0, 16), 0.0); ms(A(q, 256, 288), 0.0)
    ADW, LEW = A("AD", 32, 2080), A("LE", 32, 544)
    for m in range(1, STEPS + 1):
        last = m == STEPS
        cfg = dict(cfg0); cfg.update(cfg0.get(m, {}))
        U, C = "UN", "CN%d" % (m % 2)
        VW, VN = "VW%d" % (m % 2), "VW%d" % ((m + 1) % 2)
        VF = A(VW, 0, 4096)
        for h in range(2):
            x, y = A(VN, 2048 * h, 2048 * h + 2048), A(VW, 2048 * h, 2048 * h + 2048)
            dma(x, y, 128 * 4096, [y], [x])
        for a, b in cfg["ad"]:
            zs = segs(m, "N", 0, a, b)
            for x0, x1, z in zs:
                mm([(ps("U", x0, x1), A("WT"), z)])
            act(A("QB", a, b), ps("U", a, b), bias=135.5 + 2.0 ** -13, scale=2.0 ** -12)
            mm([(ps("uc", a, b), A("IM4096"), A("QB", a, b))] + [(ps("uc", x0, x1), A("WT"), z) for x0, x1, z in zs])
            lin(A(U, a, b), ps("uc", a, b), 4096.0 * 136 - 2048)
            if m > 1:
                lin(A("QH", a, b), A(U, a, b), 1555.25, 1103.0 / 8192)
                mm([(ps("X", a, b), A("I69"), A(U, a, b)), (ps("X", a, b), A("IM512"), A("QH", a, b))])
                ts(A(C, a, b), ps("X", a, b), 796544.0, OP.add, 1279.53125, OP.add)
            x = ps("X", a, b)
            mm([(x, A("IC16"), A(C, a, b)), (x, A("IC16"), A("M256", 0, b - a)), (x, A("KH"), A(U, a, b)), (x, A("KL"), A(U, a, b))])
            lin(A("XI", a, b), x, col(cCP))
            ts(A("A32", a, b), A("XI", a, b), 5, OP.arith_shift_right, 2047, OP.bitwise_and)
            lin(A("A16", a, b), A("A32", a, b), 0.0)
            ja, jb = a // 16, b // 16
            mm([(ps("cw", a, b), ID, A("MSK", a, b)), (ps("cw", a, b), ID, A(C, a, b))])
            hold("HC", ps("cw", a, b), a, b)
            if m == 1:
                cp(A("CW16", ja, jb), A("CBi", ja, jb))
            else:
                lin(A("CW16", ja, jb), A("HC", a + 15, b, 16), -1280.0)
            act(A("SH", a, b), IND(LEW, A("CW16", ja, jb)), bias=-2048.0 - les)
            lin(A("S16", a, b), A("SH", a, b), 2048.0)
        for q, (a, b) in enumerate(cfg["p1"]):
            lo, hi = 16 * a, 16 * b
            src = IND(A("ADi") if m == 1 else ADW, A("A16", a, b))
            act(A("G16", lo, hi), src, bias=-2048.0, vec=q in cfg["adv"])
            mm([(ps("n", a, b), blk("SEL", k), A("G16", lo + k, hi, 16)) for k in range(16)])
            lin(A("N16", a, b), ps("n", a, b), 2048.0)
            sv = A(VW, svo(a) + lo, svo(a) + hi)
            act(sv, IND(VF, A("S16", a, b)))
            tt(A("DD", lo, hi), IND(VF, A("N16", a, b)), sv, OP.subtract)
            key = ps("key", a, b)
            it = [(key, A("IM32"), segs(m, "N", 1, a, b)[0][2])]
            if q in cfg["abss"]:
                act(A("RR", lo, hi), A("DD", lo, hi), AF.Abs)
                it += [(key, zw("Z1", k), A("RR", lo + k, hi, 16)) for k in range(16)]
            else:
                ts(A("RR", lo, hi), A("DD", lo, hi), 0.0, OP.max)
                it += [(key, zw("ZM1", k), A("DD", lo + k, hi, 16)) for k in range(16)]
                it += [(key, zw("Z2", k), A("RR", lo + k, hi, 16)) for k in range(16)]
            mm(it)
        first_of_32(ID, C, "HC", "QC", "dedC", "LOFF", -1280.0)
        for a, b in cfg["lg"]:
            nok = A("NOK", a, b)
            act(nok, ps("key", a, b), AF.Sign, bias=col(cTHR))
            mm([(ps("val", a, b), A("SU"), nok)])
            act(A("IND", a, b), ps("val", a, b), AF.Sign, bias=col(c16K), scale=-1.0, other=(col(c16K), OP.is_lt, None, None))
            an = segs(m, "N", 1, a, b)
            ao = [(a, b, A("AO", a, b))] if last else segs(m, "O", 1, a, b)
            mm([(ps("xA", a, b), A("B32"), nok)] + [(ps("xA", x0, x1), ID, x) for x0, x1, x in an])
            for x0, x1, x in ao:
                act(x, ps("xA", x0, x1), bias=0.421875)
            mm([(ps("rr", a, b), A("MI8"), nok), (ps("rr", a, b), A("BO"), A("IND", a, b))])
            act(A("RL", a, b), ps("rr", a, b), AF.Relu, bias=col(cK1))
            y = ps("Y23", a, b)
            mm([(y, A("BO"), A("TC", a, b)), (y, A("BO"), A("IND", a, b))] +
               [(ps("Y23", x0, x1), A("I8192"), x) for x0, x1, x in an] + [(ps("Y23", x0, x1), A("IM8192"), x) for x0, x1, x in ao] +
               [(y, A("MI1"), A("RL", a, b))])
            tt(A("P16", a, b), y, A("N16", a, b), OP.max)
        for a, b in cfg["mr"]:
            nok, nh, sh = A("NOK", a, b), A("NH", a, b), A("SH", a, b)
            lin(nh, A("N16", a, b), -2048.0)
            if les:
                mm([(ps("dn", a, b), ID, sh), (ps("dn", a, b), A("MI1"), nh), (ps("dn", a, b), A("IM8192"), nok)])
                act(A("M0", a, b), ps("dn", a, b), AF.Relu)
                mm([(ps("m1", a, b), ID, nh), (ps("m1", a, b), A("ID32"), A("M0", a, b)), (ps("m1", a, b), A("I4096"), nok)])
                act(A("M1", a, b), ps("m1", a, b), bias=les - 2048.0)
            else:
                mm([(ps("dn", a, b), ID, sh), (ps("dn", a, b), A("IM4096"), nok)])
                act(A("M0", a, b), ps("dn", a, b), AF.Relu, bias=-2048.0)
                mm([(ps("m1", a, b), ID, nh), (ps("m1", a, b), A("I4096"), nok)])
                act(A("M1", a, b), ps("m1", a, b), AF.Relu, bias=-2048.0)
        for a, b in cfg["am"]:
            absd = [q in cfg["abss"] for q, (x0, x1) in enumerate(cfg["p1"]) if x0 == a][0]
            if not last:
                if cfg["tl"]:
                    y = ps("oh", a, b)
                    it = [(y, A("ONES"), A("K0"))]
                    for src, w in (("RR", "GZ1"),) if absd else (("DD", "GZM"), ("RR", "GZ2")):
                        it += [(ps("oh", a + k, b, 16), A(src, 16 * a + k, 16 * b, 16), A(w)) for k in range(16)]
                    mm(it)
                    scan(A("KH1", a, b), A("RSK", 0, 128), y, OP.max, OP.min)
                    scan(A("KH2", a, b, -1), A("RSK", 0, 128), A("KH1", a, b, -1), OP.max, OP.min)
                    mm([(ps("D", a, b), A("KH2", a, b), ID), (ps("D", a, b), A("KH1", a, b), A("MI1"))])
                else:
                    tr(A("KTT", a, b), ps("key", a, b))
                    scan(A("KSC", a, b), A("RSK", 0, b - a), A("KTT", a, b), OP.max, OP.min)
                    tr(A("MX", a, b), A("KSC", a, b))
                    mm([(ps("D", a, b), A("DM"), A("MX", a, b))])
                act(A("IND2", a, b), ps("D", a, b), AF.Relu, bias=1.0, scale=-1.0, other=(0.5, OP.is_lt, None, None))
                i2, oha, msk = A("IND2", a, b), A("OHA", a, b), A("MSK", a, b)
                mm([(ps("oh", a, b), A("OH"), i2)])
                tt(oha, ps("oh", a, b), A("A32", a, b), OP.mult)
                if not cfg["q1s"]:
                    act(A("OHS", a, b), ps("oh", a, b), bias=1.0, scale=-1.0)
                mm([(ps("colw", a, b), ID, msk), (ps("colw", a, b), A("BO"), oha)])
                hold("HA", ps("colw", a, b), a, b)
        for a in range(224, -1, -32):
            dst = IND(A("LE"), A("LOFF", a // 16, a // 16 + 2))
            if les:
                act(dst, A("M1", a, a + 32), AF.Silu)
            else:
                tt(dst, A("M0", a, a + 32), A("M1", a, a + 32), OP.add)
        if last:
            yl = A("YL") if les else LEW
            if les:
                ts(yl, LEW, 12582912.0 - les, OP.add, -12582912.0, OP.add)
            dma(("out", "yl", 0, 512), yl, 128 * 2048, [yl], [])
        else:
            first_of_32(A("BO"), "OHA", "HA", "QA", "dedA", "AOFF", 0.0)
            for a, b in cfg["da"]:
                src = IND(A("AD"), A("AOFF", a // 16, b // 16))
                if not cfg["q1s"]:
                    tt(A("Q1", a, b), src, A("OHS", a, b), OP.mult)
                    continue
                act(A("Q0", a, b), src)
                for x0 in range(a, b, 128):
                    x1 = min(b, x0 + 128)
                    mm([(ps("oh2", x0, x1), A("ID32"), A("Q0", x0, x1)), (ps("oh2", x0, x1), A("MOH8"), A("IND2", x0, x1))])
                    act(A("Q1", x0, x1), ps("oh2", x0, x1), AF.Relu)
        two = set()
        for q, (a, b) in enumerate(cfg["p3"]):
            lo, hi = 16 * a, 16 * b
            lb = [x1 for x0, x1 in cfg["lg"] if x0 <= a < x1][0]
            src = IND(A(VW, 0, svo(a) + 16 * lb), A("P16", a, b))
            if q in cfg["vv"]:
                two |= set(range(a, b))
                tt(A("G16", lo, hi), src, A("OFS", 0, hi - lo), OP.add)
                for c0 in range(lo, hi, 256):
                    scan(A("HI2", c0 // 2, c0 // 2 + 128), A("G16", c0, c0 + 256, 2), A("G16", c0 + 1, c0 + 256, 2), OP.max, OP.max, -4096.0)
                    scan(A("LO2", c0 // 2, c0 // 2 + 128, -1), A("G16", c0 + 1, c0 + 256, -2), A("G16", c0, c0 + 255, -2), OP.min, OP.min, 4096.0)
                continue
            act(A("VV", lo, hi), src)
            scan(A("HI", lo, hi), A("RSN", 0, hi - lo), A("VV", lo, hi), OP.max, OP.min)
            scan(A("LO", lo, hi), A("RSP", 0, hi - lo), A("VV", lo, hi), OP.min, OP.max)
        for a, b in cfg["tail"]:
            ja, jb, lo, hi = a // 16, b // 16, 16 * a, 16 * b
            zo = A("ZO", a, b) if last else segs(m, "O", 0, a, b)[0][2]
            x = ps("Xz", a, b)
            if a in two:
                it = [(x, A("BO"), A("OF2", a, b)), (x, A("MIH"), A("HI2", lo // 2 + 7, hi // 2, 8)), (x, A("MIH"), A("LO2", lo // 2, hi // 2, 8))]
            else:
                it = [(x, A("IQ"), A("ONES", 0, b - a)), (x, A("MIH"), A("HI", lo + 15, hi, 16)), (x, A("MIH"), A("LO", lo + 15, hi, 16))]
            mm(it[:1] + [(ps("Xz", x0, x1), ID, z) for x0, x1, z in segs(m, "N", 0, a, b)] + it[1:])
            act(A("ZR", a, b), x, bias=12582912.0)
            act(zo, A("ZR", a, b), AF.Abs, bias=-12582912.0)
            mm([(ps("U16", a, b), A("W16"), zo)])
            lin(A("FL", a, b), ps("U16", a, b), -24568.5, -1.0)
            w = ps("ww", a, b)
            mm([(w, ID, A("T16M", a, b)), (w, A("W16"), zo), (w, ID, A("FL", a, b))])
            wrap("WS", w, a, b)
            lin(A("WW16", ja, jb), A("WS", a + 15, b, 16), 24576.0 - lo)
            yv = A(VN, lo, hi)
            cp(IND(yv, A("WW16", ja, jb)), zo)
            if last:
                dma(("out", "yv", lo, hi), yv, 4096 * (b - a), [yv], [])
                dma(("out", "yz", a, b), zo, 256 * (b - a), [zo], [])
                continue
            y = ps("q2", a, b)
            mm([(y, ID, A("T16", a, b)), (y, A("OH8"), A("IND2", a, b)), (y, A("W16"), zo), (y, ID, A("FL", a, b))])
            act(A("Q2", a, b), y, AF.Relu, bias=24576.0 - 8192)
            for bb in range(3, -1, -1):
                if a <= 64 * bb < b and (bb + m) % 4:
                    src, dst = A("PO%d" % m, 128 * bb, 128 * bb + 128), A("PN%d" % (m + 1), 128 * bb, 128 * bb + 128)
                    add("g", "send", (m, bb, src, dst), [src], [dst], cfg["si"] + (cfg["s1"] if (m, bb) == (1, 2) else 0.0), cfg["sl"])
            for x0 in range(b - 32, a - 1, -32):
                tt(IND(A("AD"), A("AOFF", x0 // 16, x0 // 16 + 2)), A("Q1", x0, x0 + 32), A("Q2", x0, x0 + 32), OP.add)
    while True:
        used = {}
        for o in ops:
            for x in o["r"]:
                used.setdefault(x[0], []).append((x[1], x[2]))
        keep = [o for o in ops if not o["w"] or o["k"] == "send" or any(
            lo < o["w"][0][2] and o["w"][0][1] < hi for lo, hi in used.get(o["w"][0][0], ()))]
        if len(keep) == len(ops):
            return ops
        ops[:] = keep


def schedule(ops, cfg):
    n = len(ops)
    hist = {}
    for i, o in enumerate(ops):
        d = set()
        for accs, w in ((o["r"], False), (o["w"], True)):
            for x in accs:
                for j, lo, hi, jw in hist.get(x[0], ()):
                    if (w or jw) and lo < x[2] and x[1] < hi and j != i:
                        d.add(j)
        for accs, w in ((o["r"], False), (o["w"], True)):
            for x in accs:
                h = hist.setdefault(x[0], [])
                if w and abs(x[3]) == 1:
                    h[:] = [y for y in h if not (x[1] <= y[1] and y[2] <= x[2])]
                h.append((i, x[1], x[2], w))
        o["d"] = d
        o["b"] = {x[0] for x in o["r"] + o["w"] if psum(x)}
    anc = [0] * n
    for i, o in enumerate(ops):
        m = 0
        for j in o["d"]:
            m |= anc[j]
        o["d"] = {j for j in o["d"] if not (m >> j) & 1}
        for j in o["d"]:
            m |= 1 << j
        anc[i] = 0 if o["k"] == "send" else m
    succ = [[] for _ in ops]
    for i, o in enumerate(ops):
        for j in sorted(o["d"]):
            succ[j].append(i)
    lat = cfg["lat"]
    eng = [o["e"] for o in ops]; cost = [o["c"] for o in ops]; after = [o["l"] for o in ops]; xf = [o["x"] for o in ops]
    banks = [sorted(o["b"]) for o in ops]; deps = [sorted(o["d"]) for o in ops]

    E = {e: x for x, e in enumerate("vspgy")}
    en = [E[e] for e in eng]; bk = [[int(b[1:]) for b in bs_] for bs_ in banks]
    dur = [xf[i] or cost[i] for i in range(n)]
    pre = [cost[i] + after[i] if xf[i] else 0.0 for i in range(n)]
    post = [0.0 if xf[i] else after[i] for i in range(n)]

    nothing = ([[]] * 13, [0.0] * n, [0.0] * n, [0.0] * 5, [0.0] * n)

    def place(seq, nxt, pre, post, fixed=nothing):
        S = [[y[0] for y in x] for x in fixed[0]]; F = [[y[1] for y in x] for x in fixed[0]]
        BS, BF, BE = S[5:], F[5:], [[y[2] for y in x] for x in fixed[0][5:]]
        rdy = list(fixed[1]); out = fixed[2]; start = list(fixed[4]); end = 0.0
        for i in seq:
            e = en[i]; c = dur[i]; t = rdy[i] + pre[i]
            s = S[e]; f = F[e]; bs = bk[i]; m = x = len(s)
            while x and f[x - 1] > t:
                x -= 1
            while True:
                while x < m and s[x] < t + c:
                    if f[x] > t:
                        t = f[x]
                    x += 1
                if not bs:
                    break
                t0 = t
                for b in bs:
                    ss = BS[b]; ff = BF[b]; ee = BE[b]
                    y = mb = len(ss)
                    while y and ff[y - 1] + lat > t:
                        y -= 1
                    while y < mb and ss[y] < t + c + lat:
                        if ee[y] != e and ff[y] + lat > t:
                            t = ff[y] + lat
                        y += 1
                if t == t0:
                    break
            s.insert(x, t); f.insert(x, t + c)
            for b in bs:
                ss = BS[b]; y = len(ss)
                while y and ss[y - 1] > t:
                    y -= 1
                ss.insert(y, t); BF[b].insert(y, t + c); BE[b].insert(y, e)
            start[i] = t
            z = t + c + post[i]
            if z + out[i] > end:
                end = z + out[i]
            z += lat
            for j in nxt[i]:
                if z > rdy[j]:
                    rdy[j] = z
        return max([end] + [F[e][-1] + fixed[3][e] for e in range(5) if F[e]]), start

    def forward(key):
        return place(np.argsort(key, kind="stable").tolist(), succ, pre, post)

    def both(key):
        r = forward(key)
        s2 = place(np.argsort(-np.add(r[1], dur), kind="stable").tolist(), deps, post, pre)[1]
        r3 = forward(-np.add(s2, dur))
        return r3 if r3[0] <= r[0] else r

    lv = [0.0] * n
    for i in range(n - 1, -1, -1):
        lv[i] = pre[i] + dur[i] + post[i] + max([lv[j] + lat for j in succ[i]] + [0.0])
    rng = np.random.RandomState(cfg["seed"])
    mode = [0] * n

    def setmode(i, x):
        mode[i] = x; en[i] = E[ops[i]["m"][x][0]]; dur[i] = ops[i]["m"][x][3]

    def anneal(W, cur, value, iters, temp):
        free = [i for i in W if "m" in ops[i]]
        inside = [False] * n
        for i in W:
            inside[i] = True
        up = [[j for j in deps[i] if inside[j]] for i in range(n)]; down = [[j for j in succ[i] if inside[j]] for i in range(n)]
        best = cur; top = list(mode); t0, t1 = min(cur[1][i] for i in W), max(cur[1][i] for i in W)
        for it in range(iters):
            key = list(cur[1]); undo = []
            if rng.uniform() < cfg["flip"]:
                for _ in range(1 + rng.randint(2)):
                    i = free[rng.randint(len(free))]; k = len(ops[i]["m"])
                    undo.append((i, mode[i]))
                    setmode(i, (mode[i] + 1 + rng.randint(k - 1)) % k)
            elif rng.uniform() < 0.3:
                a = rng.uniform(t0 - 3000, t1); sp = rng.uniform(1000, 10000)
                nz = (rng.normal(0, rng.choice([200.0, 600.0, 1500.0]), n) * (rng.uniform(size=n) < 0.4)).tolist()
                for i in W:
                    if a <= key[i] < a + sp:
                        key[i] += nz[i]
                    for j in up[i]:
                        if key[j] >= key[i]:
                            key[i] = key[j] + 0.01
            else:
                for _ in range(1 + rng.randint(2)):
                    i = W[rng.randint(len(W))]; dl = rng.exponential(1500.0); st = [i]
                    if rng.uniform() < 0.5:
                        key[i] -= dl
                        while st:
                            x = st.pop()
                            for j in up[x]:
                                v = key[x] - dur[j] - pre[x] - post[j] - lat
                                if key[j] > v:
                                    key[j] = v; st.append(j)
                    else:
                        key[i] += dl
                        while st:
                            x = st.pop()
                            for j in down[x]:
                                v = key[x] + dur[x] + pre[j] + post[x] + lat
                                if key[j] < v:
                                    key[j] = v; st.append(j)
            r = value(key)
            if r[0] <= cur[0] + temp * (1.0 - it / iters) * rng.exponential():
                cur = r
                if r[0] < best[0]:
                    best = r; top = list(mode)
            else:
                for i, x in reversed(undo):
                    setmode(i, x)
        for i in free:
            setmode(i, top[i])
        return best

    best = anneal(list(range(n)), both([-x for x in lv]), lambda key: both(key) if rng.uniform() < cfg["both"] else forward(key),
                  cfg["iters"], cfg["temp"])
    for sweep in range(cfg["sweeps"]):
        t0 = -rng.uniform(0, cfg["span"] / 2)
        while t0 < best[0] - 5000:
            st = best[1]; t1 = t0 + cfg["span"]
            back = place(np.argsort(-np.add(st, dur), kind="stable").tolist(), deps, post, pre)[1]
            W = [i for i in range(n) if t0 <= st[i] - pre[i] < t1]
            rdy = [max(t0 - 2000, 0.0)] * n; out = [0.0] * n; last = [0.0] * 5
            S = [[] for _ in range(13)]
            for i in sorted(range(n), key=lambda i: st[i]):
                if st[i] - pre[i] >= t1:
                    last[en[i]] = max(last[en[i]], back[i] + dur[i])
                    for j in deps[i]:
                        out[j] = max(out[j], lat + pre[i] + back[i] + dur[i])
                elif st[i] - pre[i] < t0:
                    for j in succ[i]:
                        rdy[j] = max(rdy[j], st[i] + dur[i] + post[i] + lat)
                    if st[i] + dur[i] > t0 - 2500:
                        for x in [en[i]] + [5 + b for b in bk[i]]:
                            S[x].append((st[i], st[i] + dur[i], en[i]))
            fixed = (S, rdy, out, last, st)
            old = list(mode)

            def value(key):
                return place(sorted(W, key=lambda i: key[i]), succ, pre, post, fixed)
            r = anneal(W, value(st), value, cfg["its"], cfg["temp"] * (1.0 - sweep / cfg["sweeps"]))
            r = both([r[1][i] if st[i] - pre[i] < t1 else r[0] - back[i] - dur[i] for i in range(n)])
            if r[0] <= best[0]:
                best = r
            else:
                for i in W:
                    if mode[i] != old[i]:
                        setmode(i, old[i])
            t0 += cfg["span"] / 2
    for i in range(n):
        if "m" in ops[i]:
            cost[i] = dur[i]
    key = [best[1][i] - pre[i] for i in range(n)]
    order = sorted(range(n), key=lambda i: key[i])
    sets = [(cost, lat, after, xf)]; plans = [ops]
    for alt in cfg["alts"]:
        c2 = dict(cfg); c2.update(alt); p2 = plan(c2); plans.append(p2)
        sets.append(([o["m"][mode[i]][3] if "m" in o else o["c"] for i, o in enumerate(p2)], c2["lat"], [o["l"] for o in p2], [o["x"] for o in p2]))

    def timed(order, costs, old=None, lo=0):
        c2, l2, after, xf = costs
        if old is None:
            x0 = 0; snaps = []
            free = [0.0] * 5; prev = [-1] * 5; fin = [0.0] * n; why = [-1] * n; xfree = 0.0
            lastb = [[-1, -1, -1] for _ in range(8)]
        else:
            x0 = lo >> 5; snaps = old[3][:x0]; sn = old[3][x0]; x0 <<= 5
            free = list(sn[0]); prev = list(sn[1]); xfree = sn[2]; lastb = [list(y) for y in sn[3]]
            fin = list(old[1]); why = list(old[2])
        for x in range(x0, n):
            if not x & 31:
                snaps.append((list(free), list(prev), xfree, [list(y) for y in lastb]))
            i = order[x]
            e = en[i]; t = free[e]; w = prev[e]
            for j in deps[i]:
                if fin[j] > t:
                    t = fin[j]; w = j
            for b in bk[i]:
                lb = lastb[b]
                for e2 in (0, 1, 2):
                    j = lb[e2]
                    if j >= 0 and e2 != e and fin[j] > t:
                        t = fin[j]; w = j
                lb[e] = i
            why[i] = w; prev[e] = i
            t += c2[i]; free[e] = t; t += after[i]
            if xf[i]:
                t = xfree = (t if t > xfree else xfree) + xf[i]
            fin[i] = t + l2
        end = max(fin)
        return end - l2, fin, why, snaps

    def total(order, olds=None, lo=0):
        rs = [timed(order, costs, olds[x] if olds else None, lo) for x, costs in enumerate(sets)]
        return sum(r[0] for r in rs), rs

    dset = [set(d) for d in deps]
    cur, rs = total(order); keep = (cur, list(order), list(mode))
    for it in range(cfg["moves"]):
        pos = [0] * n
        for x, i in enumerate(order):
            pos[i] = x
        r = rs[rng.randint(len(rs))]
        i = r[1].index(max(r[1])); pairs = []
        while r[2][i] >= 0:
            j = r[2][i]
            if j not in dset[i] and en[i] != 4:
                pairs.append((j, i))
            i = j
        j, i = pairs[rng.randint(len(pairs))]
        u = rng.uniform()
        new = list(order)
        if u > 0.8 and "m" in ops[i]:
            was = mode[i]; to = (was + 1 + rng.randint(len(ops[i]["m"]) - 1)) % len(ops[i]["m"])
            for x in (to, was):
                setmode(i, x)
                for c2, p2 in zip(sets, plans):
                    c2[0][i] = p2[i]["m"][x][3]
                if x == was:
                    break
                s, r2 = total(order, rs, pos[i])
                if s <= cur:
                    cur, rs = s, r2
                    if s < keep[0]:
                        keep = (s, list(order), list(mode))
                    break
            continue
        if u < 0.45:
            lo = max(0, pos[j] - (rng.randint(30) if rng.uniform() < 0.4 else 0)); grp = {i}
            for x in range(pos[i] - 1, lo - 1, -1):
                if en[order[x]] != 4 and any(k in grp for k in succ[order[x]]):
                    grp.add(order[x])
                elif any(k in grp for k in succ[order[x]]):
                    lo = x + 1
                    break
            seg = order[lo:pos[i] + 1]
            new[lo:pos[i] + 1] = [k for k in seg if k in grp] + [k for k in seg if k not in grp]
        elif u < 0.9:
            hi = min(n - 1, pos[i] + (rng.randint(30) if rng.uniform() < 0.4 else 0)); grp = {j}
            for x in range(pos[j] + 1, hi + 1):
                if any(k in grp for k in deps[order[x]]):
                    grp.add(order[x])
            seg = order[pos[j]:hi + 1]
            new[pos[j]:hi + 1] = [k for k in seg if k not in grp] + [k for k in seg if k in grp]
        else:
            i = rng.randint(n)
            lo = max([pos[k] for k in deps[i]] + [-1]) + 1; hi = min([pos[k] for k in succ[i]] + [n]) - 1
            new.pop(pos[i]); new.insert(rng.randint(max(lo, pos[i] - 60), min(hi, pos[i] + 60) + 1), i)
        if new == order:
            continue
        s, r2 = total(new, rs, next(x for x in range(n) if new[x] != order[x]))
        if s <= cur + cfg["temp2"] * (1.0 - it / cfg["moves"]) * rng.exponential():
            order, cur, rs = new, s, r2
            if s < keep[0]:
                keep = (s, list(order), list(mode))
    order = keep[1]
    for i in range(n):
        o = ops[i]
        if "m" in o:
            setmode(i, keep[2][i])
            o["e"], o["k"], o["a"], o["c"] = o["m"][mode[i]]
            for c2, p2 in zip(sets, plans):
                c2[0][i] = p2[i]["m"][mode[i]][3]
    end, fin = timed(order, sets[0])[:2]
    cfg["ends"] = [int(timed(order, x)[0]) for x in sets]
    lastb = {}
    for i in order:
        o = ops[i]
        o["d"] = set(deps[i]); o["t"] = fin[i] - lat - cost[i] - after[i] - xf[i]
        for b in bk[i]:
            o["d"] |= {j for e2, j in lastb.get(b, {}).items() if e2 != en[i]}
            lastb.setdefault(b, {})[en[i]] = i
    return order, end


_PLAN = {}


def rank_program(g, core, T, topo):
    rank = T.rank_of(core)
    if rank is None:
        return
    if not _PLAN:
        ops_ = plan(CFG)
        _PLAN["ops"] = ops_; _PLAN["order"] = schedule(ops_, CFG)[0]
    ops, order = _PLAN["ops"], _PLAN["order"]
    Q = {"v": g.vector, "s": g.scalar, "p": g.tensor, "g": g, "y": g.sync}
    N = len(T.cores)

    def X(a):
        if not isinstance(a, tuple):
            return a
        if a[0] == "*":
            return X(a[1]).indirect(X(a[2]))
        if a[0] in ("in", "out"):
            t = T[a[1]]
            return t[:] if a[3] - a[2] == t.shape[1] else t[:, a[2]:a[3]]
        return T[a[0]][:, a[1]:a[2]] if a[3] == 1 else T[a[0]][:, cols(a)]

    count = {}; done = {}; seen = {}; ndma = [0]; final = []; sent = [0]

    known = {}; rank_in = {i: x for x, i in enumerate(order)}

    def wait(e, sem, val):
        mine = seen.setdefault(e, {})
        if mine.get(sem, 0) < val:
            mine[sem] = val
            Q[e].wait_ge(T.sem[sem], val)

    for i in order:
        o = ops[i]; e = o["e"]; k = o["k"]; a = o["a"]; q = Q[e]
        mine = seen.setdefault(e, {})
        for j in sorted(o["d"], key=lambda j: -rank_in[j]):
            if mine.get(done[j][0], 0) < done[j][1]:
                wait(e, *done[j])
                for s, v in known[j].items():
                    if mine.get(s, 0) < v:
                        mine[s] = v
        known[i] = {} if k == "send" else dict(mine)
        if k == "dma":
            s = "d%d" % ndma[0]; ndma[0] += 1
            q.dma_start(X(a[0]), X(a[1])).then_inc(T.sem[s], 16)
            done[i] = (s, 16); final.append((s, 16))
            continue
        if k == "send":
            m, b, src4, dst4 = a
            dst = T.cores[(rank + b + m) % N]
            rid, pid = topo.addr(dst)[:2]
            en = topo.engines(core, dst)
            s = "arr%d_%d" % (m, b)
            g.remote_dma(X(dst4), X(src4), T.sem[s], T.sem.sent, pid, rid, sum(1 << x for x in en[:8]))
            sent[0] += 8
            done[i] = (s, 8); final.append((s, 8))
            continue
        if k == "ts":
            if a[3] is None:
                ins = q.tensor_scalar(X(a[0]), X(a[1]), X(a[2]), None, a[4])
            else:
                ins = q.tensor_scalar(X(a[0]), X(a[1]), X(a[2]), X(a[3]), a[4], a[5])
        elif k == "cp":
            ins = q.tensor_copy(X(a[0]), X(a[1]))
        elif k == "tt":
            ins = q.tensor_tensor(X(a[0]), X(a[1]), X(a[2]), a[3])
        elif k == "ms":
            ins = q.memset(X(a[0]), a[1])
        elif k == "scan":
            ins = q.tensor_tensor_scan(X(a[0]), X(a[1]), X(a[2]), a[5], a[4], a[3])
        elif k == "tr":
            ins = q.transpose(X(a[0]), X(a[1]))
        elif k == "act":
            if a[0][0] == "*":
                ins = q.activation(X(a[0]), X(a[1]), a[2])
            else:
                ins = q.activation(X(a[0]), X(a[1]), a[2], bias=X(a[3]), scale=X(a[4]))
        elif k == "iota":
            if dty(a[0]) == I32:
                ins = q.iota(X(a[0]), a[1], a[2], a[3])
            else:
                ins = q.iota(X(a[0]), a[1], a[2], a[3], allow_small_or_imprecise_dtypes=True)
        elif k == "asel":
            ins = q.affine_select(X(a[0]), X(a[1]), a[2], a[3], 0.0, a[4], a[5])
        else:
            for x, (po, l, r) in enumerate(a):
                ins = q.matmul(X(po), X(l), X(r), x == 0, x == len(a) - 1)
        count[e] = count.get(e, 0) + 1
        ins.then_inc(T.sem[SEM[e]], 1)
        done[i] = (SEM[e], count[e])
    for e, c in count.items():
        wait("y", SEM[e], c)
    wait("y", "sent", sent[0])
    for s, v in final:
        wait("y", s, v)
